import numpy as np, ml_dtypes
CORES = [6,15,38,47]
N = 4
BF = ml_dtypes.bfloat16
def gentries(a):
    return np.ascontiguousarray(a.reshape(8, 16, -1).transpose(0, 2, 1)).reshape(8, -1)
def gtable(e):
    e = np.asarray(e); return np.ascontiguousarray(e.reshape(8, -1, 16).transpose(0, 2, 1)).reshape(128, -1).astype(np.int32)
C, M, G, T, TH, S = 8192, 1024, 256, 4, 10, 32
def parts(rng):
    R = rng.integers(0, 256, (N, 8, 16, C)); P = rng.integers(0, M, (N, 8, 16, M)); O = rng.integers(0, M, (N, 8, 16, M))
    z = (256 * rng.choice(np.array([0.6, 0.8, 1.0]), (N, 8, 1, G)) * rng.random((N, 8, 16, G))).astype(np.int64)
    return R, P, O, z, rng.integers(0, M, (N, 8, G)), rng.integers(1, 257, (N, 8, 16))
def pack(R, P, O, z, mv, w):
    P = np.array(P); O = np.array(O); P[:, :, 0] = np.arange(M); O[:, :, 0] = np.arange(M)
    return {"strat": R.reshape(N, 128, C).astype(np.float32).astype(BF), "vp": P.reshape(N, 128, M).astype(np.int32), "vo": O.reshape(N, 128, M).astype(np.int32),
            "z0": z.reshape(N, 128, G).astype(np.float32).astype(BF), "mv": np.stack([gtable(a) for a in mv]), "wt": w.reshape(N, 128, 1).astype(np.int32)}
def plant(rng, R, P, O, z, mv, w):
    h = 17 - TH; m = np.arange(M)
    w[:, :, 13] = 16; w[:, :, 14] = 1; w[:, 2, :13] = np.maximum(w[:, 2, :13], 160)
    for r in range(N):
        q = (r + 1) % N
        for g in range(8):
            own = rng.permutation(M)[:12]; i = 1 + rng.permutation(G - 17)[:5]; wq = w[q, g]
            for e in range(4):
                a = int(i[e]); mv[r, g, a] = own[e]; P[r, g, 3 + 4 * e, own[e]] = M - 1
                z[r, g, :h, a] = 255; z[r, g, 13:15, a] = 0
                d = (4065 - int(np.sum(wq * z[r, g, :, a]))) & 4095
                z[r, g, 13, a] = d >> 4; z[r, g, 14, a] = d & 15
            if g == 2:
                left = 2 ** 19
                for j in list(range(13)) + [15, 13, 14]:
                    n = min(255, left // int(wq[j])); z[r, g, j, int(i[4])] = n; left -= n * int(wq[j])
            end = G - 15 + 2 * np.arange(8); mv[r, g, end] = own[4:]
            z[r, g, :h, G - 15::2] = 255
            u = np.sum(wq[:, None] * z[r, g], axis=0) & 4095; p0 = int(u[0]) & (S - 1)
            R[q, g, :, p0] = 255 * rng.integers(0, 2, 16)
            ad = (((m[:, None] * u[end][None, :]) >> 5) + m[:, None] + 37 * 15) & (C - 1)
            for e in range(8):
                good = np.flatnonzero(ad[:, e] == p0)
                if len(good): P[r, g, 15, own[4 + e]] = rng.choice(good)
    return R, P, O, z, mv, w
def setup_inputs(rng):
    return pack(*plant(rng, *parts(rng)))
def corner(rng, first):
    R, P, O, z, mv, w = parts(rng); R = np.maximum(R, 1); m = np.arange(M)[None, :]; j = np.arange(16)[:, None]
    forms = [m + 0 * j, np.maximum(m - j, 0), np.minimum(m + j, M - 1), np.where((m + j) % 2 == 0, 0, M - 1)]
    P = np.stack([np.stack([forms[(g + r) % 4] for g in range(8)]) for r in range(N)])
    O = np.stack([np.stack([forms[(g + r + 1 + g // 4) % 4] for g in range(8)]) for r in range(N)])
    cnt = np.array([255, 256, 1024, 512, 257, 511, 1, 8 * G - 1, 8 * G, 0, 1536, 4 * G, 6 * G, 8 * G - 256, 1023, 1025])[first * N:first * N + N]
    cnt = np.roll(cnt, int(rng.integers(0, N)))
    for r in range(N):
        for g in range(8):
            e = (g + r) % 3
            if e == 0: mv[r, g] = rng.choice(np.array([0, M - 1]), G)
            elif e == 1: mv[r, g] = rng.integers(0, M)
            else: mv[r, g] = rng.permutation(M)[:G]
        hit = np.zeros(8 * G, bool); hit[rng.permutation(8 * G)[:int(cnt[r])]] = True
        z[r] = np.where(hit.reshape(8, 1, G), 0, 255)
    w[:, 1] = 1; w[:, 5] = 256
    return pack(R, P, O, z, mv, w)
def setup_inputs_corners(rng):
    return corner(rng, 0)
def setup_inputs_corners_two(rng):
    return corner(rng, 1)
def setup_inputs_ends(rng):
    R = np.where(rng.random((N, 8, 16, C)) < rng.choice(np.array([0.1, 0.5, 0.75, 0.9]), (N, 8, 1, C)), 255, 0)
    z = np.where(rng.random((N, 8, 16, G)) < rng.choice(np.array([0.05, 0.3, 0.8]), (N, 8, 1, G)), 255, 0)
    P = (M - 1) * rng.integers(0, 2, (N, 8, 16, M)); O = (M - 1) * rng.integers(0, 2, (N, 8, 16, M)); mv = (M - 1) * rng.integers(0, 2, (N, 8, G))
    w = np.where(rng.random((N, 8, 16)) < 0.5, 256, 1)
    mv[:, :, G - 1] = M - 1; P[:, :, 15, M - 1] = M - 1; O[:, :, 15, M - 1] = M - 1
    w[:, 0] = 256; R[:, 0] = np.where(rng.random((N, 1, C)) < 0.5, 255, 0); z[:, 0, :, G - 1] = 255; z[:, 0, :, 0] = 0
    w[:, 5:] = 256; w[:, 5:, 15] = 1
    c = np.zeros(16, np.int64); c[3] = 255; c[15] = 255
    x8 = np.array([0, 1, 2, 4, 5, 6, 7, 8]); y4 = np.array([9, 10, 11, 12])
    for g in (6, 7):
        hot = ((np.arange(C) >> 7) + g) % 2 == 1
        R[:, g] = c[None, :, None]
        R[:, g, x8] = np.where(hot, 192, 64 * rng.integers(0, 2, (N, 1, C))); R[:, g, y4] = np.where(hot, 128, 0)
        z[:, g, :, 1::2] = c[None, :, None]; z[:, g, :, G - 1] = c[None, :]
    R[:, 5] = 0; R[:, 5, 15] = 255; R[:, 5, y4] = 128 * rng.integers(0, 2, (N, 1, C))
    R[:, 5, x8, C - 1] = 192; R[:, 5, y4, C - 1] = 128
    z[:, 5] = 0; z[:, 5, 15] = 255
    m = np.arange(M); f = ((m * 255) >> 5) + m
    for j in range(1, 14):
        near = m[((f + 37 * (j + 1)) & (C - 1)) >= C - 256]
        P[:, 5, j] = rng.choice(near, (N, M)); O[:, 5, j] = rng.choice(near, (N, M))
    P[:, 5, 14:] = rng.integers(0, M, (N, 2, M)); O[:, 5, 14:] = rng.integers(0, M, (N, 2, M))
    mv[:, 5] = np.argsort(rng.random((N, M)), axis=1)[:, :G]; mv[:, 5, G - 1] = M - 1
    keep = np.array(R[3, 5])
    z[1, :, :17 - TH] = 255; z[2, :, :TH] = 0; R[3, :, :TH] = 255
    a0 = f[mv[2, 5]] & (C - 1); keep[np.ix_(x8, a0)] = 192; keep[np.ix_(y4, a0)] = 128; R[3, 5] = keep
    return pack(R, P, O, z, mv, w)
def setup_inputs_spread(rng):
    R = np.minimum((np.exp2(8 * rng.random((N, 8, 1, C))) * rng.random((N, 8, 16, C))).astype(np.int64), 255)
    z = np.minimum((np.exp2(8 * rng.random((N, 8, 1, G))) * rng.random((N, 8, 16, G))).astype(np.int64), 255)
    P = np.minimum((M * rng.random((N, 8, 16, M)) ** 3).astype(np.int64), M - 1); O = np.minimum((M * rng.random((N, 8, 16, M)) ** 3).astype(np.int64), M - 1)
    mv = np.minimum((M * rng.random((N, 8, G)) ** 2).astype(np.int64), M - 1)
    w = np.minimum(np.maximum(np.rint(np.exp2(8 * rng.random((N, 8, 16)))).astype(np.int64), 1), 256)
    v0 = [v for v in range(M + G * (T - 2), M + G * (T - 1)) if (-(2 ** 22)) % v < 32][0]
    u0 = (2 ** 22 + v0 - 1) // v0 - 32
    r = int(rng.integers(0, N)); q = (r + 1 + (T - 1) % (N - 1)) % N; p = (r + 1 + (T - 2) % (N - 1)) % N
    R[q, :, :17 - TH] = 0
    for g in (1, 3, 4, 6):
        w[q, g, 13] = 16; w[q, g, 14] = 1
        c = rng.integers(0, 256, 16); c[13:15] = 0
        d = (u0 - int(np.sum(w[q, g] * c))) & 4095
        c[13] = d >> 4; c[14] = d & 15
        R[p, g] = c[:, None]
        R[q, g, 15] = 0; R[q, g, 15, 0] = 255
    return pack(R, P, O, z, mv, w)
def setup_inputs_ties(rng):
    R, P, O, z, mv, w = parts(rng)
    b = rng.integers(0, 255, (8, 16)); b[0] = 0; b[6] = 254
    share = rng.permutation(np.array([0.02, 0.04, 0.07, 0.1, 0.15, 0.2, 0.3, 0.5])).reshape(1, 8, 1, 1)
    cnt = np.where(rng.random((N, 8, 1, C)) < share, rng.choice(np.array([TH, TH, TH, TH + 1, 16]), (N, 8, 1, C)), rng.choice(np.array([TH - 1, TH - 1, TH - 1, 0]), (N, 8, 1, C)))
    R = b[None, :, :, None] + (np.argsort(rng.random((N, 8, 16, C)), axis=2) < cnt)
    z = b[None, :, :, None] + (rng.random((N, 8, 1, G)) < 0.125) + np.zeros((N, 8, 16, G), np.int64)
    return pack(R, P, O, z, mv, w)
def check_inputs(d):
    bad = []
    for k, lo, hi in (("strat", 0, 255), ("vp", 0, M - 1), ("vo", 0, M - 1), ("z0", 0, 255), ("mv", 0, M - 1), ("wt", 1, 256)):
        a = np.asarray(d[k]).astype(np.float64)
        if not (np.min(a) >= lo and np.max(a) <= hi): bad.append("range of " + k)
        elif np.any(a != np.floor(a)): bad.append("whole numbers in " + k)
    for k in ("vp", "vo"):
        if np.any(np.asarray(d[k]).reshape(-1, 8, 16, M)[:, :, 0] != np.arange(M)): bad.append("row 0 of the views in " + k)
    return bad
def reference(strat, vp, vo, z0, mv, wt):
    R = strat.astype(np.float32).astype(np.int32).reshape(N, 8, 16, C); z = z0.astype(np.float32).astype(np.int32).reshape(N, 8, 16, G)
    w = wt.astype(np.int32).reshape(N, 8, 16, 1); v = np.stack([gentries(a) for a in mv]).astype(np.int64)
    room = np.zeros((N, 8, 16, G * T), np.int32)
    views = [np.concatenate([a.astype(np.int32).reshape(N, 8, 16, M), room], axis=3) for a in (vp, vo)]
    count = np.zeros(N, np.int64); kk = np.arange(16)[None, None, :, None]; verdicts = np.zeros((N, 8, T, G), np.int64)
    for t in range(T):
        mover, other = views[t % 2], views[1 - t % 2]
        q = (np.arange(N) + 1 + t % (N - 1)) % N
        L = np.take_along_axis(mover, v[:, :, None, :], 3).astype(np.int64)
        u = np.add.reduce(w[q] * z, axis=2).astype(np.int64) & 4095
        ad = (((L * u[:, :, None, :]) >> 5) + L + 37 * kk + (count[q] & 255)[:, None, None, None]) & (C - 1)
        Y = np.take_along_axis(R[q], ad.reshape(N, 8, 1, 16 * G), 3).reshape(N, 8, 16, 16, G)
        hit = np.add.reduce((Y > z[:, :, :, None, :]).astype(np.int32), axis=2) >= TH
        hit[:, :, 15] = True
        kap = np.argmax(hit, axis=2)
        use = (kk <= kap[:, :, None, :])[:, :, None]
        z = (np.maximum.reduce(np.where(use, Y, 0), axis=3) + np.minimum.reduce(np.where(use, Y, 255), axis=3)) >> 1
        z = z.astype(np.int32)
        if t < T - 1:
            place = S * np.arange(G) + (u & (S - 1))
            for r in range(N):
                ix = np.repeat(place[r][:, None, :], 16, axis=1); mine = R[int(q[r])]
                np.put_along_axis(mine, ix, (np.take_along_axis(mine, ix, 2) + z[r]) >> 1, 2)
        count[q] = np.add.reduce((kap < 15).reshape(N, 8 * G).astype(np.int64), axis=1)
        named = np.take_along_axis(L, kap[:, :, None, :], 2)
        resumed = np.take_along_axis(other, named, 3)
        n0 = M + G * t; n = np.zeros((N, 8, 1, G), np.int64) + n0 + np.arange(G)
        mover[..., n0:n0 + G] = np.concatenate([n, L[:, :, :15]], axis=2)
        other[..., n0:n0 + G] = np.concatenate([n, resumed[:, :, :15]], axis=2)
        v = n[:, :, 0]; verdicts[:, :, t] = kap
    e = M + G * (T - 1)
    return {"yp": views[0][..., e:e + G].reshape(N, 128, G).astype(np.float32), "yo": views[1][..., e:e + G].reshape(N, 128, G).astype(np.float32),
            "yz": z.reshape(N, 128, G).astype(np.float32).astype(BF), "yk": verdicts.reshape(N, 8, T * G).astype(np.float32)}

@@ -1,0 +1,824 @@
+import math
+import numpy as np
+from concourse.bass import DstId, RemoteDMATransfer
+from concourse.mybir import dt, AluOpType, AxisListType, ActivationFunctionType
+
+A = AluOpType
+COPY = ActivationFunctionType.Copy
+IDN = ActivationFunctionType.Identity
+MAGIC = 12582912.0
+
+BC = 2
+SUB = {0: [0, 8, 72, 128], 1: [0, 72, 128]}
+
+
+def _scratch():
+    s = {}
+
+    def sb(name, n, d):
+        s[name] = ("sbuf", [128, n], d)
+    f, b, i, u, h = "float32", "bfloat16", "int32", "uint16", "float16"
+    sb("R", 8192, b)
+    for k in range(2):
+        sb("Y%d" % k, 2048, b); sb("B%d" % k, 2048, b); sb("HI%d" % k, 2048, b); sb("LO%d" % k, 2048, b)
+        sb("al%d" % k, 128, u); sb("nM%d" % k, 128, f); sb("nb%d" % k, 128, b); sb("pr%d" % k, 128, f)
+        sb("aI%d" % k, 128, i); sb("aJ%d" % k, 128, i); sb("rm%d" % k, 128, b); sb("st%d" % k, 128, h)
+        sb("ML%d" % k, 128, h); sb("hs%d" % k, 128, b); sb("ls%d" % k, 128, b)
+        sb("rn%d" % k, 128, b)
+        for p in range(2):
+            sb("L%d%d" % (p, k), 128, f)
+    for t in range(4):
+        sb("MSG%d" % t, 32, u); sb("zo%d" % t, 256, b); sb("zr%d" % t, 256, b); sb("HM%d" % t, 32, u)
+        sb("it%d" % t, 256, f); sb("N%d" % t, 256, f); sb("Hi%d" % t, 256, b)
+        if t:
+            sb("LR%d" % t, 32, u)
+        if t < 3:
+            sb("rb%d" % t, 16, i)
+    sb("Lo", 256, b); sb("e0", 256, b); sb("il", 256, f)
+    sb("zf", 256, b); sb("rM", 128, f)
+    for n in ("uI", "uJ", "uK"):
+        sb(n, 16, i)
+    sb("UL", 16, u); sb("old", 256, b)
+    for n, w in (("OB", 1024), ("PC", 1280), ("OA", 1536), ("SP", 1792)):
+        sb(n, w, f)
+    for n in ("oS", "pS", "rOB", "rPC", "rOA"):
+        sb(n, 1024, h)
+    for n in ("vpI", "voI"):
+        sb(n, 1024, i)
+    sb("mvI", 16, i); sb("mvu", 16, u); sb("wI", 1, i); sb("zn", 256, b); sb("zs", 256, b)
+    sb("L0n", 256, f)
+    for n in ("L0h", "L0A", "L0C", "L1A", "L2H", "L3h", "L3r"):
+        sb(n, 256, h)
+    for n in ("ip", "p16", "pg", "i1", "i2", "i3", "i4", "i5", "i6", "i7", "cAi", "cAj"):
+        sb(n, 1, i)
+    for n in ("pf", "p16f", "pgf", "pg16", "p1", "p2", "k15", "k14", "m0", "m1", "wf", "ck", "cA", "cR", "f1", "f2", "f3",
+              "f4", "f5", "f6", "g1", "g2", "g3", "g4", "g5", "g6", "x128"):
+        sb(n, 1, f)
+    sb("fr", 144, f); sb("fy", 64, f); sb("Dn", 144, b); sb("Dw", 144, b); sb("D16", 144, b)
+    for n in ("I1", "I2", "I4", "I4k", "bda", "bdb", "BD", "WB", "I2e", "cr", "cu", "c32", "ones", "nones"):
+        sb(n, 128, b)
+    sb("ik", 128, f); sb("ck16", 128, f)
+    for n in ("Sh1", "Sh2"):
+        sb(n, 128, b)
+    sb("EX", 2048, b); sb("ind", 16, f); sb("s0", 2048, b); sb("s1", 2048, b)
+    sb("q1", 128, f); sb("Bq", 128, f); sb("Br", 128, f); sb("Bc", 128, f); sb("iy", 128, f); sb("i8", 8, f); sb("k16", 8, f)
+    sb("jp", 96, f)
+    sb("pl", 16, u); sb("yc", 64, i); sb("yq", 64, i); sb("ye", 64, i); sb("yb", 64, i); sb("yd", 64, i); sb("yl", 64, u)
+    sb("hk", 128, f); sb("kall", 64, b)
+    sb("ykr", 768, f); sb("ykr3", 256, f); sb("ykn", 1024, f); sb("ypb", 256, f); sb("yob", 256, f)
+    return s
+
+
+_ALL = _scratch()
+_PACK = {}
+
+
+def _pack():
+    out, width = {}, {}
+    size = {"float32": 4, "int32": 4, "bfloat16": 2, "uint16": 2, "float16": 2}
+    for name, (w, sh, d) in _ALL.items():
+        if sh[1] <= 256:
+            al = 32 // size[d]
+            o = width.get(d, 0)
+            _PACK[name] = ("pk_" + d, o, sh[1])
+            width[d] = o + -(-sh[1] // al) * al
+        else:
+            out[name] = (w, sh, d)
+    for d, w in width.items():
+        out["pk_" + d] = ("sbuf", [128, w], d)
+    for k in range(8):
+        out["P%d" % k] = ("psum", [128, 512], "float32")
+    return out
+
+
+SCRATCH = _pack()
+_ARR = ["aL0", "az0", "aOB", "aPC", "aL0C", "aOA", "aL3"] + ["al%d%d" % (t, h) for t in (1, 2, 3) for h in (0, 1)] \
+    + ["az%d%d" % (t, h) for t in (1, 2, 3, 4) for h in (0, 1)] + ["ah0", "ah1", "ah2", "ah30", "ah31", "aho"]
+SEMAPHORES = ["sV", "sT", "sS", "sG", "ls"] + ["d%d" % k for k in range(20)] + _ARR
+
+
+def rank_program(g, core, T, topo):
+    q = T.rank_of(core)
+    if q is None:
+        return
+    ENG = {"V": g.vector, "T": g.tensor, "S": g.scalar, "G": g, "Y": g.sync}
+    QSEM = {"V": "sV", "T": "sT", "S": "sS", "G": "sG"}
+    cnt = {k: 0 for k in QSEM}
+    clock = {k: {} for k in ENG}
+    last, readers = {}, {}
+    used = {}
+    dn = [0]
+
+    def X(name, a=None, b=None, step=None, rows=None):
+        buf, o, w = _PACK.get(name, (name, 0, None))
+        t = T[buf]
+        if w is None:
+            w = t.shape[1]
+        a = 0 if a is None else a
+        b = w if b is None else b
+        r = slice(0, 128) if rows is None else rows
+        if step is None:
+            return t[r, o + a:o + b]
+        return t[r, o + a:o + b:step]
+
+    def wait(qn, tok):
+        sem, val, snap, _ = tok
+        ck = clock[qn]
+        if ck.get(sem, 0) >= val:
+            return
+        ENG[qn].wait_ge(T.sem[sem], val)
+        ck[sem] = val
+        for s, v in snap.items():
+            if ck.get(s, 0) < v:
+                ck[s] = v
+
+    def before(qn, R, W):
+        for k in R:
+            if k in last:
+                wait(qn, last[k])
+            if k[0] == "P" and k[1].isdigit():
+                for e, tok in readers.get(k, {}).items():
+                    if e != qn:
+                        wait(qn, tok)
+        for k in W:
+            if k in last and (last[k][3] != qn or qn == "Y"):
+                wait(qn, last[k])
+            for e, tok in readers.get(k, {}).items():
+                if e != qn:
+                    wait(qn, tok)
+
+    def after(qn, tok, R, W):
+        for k in R:
+            readers.setdefault(k, {})[qn] = tok
+        for k in W:
+            last[k] = tok
+            readers[k] = {}
+
+    prog, cur = [], [0.0]
+
+    def at(stage):
+        cur[0] = float(stage)
+
+    def op(*a):
+        prog.append((cur[0], len(prog), op_now, a))
+
+    def dma(*a):
+        prog.append((cur[0], len(prog), dma_now, a))
+
+    def send(*a):
+        prog.append((cur[0], len(prog), send_now, a))
+
+    def op_now(qn, calls, R, W):
+        before(qn, R, W)
+        calls = calls if isinstance(calls, list) else [calls]
+        for c in calls:
+            ins = c()
+        cnt[qn] += 1
+        ins.then_inc(T.sem[QSEM[qn]], 1)
+        used[QSEM[qn]] = cnt[qn]
+        after(qn, (QSEM[qn], cnt[qn], dict(clock[qn]), qn), R, W)
+
+    def dma_now(qn, out, in_, R, W):
+        before(qn, R, W)
+        sem = "d%d" % dn[0]
+        dn[0] += 1
+        ENG[qn].dma_start(out, in_).then_inc(T.sem[sem], 16)
+        used[sem] = 16
+        after("D" + sem, (sem, 16, dict(clock[qn]), "D" + sem), R, W)
+
+    def send_now(dst, out, in_, sem, R):
+        before("G", R, [])
+        c = T.cores[dst % 4]
+        rid, pid = topo.addr(c)[:2]
+        m = topo.mask(core, c)
+        g.remote_dma(out, in_, T.sem[sem], T.sem.ls, pid, rid, m)
+        used["ls"] = used.get("ls", 0) + len(topo.engines(core, c))
+
+    def arrives(src, sem, key):
+        n = len(topo.engines(T.cores[src % 4], core))
+        used[sem] = n
+        last[key] = (sem, n, {}, "net")
+        readers[key] = {}
+
+    V, PE, S, G = g.vector, g.tensor, g.scalar, g
+
+    def ts(out, i, s1, s2, o0, o1=None):
+        if o1 is None:
+            return lambda: V.tensor_scalar(out, i, s1, None, o0)
+        return lambda: V.tensor_scalar(out, i, s1, s2, o0, o1)
+
+    def tt(out, a, b, o):
+        return lambda: V.tensor_tensor(out, a, b, o)
+
+    def cp(out, a):
+        return lambda: V.tensor_copy(out, a)
+
+    def act(out, a, f=COPY, **kw):
+        return lambda: S.activation(out, a, f, **kw)
+
+    def mm(out, l, r, st=True, sp=True):
+        return lambda: PE.matmul(out, l, r, st, sp)
+
+    def vts(o, i, s1, s2, o0, o1=None, R=()):
+        rd = [i] + [s for s in (s1, s2) if isinstance(s, str)]
+        f = lambda s: X(s) if isinstance(s, str) else s
+        op("V", ts(X(o), X(i), f(s1), f(s2), o0, o1), rd, [o])
+
+    at(-10)
+    dma("Y", X("mvI"), T.mv[:, :], [], ["mvI"])
+    dma("Y", X("vpI"), T.vp[:, :], [], ["vpI"])
+    dma("S", X("zn"), T.z0[:, :], [], ["zn"])
+    dma("S", X("wI"), T.wt[:, :], [], ["wI"])
+    dma("Y", X("R", 0, 4096), T.strat[:, 0:4096], [], ["Ra"])
+    dma("S", X("R", 4096, 8192), T.strat[:, 4096:8192], [], ["R"])
+    dma("Y", X("voI"), T.vo[:, :], [], ["voI"])
+    at(-9)
+
+    def iota(name, pattern, base=0, cm=0, a=None, b=None, integer=False, key=None, early=None):
+        o = X(name, a, b)
+        at0 = cur[0]
+        at(at0 if early is None else early)
+        if integer:
+            op("G", lambda: G.iota(o, pattern, base, cm), [], [key or name])
+        else:
+            op("G", lambda: G.iota(o, pattern, base, cm, allow_small_or_imprecise_dtypes=True), [], [key or name])
+        at(at0)
+
+    iota("ip", [[0, 1]], 0, 1, integer=True)
+    iota("jp", [[128, 2], [1, 4], [64, 2]], a=0, b=16, key="jp0")
+    vts("p16", "ip", 15, None, A.bitwise_and)
+    vts("g1", "p16", 4.0, None, A.mult)
+    op("V", cp(X("mvu"), X("mvI")), ["mvI"], ["mvu"])
+    op("V", ts(X("pl"), X("jp", 0, 16), X("g1"), None, A.add), ["jp0", "g1"], ["pl"])
+    op("V", cp(X("L0n"), X("vpI").indirect(X("mvu"))), ["vpI", "mvu"], ["L0n"])
+    op("V", cp(X("L0h"), X("L0n").indirect(X("pl"))), ["L0n", "pl"], ["L0h"])
+    op("S", act(X("zs"), X("zn").indirect(X("pl"))), ["zn", "pl"], ["zs"])
+    send(q + 1, X("zr0"), X("zs"), "az0", ["zs"])
+    send(q + 1, X("L0A"), X("L0h"), "aL0", ["L0h"])
+    arrives(q - 1, "az0", "zr0"); arrives(q - 1, "aL0", "L0A")
+
+    iota("fr", [[1, 144]], -16, early=-9.5)
+    vts("pg", "ip", 112, None, A.bitwise_and)
+    op("V", cp(X("pf"), X("ip")), ["ip"], ["pf"])
+    op("V", cp(X("p16f"), X("p16")), ["p16"], ["p16f"])
+    op("V", cp(X("pgf"), X("pg")), ["pg"], ["pgf"])
+    op("V", cp(X("wf"), X("wI")), ["wI"], ["wf"])
+    op("V", ts(X("I1"), X("fr", 16, 144), X("pf"), None, A.is_equal), ["fr", "pf"], ["I1"])
+    vts("pg16", "pgf", 16.0, None, A.add)
+    vts("m0", "p16f", 0.0, None, A.is_equal)
+    vts("ck", "p16f", 1184.0, None, A.mult)
+    fr = X("fr", 16, 144)
+    op("V", ts(X("bda"), fr, X("pgf"), None, A.is_ge), ["fr", "pgf"], ["bda"])
+    op("V", ts(X("bdb"), fr, X("pg16"), None, A.is_lt), ["fr", "pg16"], ["bdb"])
+    op("V", tt(X("BD"), X("bda"), X("bdb"), A.mult), ["bda", "bdb"], ["BD"])
+    op("S", act(X("WB"), X("BD"), scale=X("wf")), ["BD", "wf"], ["WB"])
+    op("S", act(X("I4k"), X("I1"), scale=-4096.0), ["I1"], ["I4k"])
+    op("V", lambda: V.memset(X("cu", rows=slice(0, 64)), -32.0), [], ["cu"])
+    op("V", lambda: V.memset(X("cu", rows=slice(64, 128)), 2.0 ** -7), [], ["cu"])
+    for n, v in (("ones", 1.0), ("c32", 0.25)):
+        op("V", lambda n=n, v=v: V.memset(X(n), v), [], [n])
+    op("V", ts(X("D16"), X("fr"), X("pgf"), None, A.is_equal), ["fr", "pgf"], ["D16"])
+    op("S", act(X("Dw"), X("D16"), scale=X("wf")), ["D16", "wf"], ["Dw"])
+    op("S", act(X("Dn"), X("D16"), scale=-1.0), ["D16"], ["Dn"])
+    op("V", ts(X("ind"), X("fr", 16, 32), X("p16f"), None, A.is_equal), ["fr", "p16f"], ["ind"])
+    for x in range(16):
+        op("S", act(X("EX", 128 * x, 128 * x + 128), X("BD"), scale=X("ind", x, x + 1)), ["BD", "ind"], ["EX%d" % x])
+    at(-7.5)
+    op("V", cp(X("pS"), X("vpI")), ["vpI"], ["pS"])
+    at(2)
+    send(q + 3, X("rPC"), X("pS"), "aPC", ["pS"])
+    send(q + 3, X("L0C"), X("L0h"), "aL0C", ["L0h"])
+    arrives(q - 2, "aOB", "rOB"); arrives(q + 1, "aPC", "rPC"); arrives(q + 1, "aL0C", "L0C"); arrives(q - 1, "aOA", "rOA")
+
+    at(-7)
+    op("V", lambda: V.memset(X("s0"), 1.0), [], ["s0"])
+    op("V", lambda: V.memset(X("s0", 0, 2048, 16), 0.0), ["s0"], ["s0"])
+    at(2)
+    op("S", act(X("s1"), X("s0"), IDN, bias=256.0, scale=-256.0), ["s0"], ["s1"])
+    at(-7)
+    op("V", lambda: V.memset(X("q1"), -10.0), [], ["q1"])
+    op("V", lambda: V.memset(X("q1", 15, 128, 16), -9.0), ["q1"], ["q1"])
+    iota("iy", [[16, 8], [0, 16]], early=-9.5)
+    iota("i8", [[16, 8]], early=-9.5)
+    vts("x128", "p16f", 128.0, None, A.mult)
+    vts("Bq", "iy", "x128", 150.0, A.add, A.add)
+    op("V", ts(X("Br"), X("s0", 0, 128), -30000.0, None, A.mult), ["s0"], ["Br"])
+    op("V", tt(X("Bc"), X("Bq"), X("Br"), A.add), ["Bq", "Br"], ["Bc"])
+    at(1)
+    vts("k16", "i8", "x128", None, A.add)
+    for n, v in (("cr", -3 * 2.0 ** -10), ("nones", -1.0)):
+        op("V", lambda n=n, v=v: V.memset(X(n), v), [], [n])
+    iota("ik", [[16, 128]], early=-9.5)
+    op("S", act(X("ck16"), X("ik"), IDN, bias=X("p16f")), ["ik", "p16f"], ["ck16"])
+    at(-7)
+    op("S", act(X("I2"), X("I1"), scale=0.5), ["I1"], ["I2"])
+    op("S", act(X("I2e"), X("I1"), scale=0.5 - 2.0 ** -9), ["I1"], ["I2e"])
+    op("S", act(X("I4"), X("I1"), scale=0.25), ["I1"], ["I4"])
+    pats = [[[128, 2], [1, 32], [32, 4]], [[128, 2], [1, 2], [2, 64]], [[128, 2], [1, 16], [16, 8]], [[1, 256]]]
+    for t in range(4):
+        at(1)
+        iota("it%d" % t, pats[t], 1024 + 256 * t)
+
+    at(1)
+    vts("i1", "p16", 3, None, A.bitwise_and)
+    vts("i2", "p16", 2, None, A.arith_shift_right)
+    vts("i3", "p16", 7, None, A.bitwise_and)
+    vts("i4", "p16", 3, None, A.arith_shift_right)
+    op("V", cp(X("f2"), X("i2")), ["i2"], ["f2"])
+    op("V", cp(X("f4"), X("i4")), ["i4"], ["f4"])
+    vts("f1", "i1", 32.0, "f2", A.mult, A.add)
+    vts("f3", "i3", 16.0, "f4", A.mult, A.add)
+    vts("g2", "p16f", 2.0, None, A.mult)
+    iota("jp", [[128, 2], [4, 8]], a=16, b=32, key="jp1")
+    iota("jp", [[128, 2], [1, 2], [32, 4]], a=32, b=48, key="jp2")
+    iota("jp", [[128, 2], [2, 8]], a=48, b=64, key="jp3")
+    for t, (k, c) in enumerate(((1, "f1"), (2, "g2"), (3, "f3"))):
+        op("V", ts(X("rb%d" % t), X("jp", 16 * k, 16 * k + 16), X(c), 32.0, A.add, A.mult), ["jp%d" % k, c], ["rb%d" % t])
+
+    def late_constants():
+        for n, d in (("Sh1", 1), ("Sh2", 2)):
+            op("G", lambda n=n, d=d: G.affine_select(X(n), X("BD"), [[1, 128]], A.is_equal, 0.0, -d, -1), ["BD"], [n])
+        iota("il", [[1, 256]])
+
+    def number_n(k):
+        op("S", act(X("N%d" % k), X("it%d" % k), scale=X("m0")), ["it%d" % k, "m0"], ["N%d" % k])
+
+    def number_lo():
+        op("S", act(X("Lo"), X("il"), scale=X("m0")), ["il", "m0"], ["Lo"])
+        op("S", act(X("e0"), X("il"), IDN, scale=0.0, bias=X("m0")), ["il", "m0"], ["e0"])
+
+    def number_hi(k):
+        op("S", act(X("Hi%d" % k), X("e0"), scale=1024.0 + 256 * k), ["e0"], ["Hi%d" % k])
+
+    for k, pat in enumerate(([[0, 2], [4, 8]], [[0, 2], [1, 4], [64, 2]], [[0, 2], [8, 8]], [[0, 2], [1, 8]])):
+        iota("fy", pat, a=16 * k, b=16 * k + 16, key="fy%d" % k, early=2.5)
+    iota("yb", [[16, 4], [8, 2], [0, 8]], integer=True, early=2.5)
+
+    def verdicts_home(k):
+        op("V", cp(X("hk", 32 * k, 32 * k + 32), X("HM%d" % k)), ["HM%d" % k], ["hk%d" % k])
+        for h in range(2):
+            c = 32 * k + 16 * h + 8
+            op("V", tt(X("kall", 16 * k + 8 * h, 16 * k + 8 * h + 8), X("hk", c, c + 8), X("k16"), A.subtract),
+               ["hk%d" % k, "k16"], ["kall"])
+
+    def list_constants(part):
+        if part == 0:
+            vts("i5", "p16", 1, None, A.bitwise_and)
+            vts("i6", "p16", 1, None, A.arith_shift_right)
+            op("V", cp(X("f6"), X("i6")), ["i6"], ["f6"])
+            vts("f5", "i5", 64.0, "f6", A.mult, A.add)
+            vts("g3", "p16f", 8.0, None, A.mult)
+            return
+        for t, c in enumerate(("f1", "g1", "f5", "g3")):
+            op("V", ts(X("yc", 16 * t, 16 * t + 16), X("fy", 16 * t, 16 * t + 16), X(c), None, A.add), ["fy%d" % t, c], ["yc"])
+        vts("yq", "yc", 3, None, A.arith_shift_right)
+        op("V", ts(X("ye", 0, 48), X("yq", 0, 48), 40.0, None, A.mult), ["yq"], ["ye"])
+        op("V", ts(X("ye", 48, 64), X("yq", 48, 64), 8.0, None, A.mult), ["yq"], ["ye"])
+        op("V", tt(X("yd"), X("ye"), X("yc"), A.add), ["ye", "yc"], ["yd"])
+        op("V", tt(X("yq"), X("yd"), X("yb"), A.add), ["yd", "yb"], ["yq"])
+        op("V", cp(X("yl", 0, 48), X("yq", 0, 48)), ["yq"], ["yl"])
+        op("V", ts(X("yl", 48, 64), X("yq", 48, 64), -48.0, None, A.add), ["yq"], ["yl"])
+
+    def half(h):
+        return 128 * h, 128 * h + 128
+
+    def zkey(t, h):
+        return "zr0" if t == 0 else "zr%d%d" % (t, h)
+
+    for t in (1, 2, 3):
+        src = q - 1 if t < 3 else q + 2
+        for h in range(2):
+            arrives(src, "al%d%d" % (t, h), "LR%d%d" % (t, h))
+            arrives(src, "az%d%d" % (t, h), "zr%d%d" % (t, h))
+    for t in range(4):
+        src = q + 1 + t % 3
+        if t < 3:
+            arrives(src, "ah%d" % t, "HM%d" % t)
+        else:
+            for h in range(2):
+                arrives(src, "ah3%d" % h, "HM3%d" % h)
+                arrives(src, "az4%d" % h, "zf%d" % h)
+            arrives(src, "aL3", "L3r")
+            arrives(src, "aho", "HM3o")
+
+    def Lk(t, h):
+        return "L%d%d" % (t % 2, h)
+
+    def pre_L(t, h):
+        a, b = half(h)
+        k = Lk(t, h)
+        if t == 0:
+            op("V", cp(X(k), X("L0A", a, b)), ["L0A"], [k])
+        else:
+            w = ("OB", "PC", "OA")[t - 1]
+            op("V", tt(X(k), X(w).indirect(X("LR%d" % t, 16 * h, 16 * h + 8)), X("N%d" % (t - 1), a, b), A.add),
+               [w, "LR%d%d" % (t, h), "N%d" % (t - 1)], [k])
+
+    def pre_n(t, h):
+        a, b = half(h)
+        z, zk, pu = X("zr%d" % t, a, b), zkey(t, h), "P%d" % (2 + h)
+        o = X(pu, 0, 128)
+        op("T", [mm(o, X("cu"), X("ones"), True, False)], ["cu", "ones"], [pu])
+        op("T", [mm(o, X("WB"), z, False, True)], ["WB", zk], [pu])
+        op("S", act(X("nM%d" % h), o, IDN, bias=MAGIC, scale=2.0 ** -12), [pu], ["nM%d" % h])
+        op("S", act(X("nb%d" % h), X("nM%d" % h), IDN, bias=-MAGIC), ["nM%d" % h], ["nb%d" % h])
+
+    def pre_u(t, h):
+        a, b = half(h)
+        z, zk, pu = X("zr%d" % t, a, b), zkey(t, h), "P%d" % (2 + h)
+        o = X(pu, 128, 256)
+        op("T", [mm(o, X("c32"), X("ones"), True, False), mm(o, X("WB"), z, False, False)], ["c32", "ones", "WB", zk], [pu])
+        op("T", [mm(o, X("I4k"), X("nb%d" % h), False, True)], ["I4k", "nb%d" % h], [pu])
+
+    def pre_z(t, h):
+        a, b = half(h)
+        op("T", [mm(X("P%d" % h, d, 512, 4), X("I1"), X("zr%d" % t, a, b)) for d in range(4)], ["I1", zkey(t, h)], ["P%d" % h])
+
+    def slist(t, h):
+        a, b = half(h)
+        if t < 3:
+            op("T", [mm(X("P6", 256 + 8 * h, 264 + 8 * h), X("Dw", 16 - x, 144 - x), X("zr%d" % t, a + 8 * x, a + 8 * x + 8),
+                        x == 0, x == 15) for x in range(16)], ["Dw", zkey(t, h)], ["P6"])
+
+    def pre_a(t, h):
+        pu = "P%d" % (2 + h)
+        op("V", tt(X("pr%d" % h), X(pu, 128, 256), X(Lk(t, h)), A.mult), [pu, Lk(t, h)], ["pr%d" % h])
+
+    def pre_b(t, h):
+        k = "cA" if t else "ck"
+        op("V", ts(X("aI%d" % h), X("pr%d" % h), X(k), None, A.add), ["pr%d" % h, k], ["aI%d" % h])
+        op("V", ts(X("aJ%d" % h), X("aI%d" % h), 5, 8191, A.arith_shift_right, A.bitwise_and), ["aI%d" % h], ["aJ%d" % h])
+        op("V", cp(X("al%d" % h), X("aJ%d" % h)), ["aJ%d" % h], ["al%d" % h])
+
+    def ulist(t):
+        op("V", cp(X("uI"), X("P6", 256, 272)), ["P6"], ["uI"])
+        vts("uJ", "uI", 31, None, A.bitwise_and)
+        op("V", tt(X("uK"), X("uJ"), X("rb%d" % t), A.add), ["uJ", "rb%d" % t], ["uK"])
+        op("V", cp(X("UL"), X("uK")), ["uK"], ["UL"])
+
+    def gather(t, h, j):
+        a, b = SUB[h][j], SUB[h][j + 1]
+        o, i = X("Y%d" % h, 16 * a, 16 * b), X("R").indirect(X("al%d" % h, a, b))
+        v = h == 0 and j == 0
+        op("V" if v else "S", cp(o, i) if v else act(o, i), ["R", "Ra", "al%d" % h], ["Y%d_%d" % (h, j)])
+
+    def compare(t, h, j, ds=(0, 1, 2, 3)):
+        a, b = 16 * SUB[h][j], 16 * SUB[h][j + 1]
+        for d in ds:
+            op("V", tt(X("B%d" % h, a + d, b, 4), X("Y%d" % h, a + d, b, 4), X("P%d" % h, a // 4, b // 4), A.is_gt),
+               ["Y%d_%d" % (h, j), "P%d" % h], ["B%d_%d" % (h, j)])
+
+    def counts(t, h, j):
+        pc = "P%d" % (4 + h)
+        op("T", [mm(X(pc, 0, 128), X("Dn", 16 - x, 144 - x), X("B%d" % h, 128 * x, 128 * x + 128), x == 0, x == 15)
+                 for x in range(SUB[h][j] // 8, SUB[h][j + 1] // 8)], ["Dn", "B%d_%d" % (h, j)], [pc])
+
+    def scans(t, h):
+        scan_hi(t, h)
+        scan_lo(t, h)
+
+    def scan_hi(t, h):
+        yk = ["Y%d_%d" % (h, j) for j in range(len(SUB[h]) - 1)]
+        op("V", lambda: V.tensor_tensor_scan(X("HI%d" % h), X("s0"), X("Y%d" % h), 0.0, A.mult, A.max), ["s0"] + yk, ["HI%d" % h])
+
+    def scan_lo(t, h):
+        yk = ["Y%d_%d" % (h, j) for j in range(len(SUB[h]) - 1)]
+        op("V", lambda: V.tensor_tensor_scan(X("LO%d" % h), X("s1"), X("Y%d" % h), 0.0, A.max, A.min), ["s1"] + yk, ["LO%d" % h])
+
+    def offs(t, h):
+        c = 16 * h + 8 if t < 3 else 16 + 8 * h
+        return X("MSG%d" % t, c, c + 8)
+
+    def lmov(t, h):
+        c = 16 * h if t < 3 else 8 * h
+        return X("MSG%d" % t, c, c + 8)
+
+    def verdict(t, h):
+        pc = "P%d" % (4 + h)
+        op("V", lambda: V.tensor_tensor_scan(X("rm%d" % h), X(pc, 0, 128), X("q1"), -9.0, A.min, A.max), [pc, "q1"], ["rm%d" % h])
+        op("V", lambda: V.tensor_tensor_scan(X("st%d" % h), X("Bc"), X("rm%d" % h), 0.0, A.max, A.add), ["Bc", "rm%d" % h],
+           ["st%d" % h])
+        op("V", cp(offs(t, h), X("st%d" % h, 14, 128, 16)), ["st%d" % h], ["of%d%d" % (t, h)])
+
+    def select(t, h, lo_on_v=False):
+        for s, w in (("hs%d" % h, "HI%d" % h), ("ls%d" % h, "LO%d" % h)):
+            i = X(w).indirect(offs(t, h))
+            if lo_on_v and s[0] == "l":
+                op("V", cp(X(s), i), [w, "of%d%d" % (t, h)], [s])
+            else:
+                op("S", act(X(s), i), [w, "of%d%d" % (t, h)], [s])
+
+    def newz_pe(t, h):
+        pu = "P%d" % (2 + h)
+        o = X(pu, 256, 384)
+        op("T", [mm(o, X("I2"), X("ls%d" % h), True, False)], ["I2", "ls%d" % h], [pu])
+        op("T", [mm(o, X("I2e"), X("hs%d" % h), False, True)], ["I2e", "hs%d" % h], [pu])
+
+    def rounded(h, out, in_, ki, ko):
+        if ko == "rn0":
+            m = "rM"
+            op("S", act(X(m), in_, IDN, bias=MAGIC), [ki], [m])
+            op("S", act(out, X(m), IDN, bias=-MAGIC), [m], [ko])
+        else:
+            op("V", ts(out, in_, MAGIC, MAGIC, A.add, A.subtract), [ki], [ko])
+
+    def newz(t, h):
+        a, b = half(h)
+        pu = "P%d" % (2 + h)
+        o = X(pu, 256, 384)
+        rounded(h, X("zo%d" % t, a, b), o, pu, "zo%d%d" % (t, h))
+        if t < 3:
+            send(q + 1 if t < 2 else q + 2, X("zr%d" % (t + 1), a, b), X("zo%d" % t, a, b), "az%d%d" % (t + 1, h), ["zo%d%d" % (t, h)])
+        else:
+            send(q - 1, X("zf", a, b), X("zo3", a, b), "az4%d" % h, ["zo3%d" % h])
+
+    def moves_pe(t, h, a=0, b=16):
+        pc = "P%d" % (4 + h)
+        op("T", [mm(X(pc, 128 + 8 * x, 136 + 8 * x), X("EX", 128 * x, 128 * x + 128), X("st%d" % h, 14, 128, 16)) for x in range(a, b)],
+           ["EX%d" % x for x in range(a, b)] + ["st%d" % h], [pc])
+
+    def moves_v(t, h, a=0, b=16):
+        pc = "P%d" % (4 + h)
+        a, b = 8 * a, 8 * b
+        op("V", tt(X(pc, 256 + a, 256 + b), X(pc, 128 + a, 128 + b), X("ck16", a, b), A.is_equal), [pc, "ck16"], [pc])
+        op("V", tt(X("ML%d" % h, a, b), X(pc, 256 + a, 256 + b), X(Lk(t, h), a, b), A.mult), [pc, Lk(t, h)], ["ML%d_%d" % (h, a)])
+
+    def moves_f(t, h, a=0, b=16):
+        pc = "P%d" % (4 + h)
+        op("T", [mm(X(pc, 384, 392), X("D16", 16 - x, 144 - x), X("ML%d" % h, 8 * x, 8 * x + 8), x == 0, x == 15)
+                 for x in range(a, b)], ["D16", "ML%d_%d" % (h, 8 * a)], [pc])
+
+    def moves_a(t, h):
+        moves_v(t, h)
+        moves_f(t, h)
+
+    def moves_b(t, h):
+        pc = "P%d" % (4 + h)
+        op("V", cp(lmov(t, h), X(pc, 384, 392)), [pc], ["lk%d%d" % (t, h)])
+        m = X("MSG%d" % t, 16 * h, 16 * h + 16)
+        ks = ["lk%d%d" % (t, h), "of%d%d" % (t, h)]
+        if t < 3:
+            send(q + 1 if t < 2 else q + 2, X("LR%d" % (t + 1), 16 * h, 16 * h + 16), m, "al%d%d" % (t + 1, h), ks)
+        else:
+            send(q - 1, X("HM3", 8 * h, 8 * h + 8), lmov(3, h), "ah3%d" % h, ks[:1])
+
+    def home_list(t):
+        send(q - 1 - t % 3, X("HM%d" % t), X("MSG%d" % t), "ah%d" % t, ["%s%d%d" % (k, t, h) for k in ("lk", "of") for h in (0, 1)])
+
+    def number_pe(t):
+        o = X("P5", 400, 408)
+        op("T", [mm(o, X("nones"), X("rm%d" % h, 14, 128, 16), h == 0, h == 1) for h in range(2)], ["nones", "rm0", "rm1"], ["P5"])
+
+    def number(t):
+        op("V", lambda: V.tensor_reduce(X("cR"), X("P5", 400, 408), AxisListType.X, A.add), ["P5"], ["cR"])
+        op("V", cp(X("cAi"), X("cR")), ["cR"], ["cAi"])
+        vts("cAj", "cAi", 255, None, A.bitwise_and)
+        vts("cA", "cAj", 32.0, "ck", A.mult, A.add)
+
+    def old(t):
+        op("S", act(X("old"), X("R").indirect(X("UL"))), ["R", "Ra", "UL"], ["old"])
+
+    def strat_pe(t, h):
+        a, b = half(h)
+        o = X("P6", a, b)
+        op("T", [mm(o, X("I4"), X("ls%d" % h), False, False), mm(o, X("I4"), X("hs%d" % h), False, True)],
+           ["I4", "hs%d" % h, "ls%d" % h], ["P6"])
+
+    def strat_pre(t, h):
+        a, b = half(h)
+        o = X("P6", a, b)
+        op("T", [mm(o, X("cr"), X("ones"), True, False), mm(o, X("I2"), X("old", a, b), False, False)],
+           ["cr", "ones", "I2", "old"], ["P6"])
+
+    def strat_r(t, h):
+        a, b = half(h)
+        rounded(h, X("rn%d" % h), X("P6", a, b), "P6", "rn%d" % h)
+
+    def strat_v(t, h):
+        op("V", cp(X("R").indirect(X("UL", 8 * h, 8 * h + 8)), X("rn%d" % h)), ["rn%d" % h, "UL"], ["R"])
+
+    def table(w, r, banks=("P0", "P7")):
+        for k in range(2):
+            a, p = 512 * k, banks[k]
+            op("T", mm(X(p), X("Sh1"), X(r, a, a + 512)), ["Sh1", r], [p])
+            op("S", act(X(w, a, a + 512), X(p)), [p], [w])
+
+    def runs(t):
+        if t == 0:
+            return [((32 * b, 32 * b + 32, None), (b, 128, 4)) for b in range(4)]
+        if t == 1:
+            return [((b, 128, 4), (32 * b, 32 * b + 32, None)) for b in range(4)]
+        if t == 2:
+            return [((64 * b, 64 * b + 64, None), (b, 128, 2)) for b in range(2)]
+        return [((b, 128, 8), (16 * b, 16 * b + 16, None)) for b in range(8)]
+
+    def permuted(at, sh, Lb, t, nf, shn):
+        cs = []
+        for h in range(2):
+            for (a, b, st), (c, d, dst) in runs(t):
+                o = X("P7", at + 128 * h + c, at + 128 * h + d, dst)
+                cs.append((o, X(sh), X(Lb, 128 * h + a, 128 * h + b, st)))
+        if nf is None:
+            return [mm(*c) for c in cs]
+        o = X("P7", at, at + 256)
+        return [mm(o, X(shn), X("Lo"), True, False), mm(o, X(shn), X("Hi%d" % nf), False, False)] + [
+            mm(*c, False, c is cs[-1]) for c in cs]
+
+    def shifted(w, at, Lb, t, t_before, t_mover):
+        shifted_pe(Lb, t, t_before, t_mover)
+        shifted_act(w, at, t_before)
+
+    def shifted_act(w, at, t_before):
+        n = 512 if t_before else 256
+        op("S", act(X(w, at, at + n), X("P7", 0, n)), ["P7"], [w])
+
+    def shifted_pe(Lb, t, t_before, t_mover):
+        n = 0
+        cs = []
+        if t_before:
+            cs += permuted(0, "Sh1", Lb, t, None, None)
+            n = 256
+        cs += permuted(n, "Sh2", Lb, t, t_mover, "Sh1")
+        op("T", cs, ["Sh1", "Sh2", Lb, "Lo", "Hi%d" % t_mover], ["P7"])
+
+    def resumed(Lb, w, lst, keys, t):
+        for h in range(2):
+            a, b = half(h)
+            op("V", tt(X(Lb, a, b), X(w).indirect(X(lst, 16 * h, 16 * h + 8)), X("N%d" % t, a, b), A.add),
+               [w, "N%d" % t] + keys, [Lb])
+
+    for t in range(4):
+        at(0 if t == 0 else 10 * t)
+        if t == 0:
+            pre_L(0, 0); pre_n(0, 0); pre_n(0, 1)
+            for h in range(2):
+                if h:
+                    pre_L(0, 1)
+                pre_u(0, h); pre_z(0, h); pre_a(0, h); pre_b(0, h)
+        for j in range(2 if t else 0, len(SUB[0]) - 1):
+            gather(t, 0, j)
+        slist(t, 0)
+        if t == 0:
+            slist(t, 1)
+            at(2)
+            late_constants()
+            at(4)
+        if t == 0:
+            compare(t, 0, 0)
+            counts(t, 0, 0)
+            gather(t, 1, 0)
+            op("V", cp(X("oS"), X("voI")), ["voI"], ["oS"])
+            send(q + 2, X("rOB"), X("oS"), "aOB", ["oS"])
+        if t:
+            table(("PC", "OA", "SP")[t - 1], ("rPC", "rOA", "pS")[t - 1], ("P7", "P5"))
+        for j in range(1, len(SUB[0]) - 1):
+            compare(t, 0, j)
+            if j == len(SUB[0]) - 2:
+                if t:
+                    pre_n(t, 1)
+                    pre_u(t, 1)
+                    pre_z(t, 1)
+            counts(t, 0, j)
+        if t:
+            slist(t, 1)
+            scan_hi(t, 0)
+            pre_L(t, 1); pre_a(t, 1); pre_b(t, 1)
+            gather(t, 1, 0)
+        if t == 1:
+            shifted_pe("L0C", 0, False, 0)
+        if t == 2:
+            resumed("L1A", "OA", "MSG0", ["lk00", "lk01"], 0)
+            shifted_pe("L1A", 1, True, 1)
+        if t == 3:
+            shifted_pe("L0h", 0, False, 0)
+        if t == 3:
+            for h in range(2):
+                op("V", cp(X("L3h", *half(h)), X(Lk(3, h))), [Lk(3, h)], ["L3h"])
+            send(q - 1, X("L3r"), X("L3h"), "aL3", ["L3h"])
+        if t == 0:
+            scan_hi(t, 0)
+        scan_lo(t, 0)
+        verdict(t, 0)
+        select(t, 0)
+        for j in range(1, len(SUB[1]) - 1):
+            gather(t, 1, j)
+        if t < 3:
+            ulist(t)
+            old(t)
+        moves_pe(t, 0, 0, BC)
+        newz_pe(t, 0)
+        moves_pe(t, 0, BC, 16)
+        compare(t, 1, 0, (0, 1))
+        newz(t, 0)
+        compare(t, 1, 0, (2, 3))
+        moves_a(t, 0)
+        if t == 0:
+            number_n(0)
+        else:
+            shifted_act(("PC", "OA", "SP")[t - 1], 1024, t == 2)
+        if t < 3:
+            strat_pre(t, 0)
+            strat_pe(t, 0)
+            strat_r(t, 0)
+        if t == 0:
+            number_lo()
+            number_hi(0)
+        if t == 1:
+            for k in (1, 2, 3):
+                number_n(k)
+                number_hi(k)
+        counts(t, 1, 0)
+        for j in range(1, len(SUB[1]) - 1):
+            compare(t, 1, j)
+            counts(t, 1, j)
+        moves_b(t, 0)
+        if t < 3:
+            strat_pre(t, 1)
+        if t == 0:
+            table("OB", "rOB", ("P1", "P7"))
+        scans(t, 1)
+        if t < 3:
+            strat_v(t, 0)
+        verdict(t, 1)
+        if t == 3:
+            send(q - 1, X("HM3", 16, 32), X("MSG3", 16, 32), "aho", ["of30", "of31"])
+        if t < 3:
+            number_pe(t)
+            pre_n(t + 1, 0)
+        select(t, 1, t == 3)
+        if t < 3:
+            number(t)
+            moves_pe(t, 1, 0, BC)
+            pre_u(t + 1, 0)
+            pre_z(t + 1, 0)
+            strat_pe(t, 1)
+            newz_pe(t, 1)
+            moves_pe(t, 1, BC, 16)
+            pre_L(t + 1, 0)
+            pre_a(t + 1, 0); pre_b(t + 1, 0)
+            strat_r(t, 1)
+            strat_v(t, 1)
+            newz(t, 1)
+            gather(t + 1, 0, 0)
+            moves_a(t, 1)
+            compare(t + 1, 0, 0)
+            counts(t + 1, 0, 0)
+            gather(t + 1, 0, 1)
+            if t == 2:
+                verdicts_home(0)
+                verdicts_home(1)
+            else:
+                list_constants(t)
+            moves_b(t, 1)
+            home_list(t)
+            if t == 0:
+                send(q + 1, X("rOA"), X("oS"), "aOA", ["oS"])
+        else:
+            moves_pe(t, 1, 0, 8)
+            moves_pe(t, 1, 8, 16)
+            newz_pe(t, 1)
+            moves_v(t, 1, 0, 8)
+            moves_f(t, 1, 0, 8)
+            verdicts_home(2)
+            moves_v(t, 1, 8, 16)
+            moves_f(t, 1, 8, 16)
+            newz(t, 1)
+            op("T", permuted(0, "Sh1", "L3r", 3, 3, "I1"), ["Sh1", "I1", "L3r", "Lo", "Hi3"], ["P7"])
+            op("S", act(X("yob"), X("P7", 0, 256)), ["P7"], ["yob"])
+            dma("Y", T.yo[:, :], X("yob"), ["yob"], [])
+            for k in range(2):
+                op("T", [mm(X("P%d" % k, 48 * x, 48 * x + 48), X("EX", 128 * (8 * k + x), 128 * (8 * k + x) + 128), X("kall", 0, 48))
+                         for x in range(8)],
+                   ["kall"] + ["EX%d" % x for x in range(16)], ["P%d" % k])
+                op("S", act(X("ykr", 384 * k, 384 * k + 384), X("P%d" % k, 0, 384)), ["P%d" % k], ["ykr"])
+            moves_b(t, 1)
+            resumed("L2H", "SP", "HM1", ["HM1"], 1)
+            shifted("SP", 1280, "L2H", 2, True, 2)
+            op("V", cp(X("hk", 96, 112), X("HM3", 16, 32)), ["HM3o"], ["hk3"])
+            for h in range(2):
+                op("V", tt(X("kall", 48 + 8 * h, 56 + 8 * h), X("hk", 96 + 8 * h, 104 + 8 * h), X("k16"), A.subtract),
+                   ["hk3", "k16"], ["kal3"])
+
+    at(50)
+    op("T", [mm(X("P2", 16 * x, 16 * x + 16), X("EX", 128 * x, 128 * x + 128), X("kall", 48, 64)) for x in range(16)],
+       ["kal3"] + ["EX%d" % x for x in range(16)], ["P2"])
+    op("S", act(X("ykn", 0, 768), X("ykr", 0, 768).indirect(X("yl", 0, 48))), ["ykr", "yl"], ["ykn"])
+
+    def yp_half(h):
+        a, b = half(h)
+        op("V", tt(X("ypb", a, b), X("SP").indirect(X("HM3", 8 * h, 8 * h + 8)), X("N3", a, b), A.add),
+           ["SP", "HM3%d" % h, "N3"], ["ypb"])
+
+    yp_half(0)
+    yp_half(1)
+    dma("Y", T.yz[:, :], X("zf"), ["zf0", "zf1"], [])
+    dma("Y", T.yp[:, :], X("ypb"), ["ypb"], [])
+    op("S", act(X("ykr3"), X("P2", 0, 256)), ["P2"], ["ykr3"])
+    op("S", act(X("ykn", 768, 1024), X("ykr3").indirect(X("yl", 48, 64))), ["ykr3", "yl"], ["ykn"])
+    dma("S", T.yk[:, :], T["ykn"][0:128:16, :], ["ykn"], [])
+    prog.sort(key=lambda e: e[:2])
+    for _, _, f, a in prog:
+        f(*a)
+    for sem, v in used.items():
+        if clock["G"].get(sem, 0) < v:
+            g.wait_ge(T.sem[sem], v)

@@ -6,10 +6,11 @@ from concourse.mybir import dt, AluOpType, AxisListType, ActivationFunctionType
 A = AluOpType
 COPY = ActivationFunctionType.Copy
 IDN = ActivationFunctionType.Identity
+SIGN = ActivationFunctionType.Sign
 MAGIC = 12582912.0
-
-BC = 2
-SUB = {0: [0, 8, 72, 128], 1: [0, 72, 128]}
+BIG = 8192.0
+STEP = 2048.0
+USES_OTHERS = True
 
 
 def _scratch():
@@ -18,54 +19,35 @@ def _scratch():
     def sb(name, n, d):
         s[name] = ("sbuf", [128, n], d)
     f, b, i, u, h = "float32", "bfloat16", "int32", "uint16", "float16"
-    sb("R", 8192, b)
+    sb("R", 9216, b); sb("Y", 4096, b); sb("HI", 4096, b); sb("LO", 4096, b)
+    s["B"] = ("sbuf", [128, 16, 256], b)
     for k in range(2):
-        sb("Y%d" % k, 2048, b); sb("B%d" % k, 2048, b); sb("HI%d" % k, 2048, b); sb("LO%d" % k, 2048, b)
-        sb("al%d" % k, 128, u); sb("nM%d" % k, 128, f); sb("nb%d" % k, 128, b); sb("pr%d" % k, 128, f)
-        sb("aI%d" % k, 128, i); sb("aJ%d" % k, 128, i); sb("rm%d" % k, 128, b); sb("st%d" % k, 128, h)
-        sb("ML%d" % k, 128, h); sb("hs%d" % k, 128, b); sb("ls%d" % k, 128, b)
-        sb("rn%d" % k, 128, b)
-        for p in range(2):
-            sb("L%d%d" % (p, k), 128, f)
+        sb("al%d" % k, 128, u); sb("nb%d" % k, 128, h); sb("pr%d" % k, 128, i); sb("aj%d" % k, 128, i); sb("pf%d" % k, 128, f)
+        sb("st%d" % k, 128, h); sb("ML%d" % k, 128, h); sb("hs%d" % k, 128, b); sb("ls%d" % k, 128, b)
+        sb("rn%d" % k, 128, i); sb("of%d" % k, 8, u); sb("zm%d" % k, 128, f)
     for t in range(4):
-        sb("MSG%d" % t, 32, u); sb("zo%d" % t, 256, b); sb("zr%d" % t, 256, b); sb("HM%d" % t, 32, u)
-        sb("it%d" % t, 256, f); sb("N%d" % t, 256, f); sb("Hi%d" % t, 256, b)
-        if t:
-            sb("LR%d" % t, 32, u)
-        if t < 3:
-            sb("rb%d" % t, 16, i)
-    sb("Lo", 256, b); sb("e0", 256, b); sb("il", 256, f)
-    sb("zf", 256, b); sb("rM", 128, f)
-    for n in ("uI", "uJ", "uK"):
-        sb(n, 16, i)
-    sb("UL", 16, u); sb("old", 256, b)
-    for n, w in (("OB", 1024), ("PC", 1280), ("OA", 1536), ("SP", 1792)):
-        sb(n, w, f)
-    for n in ("oS", "pS", "rOB", "rPC", "rOA"):
-        sb(n, 1024, h)
-    for n in ("vpI", "voI"):
-        sb(n, 1024, i)
-    sb("mvI", 16, i); sb("mvu", 16, u); sb("wI", 1, i); sb("zn", 256, b); sb("zs", 256, b)
-    sb("L0n", 256, f)
-    for n in ("L0h", "L0A", "L0C", "L1A", "L2H", "L3h", "L3r"):
+        sb("L%d" % t, 256, h); sb("zo%d" % t, 256, b); sb("zr%d" % t, 256, b); sb("d%d" % t, 16, b)
+        for k in range(2):
+            sb("mo%d%d" % (t, k), 8, u); sb("mr%d%d" % (t, k), 8, u)
+    sb("dk", 64, b); sb("zf", 256, b); sb("zs", 256, b); sb("sg", 16, b)
+    for n in ("L0h", "L1r", "L2r", "L3r"):
         sb(n, 256, h)
-    for n in ("ip", "p16", "pg", "i1", "i2", "i3", "i4", "i5", "i6", "i7", "cAi", "cAj"):
+    for n in ("uI", "uJ", "uK", "rb", "mvI"):
+        sb(n, 16, i)
+    sb("UL", 16, u); sb("mvu", 16, u); sb("old", 256, b)
+    for n, w, d in (("vpI", 1024, i), ("OS", 1024, i), ("OB", 1024, i), ("OA", 1536, i), ("PS", 1792, f), ("PC", 1280, f),
+                    ("pH", 1024, h), ("N", 1024, h), ("EX", 2048, b), ("s0", 2048, b), ("s1", 2048, b), ("ykn", 1024, f)):
+        sb(n, w, d)
+    for n in ("ip", "p16", "pg", "wI"):
         sb(n, 1, i)
-    for n in ("pf", "p16f", "pgf", "pg16", "p1", "p2", "k15", "k14", "m0", "m1", "wf", "ck", "cA", "cR", "f1", "f2", "f3",
-              "f4", "f5", "f6", "g1", "g2", "g3", "g4", "g5", "g6", "x128"):
+    for n in ("pf", "p16f", "pgf", "pg16", "wf", "ck32", "ckA", "cA", "cC", "acc", "x16", "x32", "low", "kk"):
         sb(n, 1, f)
-    sb("fr", 144, f); sb("fy", 64, f); sb("Dn", 144, b); sb("Dw", 144, b); sb("D16", 144, b)
-    for n in ("I1", "I2", "I4", "I4k", "bda", "bdb", "BD", "WB", "I2e", "cr", "cu", "c32", "ones", "nones"):
+    sb("n16", 1, h)
+    sb("fr", 144, f); sb("Dn", 144, b); sb("Dw", 144, b); sb("D16", 144, b)
+    for n in ("I1", "I2", "I2e", "I4", "I4k", "I2k", "I256", "KM", "bda", "bdb", "BD", "WB", "Cm", "ones", "qc", "Sh1", "Sh2", "Se0", "Se1"):
         sb(n, 128, b)
-    sb("ik", 128, f); sb("ck16", 128, f)
-    for n in ("Sh1", "Sh2"):
-        sb(n, 128, b)
-    sb("EX", 2048, b); sb("ind", 16, f); sb("s0", 2048, b); sb("s1", 2048, b)
-    sb("q1", 128, f); sb("Bq", 128, f); sb("Br", 128, f); sb("Bc", 128, f); sb("iy", 128, f); sb("i8", 8, f); sb("k16", 8, f)
-    sb("jp", 96, f)
-    sb("pl", 16, u); sb("yc", 64, i); sb("yq", 64, i); sb("ye", 64, i); sb("yb", 64, i); sb("yd", 64, i); sb("yl", 64, u)
-    sb("hk", 128, f); sb("kall", 64, b)
-    sb("ykr", 768, f); sb("ykr3", 256, f); sb("ykn", 1024, f); sb("ypb", 256, f); sb("yob", 256, f)
+    sb("nones", 128, f); sb("ind", 16, f); sb("il", 256, f); sb("iy", 128, f); sb("Xc", 128, h); sb("ir", 16, f)
+    sb("ypb", 256, f); sb("yob", 256, f)
     return s
 
 
@@ -77,7 +59,7 @@ def _pack():
     out, width = {}, {}
     size = {"float32": 4, "int32": 4, "bfloat16": 2, "uint16": 2, "float16": 2}
     for name, (w, sh, d) in _ALL.items():
-        if sh[1] <= 256:
+        if len(sh) == 2 and sh[1] <= 256:
             al = 32 // size[d]
             o = width.get(d, 0)
             _PACK[name] = ("pk_" + d, o, sh[1])
@@ -92,14 +74,41 @@ def _pack():
 
 
 SCRATCH = _pack()
-_ARR = ["aL0", "az0", "aOB", "aPC", "aL0C", "aOA", "aL3"] + ["al%d%d" % (t, h) for t in (1, 2, 3) for h in (0, 1)] \
-    + ["az%d%d" % (t, h) for t in (1, 2, 3, 4) for h in (0, 1)] + ["ah0", "ah1", "ah2", "ah30", "ah31", "aho"]
-SEMAPHORES = ["sV", "sT", "sS", "sG", "ls"] + ["d%d" % k for k in range(20)] + _ARR
+_ARR = ["aL0", "az0", "aOB", "aPC", "aOA", "aL1", "aL2", "aL3", "ahand"] + ["am%d%d" % (t, h) for t in range(4) for h in (0, 1)] \
+    + ["az%d%d" % (t, h) for t in (1, 2, 3, 4) for h in (0, 1)] + ["ad%d" % t for t in range(4)]
+SEMAPHORES = ["sV", "sT", "sS", "sG", "ls"] + ["d%d" % k for k in range(24)] + _ARR
+
+HANDED = (("PC", 1280, "aPC", 3), ("OA", 1024, "aOA", 1))
+
+
+def helpers(T, topo, r):
+    c = T.cores[r]
+    out = []
+    for _, _, _, d in HANDED:
+        to = T.cores[(r + d) % 4]
+        out.append([k for k in topo.cores_of(c) if topo.die(k) != topo.die(c) and topo.may_write(k, to) and k not in out][0])
+    return out
+
+
+def hand_on(g, core, T, topo):
+    for r in range(4):
+        for k, (buf, n, sem, d) in zip(helpers(T, topo, r), HANDED):
+            if k == core:
+                to = T.cores[(r + d) % 4]
+                rid, pid = topo.addr(to)[:2]
+                g.wait_ge(T.sem.ahand, len(inner(topo, T.cores[r], k, to)))
+                g.remote_dma(T[buf][:, 0:n], T[buf][:, 0:n], T.sem[sem], T.sem.ls, pid, rid, topo.mask(core, to))
+                g.wait_ge(T.sem.ls, len(topo.engines(core, to)))
+
+
+def inner(topo, c, k, far):
+    return [e for e in topo.engines(c, k) if e not in topo.engines(c, far)]
 
 
 def rank_program(g, core, T, topo):
     q = T.rank_of(core)
     if q is None:
+        hand_on(g, core, T, topo)
         return
     ENG = {"V": g.vector, "T": g.tensor, "S": g.scalar, "G": g, "Y": g.sync}
     QSEM = {"V": "sV", "T": "sT", "S": "sS", "G": "sG"}
@@ -120,6 +129,10 @@ def rank_program(g, core, T, topo):
         if step is None:
             return t[r, o + a:o + b]
         return t[r, o + a:o + b:step]
+
+    def back(name):
+        buf, o, w = _PACK.get(name, (name, 0, None))
+        return T[buf][:, o + 127:(o - 1 if o else None):-1]
 
     def wait(qn, tok):
         sem, val, snap, _ = tok
@@ -154,21 +167,7 @@ def rank_program(g, core, T, topo):
             last[k] = tok
             readers[k] = {}
 
-    prog, cur = [], [0.0]
-
-    def at(stage):
-        cur[0] = float(stage)
-
-    def op(*a):
-        prog.append((cur[0], len(prog), op_now, a))
-
-    def dma(*a):
-        prog.append((cur[0], len(prog), dma_now, a))
-
-    def send(*a):
-        prog.append((cur[0], len(prog), send_now, a))
-
-    def op_now(qn, calls, R, W):
+    def op(qn, calls, R, W):
         before(qn, R, W)
         calls = calls if isinstance(calls, list) else [calls]
         for c in calls:
@@ -178,7 +177,7 @@ def rank_program(g, core, T, topo):
         used[QSEM[qn]] = cnt[qn]
         after(qn, (QSEM[qn], cnt[qn], dict(clock[qn]), qn), R, W)
 
-    def dma_now(qn, out, in_, R, W):
+    def dma(qn, out, in_, R, W):
         before(qn, R, W)
         sem = "d%d" % dn[0]
         dn[0] += 1
@@ -186,13 +185,15 @@ def rank_program(g, core, T, topo):
         used[sem] = 16
         after("D" + sem, (sem, 16, dict(clock[qn]), "D" + sem), R, W)
 
-    def send_now(dst, out, in_, sem, R):
+    def write(c, eng, out, in_, sem, R):
         before("G", R, [])
-        c = T.cores[dst % 4]
         rid, pid = topo.addr(c)[:2]
-        m = topo.mask(core, c)
-        g.remote_dma(out, in_, T.sem[sem], T.sem.ls, pid, rid, m)
-        used["ls"] = used.get("ls", 0) + len(topo.engines(core, c))
+        g.remote_dma(out, in_, T.sem[sem], T.sem.ls, pid, rid, sum(1 << e for e in eng))
+        used["ls"] = used.get("ls", 0) + len(eng)
+
+    def send(dst, out, in_, sem, R):
+        c = T.cores[dst % 4]
+        write(c, topo.engines(core, c), out, in_, sem, R)
 
     def arrives(src, sem, key):
         n = len(topo.engines(T.cores[src % 4], core))
@@ -219,606 +220,392 @@ def rank_program(g, core, T, topo):
     def mm(out, l, r, st=True, sp=True):
         return lambda: PE.matmul(out, l, r, st, sp)
 
-    def vts(o, i, s1, s2, o0, o1=None, R=()):
+    def vts(o, i, s1, s2, o0, o1=None):
         rd = [i] + [s for s in (s1, s2) if isinstance(s, str)]
         f = lambda s: X(s) if isinstance(s, str) else s
         op("V", ts(X(o), X(i), f(s1), f(s2), o0, o1), rd, [o])
 
-    at(-10)
-    dma("Y", X("mvI"), T.mv[:, :], [], ["mvI"])
-    dma("Y", X("vpI"), T.vp[:, :], [], ["vpI"])
-    dma("S", X("zn"), T.z0[:, :], [], ["zn"])
-    dma("S", X("wI"), T.wt[:, :], [], ["wI"])
-    dma("Y", X("R", 0, 4096), T.strat[:, 0:4096], [], ["Ra"])
-    dma("S", X("R", 4096, 8192), T.strat[:, 4096:8192], [], ["R"])
-    dma("Y", X("voI"), T.vo[:, :], [], ["voI"])
-    at(-9)
+    def fill(name, v, a=None, b=None, step=None, rows=None, over=False):
+        op("V", lambda: V.memset(X(name, a, b, step, rows), v), [name] if over else [], [name])
 
-    def iota(name, pattern, base=0, cm=0, a=None, b=None, integer=False, key=None, early=None):
-        o = X(name, a, b)
-        at0 = cur[0]
-        at(at0 if early is None else early)
+    def iota(name, pattern, base=0, cm=0, integer=False):
         if integer:
-            op("G", lambda: G.iota(o, pattern, base, cm), [], [key or name])
+            op("G", lambda: G.iota(X(name), pattern, base, cm), [], [name])
         else:
-            op("G", lambda: G.iota(o, pattern, base, cm, allow_small_or_imprecise_dtypes=True), [], [key or name])
-        at(at0)
+            op("G", lambda: G.iota(X(name), pattern, base, cm, allow_small_or_imprecise_dtypes=True), [], [name])
 
-    iota("ip", [[0, 1]], 0, 1, integer=True)
-    iota("jp", [[128, 2], [1, 4], [64, 2]], a=0, b=16, key="jp0")
-    vts("p16", "ip", 15, None, A.bitwise_and)
-    vts("g1", "p16", 4.0, None, A.mult)
-    op("V", cp(X("mvu"), X("mvI")), ["mvI"], ["mvu"])
-    op("V", ts(X("pl"), X("jp", 0, 16), X("g1"), None, A.add), ["jp0", "g1"], ["pl"])
-    op("V", cp(X("L0n"), X("vpI").indirect(X("mvu"))), ["vpI", "mvu"], ["L0n"])
-    op("V", cp(X("L0h"), X("L0n").indirect(X("pl"))), ["L0n", "pl"], ["L0h"])
-    op("S", act(X("zs"), X("zn").indirect(X("pl"))), ["zn", "pl"], ["zs"])
-    send(q + 1, X("zr0"), X("zs"), "az0", ["zs"])
-    send(q + 1, X("L0A"), X("L0h"), "aL0", ["L0h"])
-    arrives(q - 1, "az0", "zr0"); arrives(q - 1, "aL0", "L0A")
-
-    iota("fr", [[1, 144]], -16, early=-9.5)
-    vts("pg", "ip", 112, None, A.bitwise_and)
-    op("V", cp(X("pf"), X("ip")), ["ip"], ["pf"])
-    op("V", cp(X("p16f"), X("p16")), ["p16"], ["p16f"])
-    op("V", cp(X("pgf"), X("pg")), ["pg"], ["pgf"])
-    op("V", cp(X("wf"), X("wI")), ["wI"], ["wf"])
-    op("V", ts(X("I1"), X("fr", 16, 144), X("pf"), None, A.is_equal), ["fr", "pf"], ["I1"])
-    vts("pg16", "pgf", 16.0, None, A.add)
-    vts("m0", "p16f", 0.0, None, A.is_equal)
-    vts("ck", "p16f", 1184.0, None, A.mult)
-    fr = X("fr", 16, 144)
-    op("V", ts(X("bda"), fr, X("pgf"), None, A.is_ge), ["fr", "pgf"], ["bda"])
-    op("V", ts(X("bdb"), fr, X("pg16"), None, A.is_lt), ["fr", "pg16"], ["bdb"])
-    op("V", tt(X("BD"), X("bda"), X("bdb"), A.mult), ["bda", "bdb"], ["BD"])
-    op("S", act(X("WB"), X("BD"), scale=X("wf")), ["BD", "wf"], ["WB"])
-    op("S", act(X("I4k"), X("I1"), scale=-4096.0), ["I1"], ["I4k"])
-    op("V", lambda: V.memset(X("cu", rows=slice(0, 64)), -32.0), [], ["cu"])
-    op("V", lambda: V.memset(X("cu", rows=slice(64, 128)), 2.0 ** -7), [], ["cu"])
-    for n, v in (("ones", 1.0), ("c32", 0.25)):
-        op("V", lambda n=n, v=v: V.memset(X(n), v), [], [n])
-    op("V", ts(X("D16"), X("fr"), X("pgf"), None, A.is_equal), ["fr", "pgf"], ["D16"])
-    op("S", act(X("Dw"), X("D16"), scale=X("wf")), ["D16", "wf"], ["Dw"])
-    op("S", act(X("Dn"), X("D16"), scale=-1.0), ["D16"], ["Dn"])
-    op("V", ts(X("ind"), X("fr", 16, 32), X("p16f"), None, A.is_equal), ["fr", "p16f"], ["ind"])
-    for x in range(16):
-        op("S", act(X("EX", 128 * x, 128 * x + 128), X("BD"), scale=X("ind", x, x + 1)), ["BD", "ind"], ["EX%d" % x])
-    at(-7.5)
-    op("V", cp(X("pS"), X("vpI")), ["vpI"], ["pS"])
-    at(2)
-    send(q + 3, X("rPC"), X("pS"), "aPC", ["pS"])
-    send(q + 3, X("L0C"), X("L0h"), "aL0C", ["L0h"])
-    arrives(q - 2, "aOB", "rOB"); arrives(q + 1, "aPC", "rPC"); arrives(q + 1, "aL0C", "L0C"); arrives(q - 1, "aOA", "rOA")
-
-    at(-7)
-    op("V", lambda: V.memset(X("s0"), 1.0), [], ["s0"])
-    op("V", lambda: V.memset(X("s0", 0, 2048, 16), 0.0), ["s0"], ["s0"])
-    at(2)
-    op("S", act(X("s1"), X("s0"), IDN, bias=256.0, scale=-256.0), ["s0"], ["s1"])
-    at(-7)
-    op("V", lambda: V.memset(X("q1"), -10.0), [], ["q1"])
-    op("V", lambda: V.memset(X("q1", 15, 128, 16), -9.0), ["q1"], ["q1"])
-    iota("iy", [[16, 8], [0, 16]], early=-9.5)
-    iota("i8", [[16, 8]], early=-9.5)
-    vts("x128", "p16f", 128.0, None, A.mult)
-    vts("Bq", "iy", "x128", 150.0, A.add, A.add)
-    op("V", ts(X("Br"), X("s0", 0, 128), -30000.0, None, A.mult), ["s0"], ["Br"])
-    op("V", tt(X("Bc"), X("Bq"), X("Br"), A.add), ["Bq", "Br"], ["Bc"])
-    at(1)
-    vts("k16", "i8", "x128", None, A.add)
-    for n, v in (("cr", -3 * 2.0 ** -10), ("nones", -1.0)):
-        op("V", lambda n=n, v=v: V.memset(X(n), v), [], [n])
-    iota("ik", [[16, 128]], early=-9.5)
-    op("S", act(X("ck16"), X("ik"), IDN, bias=X("p16f")), ["ik", "p16f"], ["ck16"])
-    at(-7)
-    op("S", act(X("I2"), X("I1"), scale=0.5), ["I1"], ["I2"])
-    op("S", act(X("I2e"), X("I1"), scale=0.5 - 2.0 ** -9), ["I1"], ["I2e"])
-    op("S", act(X("I4"), X("I1"), scale=0.25), ["I1"], ["I4"])
-    pats = [[[128, 2], [1, 32], [32, 4]], [[128, 2], [1, 2], [2, 64]], [[128, 2], [1, 16], [16, 8]], [[1, 256]]]
-    for t in range(4):
-        at(1)
-        iota("it%d" % t, pats[t], 1024 + 256 * t)
-
-    at(1)
-    vts("i1", "p16", 3, None, A.bitwise_and)
-    vts("i2", "p16", 2, None, A.arith_shift_right)
-    vts("i3", "p16", 7, None, A.bitwise_and)
-    vts("i4", "p16", 3, None, A.arith_shift_right)
-    op("V", cp(X("f2"), X("i2")), ["i2"], ["f2"])
-    op("V", cp(X("f4"), X("i4")), ["i4"], ["f4"])
-    vts("f1", "i1", 32.0, "f2", A.mult, A.add)
-    vts("f3", "i3", 16.0, "f4", A.mult, A.add)
-    vts("g2", "p16f", 2.0, None, A.mult)
-    iota("jp", [[128, 2], [4, 8]], a=16, b=32, key="jp1")
-    iota("jp", [[128, 2], [1, 2], [32, 4]], a=32, b=48, key="jp2")
-    iota("jp", [[128, 2], [2, 8]], a=48, b=64, key="jp3")
-    for t, (k, c) in enumerate(((1, "f1"), (2, "g2"), (3, "f3"))):
-        op("V", ts(X("rb%d" % t), X("jp", 16 * k, 16 * k + 16), X(c), 32.0, A.add, A.mult), ["jp%d" % k, c], ["rb%d" % t])
-
-    def late_constants():
-        for n, d in (("Sh1", 1), ("Sh2", 2)):
-            op("G", lambda n=n, d=d: G.affine_select(X(n), X("BD"), [[1, 128]], A.is_equal, 0.0, -d, -1), ["BD"], [n])
-        iota("il", [[1, 256]])
-
-    def number_n(k):
-        op("S", act(X("N%d" % k), X("it%d" % k), scale=X("m0")), ["it%d" % k, "m0"], ["N%d" % k])
-
-    def number_lo():
-        op("S", act(X("Lo"), X("il"), scale=X("m0")), ["il", "m0"], ["Lo"])
-        op("S", act(X("e0"), X("il"), IDN, scale=0.0, bias=X("m0")), ["il", "m0"], ["e0"])
-
-    def number_hi(k):
-        op("S", act(X("Hi%d" % k), X("e0"), scale=1024.0 + 256 * k), ["e0"], ["Hi%d" % k])
-
-    for k, pat in enumerate(([[0, 2], [4, 8]], [[0, 2], [1, 4], [64, 2]], [[0, 2], [8, 8]], [[0, 2], [1, 8]])):
-        iota("fy", pat, a=16 * k, b=16 * k + 16, key="fy%d" % k, early=2.5)
-    iota("yb", [[16, 4], [8, 2], [0, 8]], integer=True, early=2.5)
-
-    def verdicts_home(k):
-        op("V", cp(X("hk", 32 * k, 32 * k + 32), X("HM%d" % k)), ["HM%d" % k], ["hk%d" % k])
-        for h in range(2):
-            c = 32 * k + 16 * h + 8
-            op("V", tt(X("kall", 16 * k + 8 * h, 16 * k + 8 * h + 8), X("hk", c, c + 8), X("k16"), A.subtract),
-               ["hk%d" % k, "k16"], ["kall"])
-
-    def list_constants(part):
-        if part == 0:
-            vts("i5", "p16", 1, None, A.bitwise_and)
-            vts("i6", "p16", 1, None, A.arith_shift_right)
-            op("V", cp(X("f6"), X("i6")), ["i6"], ["f6"])
-            vts("f5", "i5", 64.0, "f6", A.mult, A.add)
-            vts("g3", "p16f", 8.0, None, A.mult)
-            return
-        for t, c in enumerate(("f1", "g1", "f5", "g3")):
-            op("V", ts(X("yc", 16 * t, 16 * t + 16), X("fy", 16 * t, 16 * t + 16), X(c), None, A.add), ["fy%d" % t, c], ["yc"])
-        vts("yq", "yc", 3, None, A.arith_shift_right)
-        op("V", ts(X("ye", 0, 48), X("yq", 0, 48), 40.0, None, A.mult), ["yq"], ["ye"])
-        op("V", ts(X("ye", 48, 64), X("yq", 48, 64), 8.0, None, A.mult), ["yq"], ["ye"])
-        op("V", tt(X("yd"), X("ye"), X("yc"), A.add), ["ye", "yc"], ["yd"])
-        op("V", tt(X("yq"), X("yd"), X("yb"), A.add), ["yd", "yb"], ["yq"])
-        op("V", cp(X("yl", 0, 48), X("yq", 0, 48)), ["yq"], ["yl"])
-        op("V", ts(X("yl", 48, 64), X("yq", 48, 64), -48.0, None, A.add), ["yq"], ["yl"])
+    def scaled(o, i, s):
+        op("S", act(X(o), X(i), scale=X(s) if isinstance(s, str) else s), [i] + ([s] if isinstance(s, str) else []), [o])
 
     def half(h):
         return 128 * h, 128 * h + 128
 
-    def zkey(t, h):
-        return "zr0" if t == 0 else "zr%d%d" % (t, h)
-
-    for t in (1, 2, 3):
-        src = q - 1 if t < 3 else q + 2
-        for h in range(2):
-            arrives(src, "al%d%d" % (t, h), "LR%d%d" % (t, h))
-            arrives(src, "az%d%d" % (t, h), "zr%d%d" % (t, h))
+    arrives(q - 1, "az0", "zr00"); arrives(q - 1, "az0", "zr01"); arrives(q - 1, "aL0", "L00"); arrives(q - 1, "aL0", "L01")
+    arrives(q - 2, "aOB", "OB"); arrives(q + 1, "aPC", "PC"); arrives(q - 1, "aOA", "OA")
+    arrives(q + 1, "aL1", "L1r"); arrives(q - 1, "aL2", "L2r"); arrives(q + 1, "aL3", "L3r")
+    for h in range(2):
+        for t in (1, 2, 3):
+            arrives(q - 1 if t < 3 else q + 2, "am%d%d" % (t - 1, h), "mr%d%d" % (t - 1, h))
+            arrives(q - 1 if t < 3 else q + 2, "az%d%d" % (t, h), "zr%d%d" % (t, h))
+        arrives(q + 1, "am3%d" % h, "mr3%d" % h)
+        arrives(q + 1, "az4%d" % h, "zf%d" % h)
     for t in range(4):
-        src = q + 1 + t % 3
-        if t < 3:
-            arrives(src, "ah%d" % t, "HM%d" % t)
-        else:
-            for h in range(2):
-                arrives(src, "ah3%d" % h, "HM3%d" % h)
-                arrives(src, "az4%d" % h, "zf%d" % h)
-            arrives(src, "aL3", "L3r")
-            arrives(src, "aho", "HM3o")
+        arrives(q + 1 + t % 3, "ad%d" % t, "dk%d" % t)
 
-    def Lk(t, h):
-        return "L%d%d" % (t % 2, h)
+    dma("Y", X("mvI"), T.mv[:, :], [], ["mvI"])
+    dma("Y", X("vpI"), T.vp[:, :], [], ["vpI"])
+    dma("S", X("zs"), T.z0[:, :], [], ["zs"])
+    dma("S", X("wI"), T.wt[:, :], [], ["wI"])
+    dma("Y", X("R", 0, 4096), T.strat[:, 0:4096], [], ["Ra"])
+    dma("S", X("R", 4096, 8192), T.strat[:, 4096:8192], [], ["R"])
+    dma("Y", X("OS", rows=slice(1, 128)), T.vo[0:127, :], [], ["OS"])
+    dma("Y", X("OS", rows=slice(0, 1)), T.vo[0:1, :], [], ["OSa"])
+    dma("Y", X("R", 8192, 9216), T.strat[:, 0:1024], [], ["Rd"])
 
-    def pre_L(t, h):
+    iota("ip", [[0, 1]], 0, 1, integer=True)
+    iota("fr", [[1, 144]], -16)
+    iota("il", [[1, 256]], 1024)
+    iota("iy", [[256, 8], [1, 16]])
+    iota("ir", [[512, 16]])
+    send(q + 1, X("zr0"), X("zs"), "az0", ["zs"])
+    fill("s0", 1.0); fill("s1", 0.0)
+    vts("p16", "ip", 15, None, A.bitwise_and)
+    vts("pg", "ip", 112, None, A.bitwise_and)
+    op("V", cp(X("pf"), X("ip")), ["ip"], ["pf"])
+    op("V", cp(X("p16f"), X("p16")), ["p16"], ["p16f"])
+    op("V", cp(X("pgf"), X("pg")), ["pg"], ["pgf"])
+    fill("s0", 0.0, 0, 2048, 16, over=True); fill("s1", 256.0, 0, 2048, 16, over=True)
+    op("V", cp(X("mvu"), X("mvI")), ["mvI"], ["mvu"])
+    fr = X("fr", 16, 144)
+    op("V", ts(X("I1"), fr, X("pf"), None, A.is_equal), ["fr", "pf"], ["I1"])
+    vts("pg16", "pgf", 16.0, None, A.add)
+    op("V", ts(X("bda"), fr, X("pgf"), None, A.is_ge), ["fr", "pgf"], ["bda"])
+    op("V", ts(X("bdb"), fr, X("pg16"), None, A.is_lt), ["fr", "pg16"], ["bdb"])
+    op("V", ts(X("D16"), X("fr"), X("pgf"), None, A.is_equal), ["fr", "pgf"], ["D16"])
+    op("V", ts(X("ind"), X("fr", 16, 32), X("p16f"), STEP, A.is_equal, A.mult), ["fr", "p16f"], ["ind"])
+    op("V", tt(X("BD"), X("bda"), X("bdb"), A.mult), ["bda", "bdb"], ["BD"])
+    op("V", cp(X("wf"), X("wI")), ["wI"], ["wf"])
+    fill("ones", 1.0)
+    for k, v in enumerate((2.0 ** 17, 128.0, 1.0, 0.0)):
+        fill("Cm", v, rows=slice(32 * k, 32 * k + 32))
+    vts("ck32", "p16f", 37.0 * 32, None, A.mult)
+    scaled("WB", "BD", "wf"); scaled("I4k", "I1", -4096.0)
+    op("V", cp(X("L0h", 0, 128), X("vpI").indirect(X("mvu", 0, 8))), ["vpI", "mvu"], ["L0h0"])
+    op("S", act(X("L0h", 128, 256), X("vpI").indirect(X("mvu", 8, 16))), ["vpI", "mvu"], ["L0h1"])
+    send(q + 1, X("L0"), X("L0h"), "aL0", ["L0h0", "L0h1"])
+
+    op("V", cp(X("pH"), X("vpI")), ["vpI"], ["pH"])
+    for n, d in (("Sh1", 1), ("Sh2", 2)):
+        op("G", lambda n=n, d=d: G.affine_select(X(n), X("BD"), [[1, 128]], A.is_equal, 0.0, -d, -1), ["BD"], [n])
+    scaled("Dn", "D16", -BIG); scaled("Dw", "D16", "wf")
+    for x in range(16):
+        op("S", act(X("EX", 128 * x, 128 * x + 128), X("BD"), scale=X("ind", x, x + 1)), ["BD", "ind"], ["EX"])
+    fill("qc", 9.5 * BIG); fill("qc", -16 * BIG, 15, 128, 16, over=True)
+    fill("nones", -1.0)
+    vts("x16", "p16f", 16.0, None, A.mult)
+    vts("x32", "p16f", 32.0, None, A.mult)
+    vts("kk", "p16f", -STEP, 15 * STEP, A.mult, A.add)
+    vts("ckA", "p16f", 37.0, 256.0 * 1025, A.mult, A.add)
+    vts("low", "p16f", 0.0, -4096.0, A.is_gt, A.mult)
+    vts("Xc", "iy", "x16", None, A.add)
+    vts("rb", "ir", "x32", None, A.add)
+    for t in range(4):
+        op("V", ts(X("N", 256 * t, 256 * t + 256), X("il"), X("low"), 256.0 * t, A.add, A.add), ["il", "low"], ["N"])
+    for n, s in (("I2", 0.5), ("I2e", 0.5 - 2.0 ** -9), ("I4", 0.25), ("I2k", -STEP), ("KM", "kk")):
+        scaled(n, "I1", s)
+    for n, d in (("Se0", "I1"), ("Se1", "Sh1")):
+        op("V", ts(X(n), X(d), X("ind", 0, 1), 1.0 / STEP, A.mult, A.mult), [d, "ind"], [n])
+
+    def table_own():
+        for k in range(2):
+            a, p = 512 * k, "P%d" % (4 + k)
+            op("T", mm(X(p), X("Sh1"), X("pH", a, a + 512)), ["Sh1", "pH"], [p])
+            op("S", act(X("PS", a, a + 512), X(p)), [p], ["PS"])
+
+    def grow_pe(Lb, keys, resumed, t):
+        cs, n = [], 0
+        if resumed:
+            cs, n = [mm(X("P7", 0, 256), X("Sh1"), X(Lb))], 256
+        o = X("P7", n, n + 256)
+        cs += [mm(o, X("Se1"), X("N", 256 * t, 256 * t + 256), True, False), mm(o, X("Sh2"), X(Lb), False, True)]
+        op("T", cs, ["Sh1", "Sh2", "Se1", "N"] + keys, ["P7"])
+
+    def grow(w, at, n):
+        op("S", act(X(w, at, at + n), X("P7", 0, n)), ["P7"], [w + "x"])
+
+    def hand(k, src, keys):
+        buf, n, _, d = HANDED[k]
+        c = helpers(T, topo, q)[k]
+        write(c, inner(topo, core, c, T.cores[(q + d) % 4]), X(buf, 0, n), X(src, 0, n), "ahand", keys)
+
+    table_own()
+    grow_pe("L0h", ["L0h0", "L0h1"], False, 0)
+    grow("PS", 1024, 256)
+
+    def lookup(t, h):
         a, b = half(h)
-        k = Lk(t, h)
-        if t == 0:
-            op("V", cp(X(k), X("L0A", a, b)), ["L0A"], [k])
-        else:
-            w = ("OB", "PC", "OA")[t - 1]
-            op("V", tt(X(k), X(w).indirect(X("LR%d" % t, 16 * h, 16 * h + 8)), X("N%d" % (t - 1), a, b), A.add),
-               [w, "LR%d%d" % (t, h), "N%d" % (t - 1)], [k])
+        w = ("OB", "PC", "OA")[t - 1]
+        op("V", tt(X("L%d" % t, a, b), X(w).indirect(X("mr%d%d" % (t - 1, h))), X("N", 256 * (t - 1) + a, 256 * (t - 1) + b), A.max),
+           [w, w + "x", "mr%d%d" % (t - 1, h), "N"], ["L%d%d" % (t, h)])
 
-    def pre_n(t, h):
+    def sums(t, h):
         a, b = half(h)
-        z, zk, pu = X("zr%d" % t, a, b), zkey(t, h), "P%d" % (2 + h)
-        o = X(pu, 0, 128)
-        op("T", [mm(o, X("cu"), X("ones"), True, False)], ["cu", "ones"], [pu])
-        op("T", [mm(o, X("WB"), z, False, True)], ["WB", zk], [pu])
-        op("S", act(X("nM%d" % h), o, IDN, bias=MAGIC, scale=2.0 ** -12), [pu], ["nM%d" % h])
-        op("S", act(X("nb%d" % h), X("nM%d" % h), IDN, bias=-MAGIC), ["nM%d" % h], ["nb%d" % h])
-
-    def pre_u(t, h):
-        a, b = half(h)
-        z, zk, pu = X("zr%d" % t, a, b), zkey(t, h), "P%d" % (2 + h)
-        o = X(pu, 128, 256)
-        op("T", [mm(o, X("c32"), X("ones"), True, False), mm(o, X("WB"), z, False, False)], ["c32", "ones", "WB", zk], [pu])
+        zk, pu = "zr%d%d" % (t, h), "P%d" % (2 + h)
+        o, pn, z = X(pu, 0, 128), "P%d" % h, X("zr%d" % t, a, b)
+        op("T", [mm(o, X("Cm"), X("ones"), True, False)], ["Cm", "ones"], [pu])
+        op("T", [mm(X(pn, 128, 256), X("WB"), z)], ["WB", zk], [pn])
+        op("T", [mm(o, X("WB"), z, False, False)], ["WB", zk], [pu])
+        op("S", act(X("nb%d" % h), X(pn, 128, 256), IDN, bias=1025 - 2047.5 / 4096, scale=2.0 ** -12), [pn], ["nb%d" % h])
         op("T", [mm(o, X("I4k"), X("nb%d" % h), False, True)], ["I4k", "nb%d" % h], [pu])
 
-    def pre_z(t, h):
+    def z4(t, h):
         a, b = half(h)
-        op("T", [mm(X("P%d" % h, d, 512, 4), X("I1"), X("zr%d" % t, a, b)) for d in range(4)], ["I1", zkey(t, h)], ["P%d" % h])
+        op("T", [mm(X("P%d" % h, d, 512, 4), X("I1"), X("zr%d" % t, a, b)) for d in range(4)], ["I1", "zr%d%d" % (t, h)], ["P%d" % h])
 
-    def slist(t, h):
+    def product(t, h):
         a, b = half(h)
-        if t < 3:
-            op("T", [mm(X("P6", 256 + 8 * h, 264 + 8 * h), X("Dw", 16 - x, 144 - x), X("zr%d" % t, a + 8 * x, a + 8 * x + 8),
-                        x == 0, x == 15) for x in range(16)], ["Dw", zkey(t, h)], ["P6"])
+        pu, o = "P%d" % (2 + h), ("pr%d" if t else "pf%d") % h
+        op("V", tt(X(o), X(pu, 0, 128), X("L%d" % t, a, b), A.mult), [pu, "L%d%d" % (t, h)], [o])
+        if t == 0:
+            vts("pr%d" % h, o, "ck32", None, A.add)
+        vts("aj%d" % h, "pr%d" % h, 5, 8191, A.arith_shift_right, A.bitwise_and)
 
-    def pre_a(t, h):
-        pu = "P%d" % (2 + h)
-        op("V", tt(X("pr%d" % h), X(pu, 128, 256), X(Lk(t, h)), A.mult), [pu, Lk(t, h)], ["pr%d" % h])
+    def address(t, h):
+        if t:
+            vts("al%d" % h, "aj%d" % h, "cA", None, A.add)
+        else:
+            op("V", cp(X("al%d" % h), X("aj%d" % h)), ["aj%d" % h], ["al%d" % h])
 
-    def pre_b(t, h):
-        k = "cA" if t else "ck"
-        op("V", ts(X("aI%d" % h), X("pr%d" % h), X(k), None, A.add), ["pr%d" % h, k], ["aI%d" % h])
-        op("V", ts(X("aJ%d" % h), X("aI%d" % h), 5, 8191, A.arith_shift_right, A.bitwise_and), ["aI%d" % h], ["aJ%d" % h])
-        op("V", cp(X("al%d" % h), X("aJ%d" % h)), ["aJ%d" % h], ["al%d" % h])
+    def ys(n, y0, y1):
+        return ["%s_%d" % (n, y) for y in range(y0, y1)]
 
-    def ulist(t):
-        op("V", cp(X("uI"), X("P6", 256, 272)), ["P6"], ["uI"])
-        vts("uJ", "uI", 31, None, A.bitwise_and)
-        op("V", tt(X("uK"), X("uJ"), X("rb%d" % t), A.add), ["uJ", "rb%d" % t], ["uK"])
-        op("V", cp(X("UL"), X("uK")), ["uK"], ["UL"])
+    def gather(t, e, y0, y1):
+        h = y0 // 8
+        w = X("R") if t else X("R", 0, 8192)
+        o, i = X("Y", 256 * y0, 256 * y1), w.indirect(X("al%d" % h, 16 * y0 - 128 * h, 16 * y1 - 128 * h))
+        op(e, cp(o, i) if e == "V" else act(o, i), ["R", "Ra", "al%d" % h] + (["Rd"] if t else []), ys("Y", y0, y1))
 
-    def gather(t, h, j):
-        a, b = SUB[h][j], SUB[h][j + 1]
-        o, i = X("Y%d" % h, 16 * a, 16 * b), X("R").indirect(X("al%d" % h, a, b))
-        v = h == 0 and j == 0
-        op("V" if v else "S", cp(o, i) if v else act(o, i), ["R", "Ra", "al%d" % h], ["Y%d_%d" % (h, j)])
+    def compare(y0, y1):
+        h = y0 // 8
+        op("V", [tt(T.B[:, y0:y1, d:256:4], X("Y", 256 * y0 + d, 256 * y1, 4), X("P%d" % h, 64 * (y0 - 8 * h), 64 * (y1 - 8 * h)), A.is_gt)
+                 for d in range(4)], ys("Y", y0, y1) + ["P%d" % h], ys("B", y0, y1))
 
-    def compare(t, h, j, ds=(0, 1, 2, 3)):
-        a, b = 16 * SUB[h][j], 16 * SUB[h][j + 1]
-        for d in ds:
-            op("V", tt(X("B%d" % h, a + d, b, 4), X("Y%d" % h, a + d, b, 4), X("P%d" % h, a // 4, b // 4), A.is_gt),
-               ["Y%d_%d" % (h, j), "P%d" % h], ["B%d_%d" % (h, j)])
-
-    def counts(t, h, j):
+    def counts0(h):
         pc = "P%d" % (4 + h)
-        op("T", [mm(X(pc, 0, 128), X("Dn", 16 - x, 144 - x), X("B%d" % h, 128 * x, 128 * x + 128), x == 0, x == 15)
-                 for x in range(SUB[h][j] // 8, SUB[h][j + 1] // 8)], ["Dn", "B%d_%d" % (h, j)], [pc])
+        op("T", mm(X(pc, 0, 128), X("I1"), X("qc"), True, False), ["I1", "qc"], [pc])
 
-    def scans(t, h):
-        scan_hi(t, h)
-        scan_lo(t, h)
+    def counts(y0, y1):
+        h = y0 // 8
+        pc = "P%d" % (4 + h)
+        op("T", [mm(X(pc, 16 * (y0 - 8 * h), 16 * (y1 - 8 * h)), X("Dn", 16 - x, 144 - x), T.B[:, y0:y1, 16 * x:16 * x + 16], False,
+                    x == 15 and y1 % 8 == 0) for x in range(16)], ["Dn"] + ys("B", y0, y1), [pc])
 
-    def scan_hi(t, h):
-        yk = ["Y%d_%d" % (h, j) for j in range(len(SUB[h]) - 1)]
-        op("V", lambda: V.tensor_tensor_scan(X("HI%d" % h), X("s0"), X("Y%d" % h), 0.0, A.mult, A.max), ["s0"] + yk, ["HI%d" % h])
+    def scan_hi(y0, y1):
+        a, b = 256 * y0, 256 * y1
+        op("V", lambda: V.tensor_tensor_scan(X("HI", a, b), X("s0", 0, b - a), X("Y", a, b), 0.0, A.mult, A.max), ["s0"] + ys("Y", y0, y1),
+           ys("HI", y0, y1))
 
-    def scan_lo(t, h):
-        yk = ["Y%d_%d" % (h, j) for j in range(len(SUB[h]) - 1)]
-        op("V", lambda: V.tensor_tensor_scan(X("LO%d" % h), X("s1"), X("Y%d" % h), 0.0, A.max, A.min), ["s1"] + yk, ["LO%d" % h])
-
-    def offs(t, h):
-        c = 16 * h + 8 if t < 3 else 16 + 8 * h
-        return X("MSG%d" % t, c, c + 8)
-
-    def lmov(t, h):
-        c = 16 * h if t < 3 else 8 * h
-        return X("MSG%d" % t, c, c + 8)
+    def scan_lo(y0, y1):
+        a, b = 256 * y0, 256 * y1
+        op("V", lambda: V.tensor_tensor_scan(X("LO", a, b), X("s1", 0, b - a), X("Y", a, b), 0.0, A.max, A.min), ["s1"] + ys("Y", y0, y1),
+           ys("LO", y0, y1))
 
     def verdict(t, h):
-        pc = "P%d" % (4 + h)
-        op("V", lambda: V.tensor_tensor_scan(X("rm%d" % h), X(pc, 0, 128), X("q1"), -9.0, A.min, A.max), [pc, "q1"], ["rm%d" % h])
-        op("V", lambda: V.tensor_tensor_scan(X("st%d" % h), X("Bc"), X("rm%d" % h), 0.0, A.max, A.add), ["Bc", "rm%d" % h],
-           ["st%d" % h])
-        op("V", cp(offs(t, h), X("st%d" % h, 14, 128, 16)), ["st%d" % h], ["of%d%d" % (t, h)])
+        pc, st = "P%d" % (4 + h), "st%d" % h
+        op("V", lambda: V.tensor_tensor_scan(back(st), back(pc), back("Xc"), 0.0, A.min, A.max), [pc, "Xc"], [st])
+        op("V", tt(X("d%d" % t, 8 * h, 8 * h + 8), X(st, 0, 128, 16), X("Xc", 15, 128, 16), A.subtract), [st, "Xc"], ["d%d%d" % (t, h)])
+        op("V", cp(X("of%d" % h), X(st, 0, 128, 16)), [st], ["of%d" % h])
 
-    def select(t, h, lo_on_v=False):
-        for s, w in (("hs%d" % h, "HI%d" % h), ("ls%d" % h, "LO%d" % h)):
-            i = X(w).indirect(offs(t, h))
-            if lo_on_v and s[0] == "l":
-                op("V", cp(X(s), i), [w, "of%d%d" % (t, h)], [s])
-            else:
-                op("S", act(X(s), i), [w, "of%d%d" % (t, h)], [s])
+    def select(e, w, h):
+        s = ("hs%d" if w == "HI" else "ls%d") % h
+        i = X(w, 2048 * h, 2048 * h + 2048).indirect(X("of%d" % h))
+        op(e, cp(X(s), i) if e == "V" else act(X(s), i), ys(w, 8 * h, 8 * h + 8) + ["of%d" % h], [s])
 
-    def newz_pe(t, h):
-        pu = "P%d" % (2 + h)
-        o = X(pu, 256, 384)
-        op("T", [mm(o, X("I2"), X("ls%d" % h), True, False)], ["I2", "ls%d" % h], [pu])
-        op("T", [mm(o, X("I2e"), X("hs%d" % h), False, True)], ["I2e", "hs%d" % h], [pu])
-
-    def rounded(h, out, in_, ki, ko):
-        if ko == "rn0":
-            m = "rM"
-            op("S", act(X(m), in_, IDN, bias=MAGIC), [ki], [m])
-            op("S", act(out, X(m), IDN, bias=-MAGIC), [m], [ko])
-        else:
-            op("V", ts(out, in_, MAGIC, MAGIC, A.add, A.subtract), [ki], [ko])
-
-    def newz(t, h):
+    def mean_pe(t, h, w):
         a, b = half(h)
-        pu = "P%d" % (2 + h)
-        o = X(pu, 256, 384)
-        rounded(h, X("zo%d" % t, a, b), o, pu, "zo%d%d" % (t, h))
-        if t < 3:
-            send(q + 1 if t < 2 else q + 2, X("zr%d" % (t + 1), a, b), X("zo%d" % t, a, b), "az%d%d" % (t + 1, h), ["zo%d%d" % (t, h)])
+        pz, pr = "P%d" % h, "P%d" % (2 + h)
+        s = ("hs%d" if w == "HI" else "ls%d") % h
+        if w == "HI":
+            op("T", [mm(X(pz, 0, 128), X("I2e"), X(s), True, False)], ["I2e", s], [pz])
+            if t < 3:
+                op("T", [mm(X(pr, 0, 128), X("I2"), X("old", a, b), True, False), mm(X(pr, 0, 128), X("I4"), X(s), False, False)],
+                   ["I2", "I4", "old", s], [pr])
         else:
-            send(q - 1, X("zf", a, b), X("zo3", a, b), "az4%d" % h, ["zo3%d" % h])
+            cs = [(mm(X(pz, 0, 128), X("I2"), X(s), False, True), pz)]
+            if t < 3:
+                cs.insert(h, (mm(X(pr, 0, 128), X("I4"), X(s), False, True), pr))
+                cs = cs[::-1] if h == 0 and False else cs
+            for c, p in (cs[::-1] if t < 3 else cs):
+                op("T", [c], ["I2", "I4", s], [p])
 
-    def moves_pe(t, h, a=0, b=16):
-        pc = "P%d" % (4 + h)
-        op("T", [mm(X(pc, 128 + 8 * x, 136 + 8 * x), X("EX", 128 * x, 128 * x + 128), X("st%d" % h, 14, 128, 16)) for x in range(a, b)],
-           ["EX%d" % x for x in range(a, b)] + ["st%d" % h], [pc])
-
-    def moves_v(t, h, a=0, b=16):
-        pc = "P%d" % (4 + h)
-        a, b = 8 * a, 8 * b
-        op("V", tt(X(pc, 256 + a, 256 + b), X(pc, 128 + a, 128 + b), X("ck16", a, b), A.is_equal), [pc, "ck16"], [pc])
-        op("V", tt(X("ML%d" % h, a, b), X(pc, 256 + a, 256 + b), X(Lk(t, h), a, b), A.mult), [pc, Lk(t, h)], ["ML%d_%d" % (h, a)])
-
-    def moves_f(t, h, a=0, b=16):
-        pc = "P%d" % (4 + h)
-        op("T", [mm(X(pc, 384, 392), X("D16", 16 - x, 144 - x), X("ML%d" % h, 8 * x, 8 * x + 8), x == 0, x == 15)
-                 for x in range(a, b)], ["D16", "ML%d_%d" % (h, 8 * a)], [pc])
-
-    def moves_a(t, h):
-        moves_v(t, h)
-        moves_f(t, h)
-
-    def moves_b(t, h):
-        pc = "P%d" % (4 + h)
-        op("V", cp(lmov(t, h), X(pc, 384, 392)), [pc], ["lk%d%d" % (t, h)])
-        m = X("MSG%d" % t, 16 * h, 16 * h + 16)
-        ks = ["lk%d%d" % (t, h), "of%d%d" % (t, h)]
-        if t < 3:
-            send(q + 1 if t < 2 else q + 2, X("LR%d" % (t + 1), 16 * h, 16 * h + 16), m, "al%d%d" % (t + 1, h), ks)
+    def newz(e, t, h):
+        a, b = half(h)
+        pz, o, k = "P%d" % h, X("zo%d" % t, a, b), "zo%d%d" % (t, h)
+        if e == "V":
+            op("V", ts(o, X(pz, 0, 128), MAGIC, MAGIC, A.add, A.subtract), [pz], [k])
         else:
-            send(q - 1, X("HM3", 8 * h, 8 * h + 8), lmov(3, h), "ah3%d" % h, ks[:1])
+            op("S", act(X("zm%d" % h), X(pz, 0, 128), IDN, bias=MAGIC), [pz], ["zm%d" % h])
+            op("S", act(o, X("zm%d" % h), IDN, bias=-MAGIC), ["zm%d" % h], [k])
+        if t < 3:
+            send(q + 1 if t < 2 else q + 2, X("zr%d" % (t + 1), a, b), o, "az%d%d" % (t + 1, h), [k])
+        else:
+            send(q - 1, X("zf", a, b), o, "az4%d" % h, [k])
 
-    def home_list(t):
-        send(q - 1 - t % 3, X("HM%d" % t), X("MSG%d" % t), "ah%d" % t, ["%s%d%d" % (k, t, h) for k in ("lk", "of") for h in (0, 1)])
+    def moves0(t, h):
+        a, b = half(h)
+        o = X("P6", 0, 128)
+        op("T", [mm(o, X("KM"), X("ones"), True, False), mm(o, X("I1"), X("L%d" % t, a, b), False, False)],
+           ["KM", "ones", "I1", "L%d%d" % (t, h)], ["P6"])
 
-    def number_pe(t):
-        o = X("P5", 400, 408)
-        op("T", [mm(o, X("nones"), X("rm%d" % h, 14, 128, 16), h == 0, h == 1) for h in range(2)], ["nones", "rm0", "rm1"], ["P5"])
+    def moves1(t, h):
+        d, pc = X("d%d" % t, 8 * h, 8 * h + 8), "P%d" % (4 + h)
+        op("T", [mm(X("P6", x, 128, 16), X("EX", 128 * x, 128 * x + 128), d, False, x == 15) for x in range(16)],
+           ["EX", "d%d%d" % (t, h)], ["P6"])
+        op("T", mm(X(pc, 128, 136), X("I2k"), d, True, False), ["I2k", "d%d%d" % (t, h)], [pc])
+
+    def moves2(t, h):
+        pc = "P%d" % (4 + h)
+        op("V", ts(X("ML%d" % h), X("P6", 0, 128), 0.0, STEP, A.max, A.min), ["P6"], ["ML%d" % h])
+        op("T", [mm(X(pc, 128, 136), X("D16", 16 - x, 144 - x), X("ML%d" % h, x, 128, 16), False, x == 15) for x in range(16)],
+           ["D16", "ML%d" % h], [pc])
+
+    def moves3(t, h):
+        pc, m = "P%d" % (4 + h), "mo%d%d" % (t, h)
+        op("V", ts(X(m), X(pc, 128, 136), -15 * STEP, None, A.add), [pc], [m])
+        send((q + 1, q + 1, q + 2, q - 1)[t], X("mr%d%d" % (t, h)), X(m), "am%d%d" % (t, h), [m])
+
+    def home(t):
+        send(q - 1 - t % 3, X("dk", 16 * t, 16 * t + 16), X("d%d" % t), "ad%d" % t, ["d%d0" % t, "d%d1" % t])
 
     def number(t):
-        op("V", lambda: V.tensor_reduce(X("cR"), X("P5", 400, 408), AxisListType.X, A.add), ["P5"], ["cR"])
-        op("V", cp(X("cAi"), X("cR")), ["cR"], ["cAi"])
-        vts("cAj", "cAi", 255, None, A.bitwise_and)
-        vts("cA", "cAj", 32.0, "ck", A.mult, A.add)
+        o = X("P7", 32, 33)
+        op("S", act(X("sg"), X("d%d" % t), SIGN, accum_out=X("acc")), ["d%d0" % t, "d%d1" % t], ["sg", "acc"])
+        op("T", mm(o, X("nones"), X("acc")), ["nones", "acc"], ["P7"])
+        op("S", act(X("n16"), o, IDN, bias=1025 - 127.5 / 256, scale=2.0 ** -8), ["P7"], ["n16"])
+        op("S", act(X("cC"), o, IDN, bias=X("ckA")), ["P7", "ckA"], ["cC"])
+        op("S", act(X("cA"), X("n16"), IDN, bias=X("cC"), scale=-256.0), ["n16", "cC"], ["cA"])
+
+    def places_pe(t):
+        op("T", [mm(X("P7", 0, 16), X("Dw", 16 - x, 144 - x), X("zr%d" % t, x, 256, 16), x == 0, x == 15) for x in range(16)],
+           ["Dw", "zr%d0" % t, "zr%d1" % t], ["P7"])
+
+    def places(t):
+        op("V", cp(X("uI"), X("P7", 0, 16)), ["P7"], ["uI"])
+        vts("uJ", "uI", 31, None, A.bitwise_and)
+        op("V", tt(X("uK"), X("uJ"), X("rb"), A.add), ["uJ", "rb"], ["uK"])
+        op("V", cp(X("UL"), X("uK")), ["uK"], ["UL"])
 
     def old(t):
-        op("S", act(X("old"), X("R").indirect(X("UL"))), ["R", "Ra", "UL"], ["old"])
+        op("S", act(X("old"), X("R", 0, 8192).indirect(X("UL"))), ["R", "Ra", "UL"], ["old"])
 
-    def strat_pe(t, h):
-        a, b = half(h)
-        o = X("P6", a, b)
-        op("T", [mm(o, X("I4"), X("ls%d" % h), False, False), mm(o, X("I4"), X("hs%d" % h), False, True)],
-           ["I4", "hs%d" % h, "ls%d" % h], ["P6"])
+    def rounded(e, h):
+        pr, o = "P%d" % (2 + h), "rn%d" % h
+        op(e, ts(X(o), X(pr, 0, 128), -0.375, None, A.add) if e == "V" else act(X(o), X(pr, 0, 128), IDN, bias=-0.375), [pr], [o])
 
-    def strat_pre(t, h):
-        a, b = half(h)
-        o = X("P6", a, b)
-        op("T", [mm(o, X("cr"), X("ones"), True, False), mm(o, X("I2"), X("old", a, b), False, False)],
-           ["cr", "ones", "I2", "old"], ["P6"])
+    def scatter(h):
+        op("V", cp(X("R", 0, 8192).indirect(X("UL", 8 * h, 8 * h + 8)), X("rn%d" % h)), ["rn%d" % h, "UL"], ["R"])
+        if h == 0:
+            op("V", cp(X("R", 8192, 9216).indirect(X("UL", 0, 2)), X("rn0", 0, 32)), ["rn0", "UL"], ["Rd"])
 
-    def strat_r(t, h):
-        a, b = half(h)
-        rounded(h, X("rn%d" % h), X("P6", a, b), "P6", "rn%d" % h)
+    def verdict_rows(p, t0, t1):
+        n = 256 * (t1 - t0)
+        op("T", [mm(X(p, x, n, 16, rows=slice(0, 8)), X("EX", 128 * x, 128 * x + 128, 16), X("dk", 16 * t0, 16 * t1)) for x in range(16)],
+           ["EX"] + ["dk%d" % t for t in range(t0, t1)], [p])
 
-    def strat_v(t, h):
-        op("V", cp(X("R").indirect(X("UL", 8 * h, 8 * h + 8)), X("rn%d" % h)), ["rn%d" % h, "UL"], ["R"])
-
-    def table(w, r, banks=("P0", "P7")):
-        for k in range(2):
-            a, p = 512 * k, banks[k]
-            op("T", mm(X(p), X("Sh1"), X(r, a, a + 512)), ["Sh1", r], [p])
-            op("S", act(X(w, a, a + 512), X(p)), [p], [w])
-
-    def runs(t):
-        if t == 0:
-            return [((32 * b, 32 * b + 32, None), (b, 128, 4)) for b in range(4)]
-        if t == 1:
-            return [((b, 128, 4), (32 * b, 32 * b + 32, None)) for b in range(4)]
-        if t == 2:
-            return [((64 * b, 64 * b + 64, None), (b, 128, 2)) for b in range(2)]
-        return [((b, 128, 8), (16 * b, 16 * b + 16, None)) for b in range(8)]
-
-    def permuted(at, sh, Lb, t, nf, shn):
-        cs = []
-        for h in range(2):
-            for (a, b, st), (c, d, dst) in runs(t):
-                o = X("P7", at + 128 * h + c, at + 128 * h + d, dst)
-                cs.append((o, X(sh), X(Lb, 128 * h + a, 128 * h + b, st)))
-        if nf is None:
-            return [mm(*c) for c in cs]
-        o = X("P7", at, at + 256)
-        return [mm(o, X(shn), X("Lo"), True, False), mm(o, X(shn), X("Hi%d" % nf), False, False)] + [
-            mm(*c, False, c is cs[-1]) for c in cs]
-
-    def shifted(w, at, Lb, t, t_before, t_mover):
-        shifted_pe(Lb, t, t_before, t_mover)
-        shifted_act(w, at, t_before)
-
-    def shifted_act(w, at, t_before):
-        n = 512 if t_before else 256
-        op("S", act(X(w, at, at + n), X("P7", 0, n)), ["P7"], [w])
-
-    def shifted_pe(Lb, t, t_before, t_mover):
-        n = 0
-        cs = []
-        if t_before:
-            cs += permuted(0, "Sh1", Lb, t, None, None)
-            n = 256
-        cs += permuted(n, "Sh2", Lb, t, t_mover, "Sh1")
-        op("T", cs, ["Sh1", "Sh2", Lb, "Lo", "Hi%d" % t_mover], ["P7"])
-
-    def resumed(Lb, w, lst, keys, t):
-        for h in range(2):
-            a, b = half(h)
-            op("V", tt(X(Lb, a, b), X(w).indirect(X(lst, 16 * h, 16 * h + 8)), X("N%d" % t, a, b), A.add),
-               [w, "N%d" % t] + keys, [Lb])
-
-    for t in range(4):
-        at(0 if t == 0 else 10 * t)
-        if t == 0:
-            pre_L(0, 0); pre_n(0, 0); pre_n(0, 1)
-            for h in range(2):
-                if h:
-                    pre_L(0, 1)
-                pre_u(0, h); pre_z(0, h); pre_a(0, h); pre_b(0, h)
-        for j in range(2 if t else 0, len(SUB[0]) - 1):
-            gather(t, 0, j)
-        slist(t, 0)
-        if t == 0:
-            slist(t, 1)
-            at(2)
-            late_constants()
-            at(4)
-        if t == 0:
-            compare(t, 0, 0)
-            counts(t, 0, 0)
-            gather(t, 1, 0)
-            op("V", cp(X("oS"), X("voI")), ["voI"], ["oS"])
-            send(q + 2, X("rOB"), X("oS"), "aOB", ["oS"])
-        if t:
-            table(("PC", "OA", "SP")[t - 1], ("rPC", "rOA", "pS")[t - 1], ("P7", "P5"))
-        for j in range(1, len(SUB[0]) - 1):
-            compare(t, 0, j)
-            if j == len(SUB[0]) - 2:
-                if t:
-                    pre_n(t, 1)
-                    pre_u(t, 1)
-                    pre_z(t, 1)
-            counts(t, 0, j)
-        if t:
-            slist(t, 1)
-            scan_hi(t, 0)
-            pre_L(t, 1); pre_a(t, 1); pre_b(t, 1)
-            gather(t, 1, 0)
-        if t == 1:
-            shifted_pe("L0C", 0, False, 0)
-        if t == 2:
-            resumed("L1A", "OA", "MSG0", ["lk00", "lk01"], 0)
-            shifted_pe("L1A", 1, True, 1)
-        if t == 3:
-            shifted_pe("L0h", 0, False, 0)
-        if t == 3:
-            for h in range(2):
-                op("V", cp(X("L3h", *half(h)), X(Lk(3, h))), [Lk(3, h)], ["L3h"])
-            send(q - 1, X("L3r"), X("L3h"), "aL3", ["L3h"])
-        if t == 0:
-            scan_hi(t, 0)
-        scan_lo(t, 0)
-        verdict(t, 0)
-        select(t, 0)
-        for j in range(1, len(SUB[1]) - 1):
-            gather(t, 1, j)
-        if t < 3:
-            ulist(t)
-            old(t)
-        moves_pe(t, 0, 0, BC)
-        newz_pe(t, 0)
-        moves_pe(t, 0, BC, 16)
-        compare(t, 1, 0, (0, 1))
-        newz(t, 0)
-        compare(t, 1, 0, (2, 3))
-        moves_a(t, 0)
-        if t == 0:
-            number_n(0)
-        else:
-            shifted_act(("PC", "OA", "SP")[t - 1], 1024, t == 2)
-        if t < 3:
-            strat_pre(t, 0)
-            strat_pe(t, 0)
-            strat_r(t, 0)
-        if t == 0:
-            number_lo()
-            number_hi(0)
-        if t == 1:
-            for k in (1, 2, 3):
-                number_n(k)
-                number_hi(k)
-        counts(t, 1, 0)
-        for j in range(1, len(SUB[1]) - 1):
-            compare(t, 1, j)
-            counts(t, 1, j)
-        moves_b(t, 0)
-        if t < 3:
-            strat_pre(t, 1)
-        if t == 0:
-            table("OB", "rOB", ("P1", "P7"))
-        scans(t, 1)
-        if t < 3:
-            strat_v(t, 0)
-        verdict(t, 1)
-        if t == 3:
-            send(q - 1, X("HM3", 16, 32), X("MSG3", 16, 32), "aho", ["of30", "of31"])
-        if t < 3:
-            number_pe(t)
-            pre_n(t + 1, 0)
-        select(t, 1, t == 3)
-        if t < 3:
-            number(t)
-            moves_pe(t, 1, 0, BC)
-            pre_u(t + 1, 0)
-            pre_z(t + 1, 0)
-            strat_pe(t, 1)
-            newz_pe(t, 1)
-            moves_pe(t, 1, BC, 16)
-            pre_L(t + 1, 0)
-            pre_a(t + 1, 0); pre_b(t + 1, 0)
-            strat_r(t, 1)
-            strat_v(t, 1)
-            newz(t, 1)
-            gather(t + 1, 0, 0)
-            moves_a(t, 1)
-            compare(t + 1, 0, 0)
-            counts(t + 1, 0, 0)
-            gather(t + 1, 0, 1)
-            if t == 2:
-                verdicts_home(0)
-                verdicts_home(1)
-            else:
-                list_constants(t)
-            moves_b(t, 1)
-            home_list(t)
-            if t == 0:
-                send(q + 1, X("rOA"), X("oS"), "aOA", ["oS"])
-        else:
-            moves_pe(t, 1, 0, 8)
-            moves_pe(t, 1, 8, 16)
-            newz_pe(t, 1)
-            moves_v(t, 1, 0, 8)
-            moves_f(t, 1, 0, 8)
-            verdicts_home(2)
-            moves_v(t, 1, 8, 16)
-            moves_f(t, 1, 8, 16)
-            newz(t, 1)
-            op("T", permuted(0, "Sh1", "L3r", 3, 3, "I1"), ["Sh1", "I1", "L3r", "Lo", "Hi3"], ["P7"])
-            op("S", act(X("yob"), X("P7", 0, 256)), ["P7"], ["yob"])
-            dma("Y", T.yo[:, :], X("yob"), ["yob"], [])
-            for k in range(2):
-                op("T", [mm(X("P%d" % k, 48 * x, 48 * x + 48), X("EX", 128 * (8 * k + x), 128 * (8 * k + x) + 128), X("kall", 0, 48))
-                         for x in range(8)],
-                   ["kall"] + ["EX%d" % x for x in range(16)], ["P%d" % k])
-                op("S", act(X("ykr", 384 * k, 384 * k + 384), X("P%d" % k, 0, 384)), ["P%d" % k], ["ykr"])
-            moves_b(t, 1)
-            resumed("L2H", "SP", "HM1", ["HM1"], 1)
-            shifted("SP", 1280, "L2H", 2, True, 2)
-            op("V", cp(X("hk", 96, 112), X("HM3", 16, 32)), ["HM3o"], ["hk3"])
-            for h in range(2):
-                op("V", tt(X("kall", 48 + 8 * h, 56 + 8 * h), X("hk", 96 + 8 * h, 104 + 8 * h), X("k16"), A.subtract),
-                   ["hk3", "k16"], ["kal3"])
-
-    at(50)
-    op("T", [mm(X("P2", 16 * x, 16 * x + 16), X("EX", 128 * x, 128 * x + 128), X("kall", 48, 64)) for x in range(16)],
-       ["kal3"] + ["EX%d" % x for x in range(16)], ["P2"])
-    op("S", act(X("ykn", 0, 768), X("ykr", 0, 768).indirect(X("yl", 0, 48))), ["ykr", "yl"], ["ykn"])
+    def verdict_out(p, t0, t1):
+        n = 256 * (t1 - t0)
+        op("S", act(X("ykn", 256 * t0, 256 * t1, rows=slice(0, 8)), X(p, 0, n, rows=slice(0, 8)), IDN, bias=15.0, scale=1.0 / STEP), [p],
+           ["ykn%d" % t0])
 
     def yp_half(h):
         a, b = half(h)
-        op("V", tt(X("ypb", a, b), X("SP").indirect(X("HM3", 8 * h, 8 * h + 8)), X("N3", a, b), A.add),
-           ["SP", "HM3%d" % h, "N3"], ["ypb"])
+        op("V", tt(X("ypb", a, b), X("PS").indirect(X("mr3%d" % h)), X("N", 768 + a, 768 + b), A.max), ["PS", "PSx", "mr3%d" % h, "N"],
+           ["ypb%d" % h])
 
-    yp_half(0)
-    yp_half(1)
-    dma("Y", T.yz[:, :], X("zf"), ["zf0", "zf1"], [])
-    dma("Y", T.yp[:, :], X("ypb"), ["ypb"], [])
-    op("S", act(X("ykr3"), X("P2", 0, 256)), ["P2"], ["ykr3"])
-    op("S", act(X("ykn", 768, 1024), X("ykr3").indirect(X("yl", 48, 64))), ["ykr3", "yl"], ["ykn"])
-    dma("S", T.yk[:, :], T["ykn"][0:128:16, :], ["ykn"], [])
-    prog.sort(key=lambda e: e[:2])
-    for _, _, f, a in prog:
-        f(*a)
+    for h in range(2):
+        sums(0, h); product(0, h); address(0, h); z4(0, h)
+    places_pe(0); places(0)
+    send(q + 2, X("OB"), X("OS"), "aOB", ["OS", "OSa"])
+    hand(0, "PS", ["PS", "PSx"])
+    hand(1, "OS", ["OS", "OSa"])
+
+    for t in range(4):
+        gather(t, "V", 0, 2); gather(t, "S", 2, 4); gather(t, "S", 4, 6); gather(t, "S", 6, 8)
+        counts0(0); moves0(t, 0)
+        compare(0, 2); compare(2, 4); counts(0, 4)
+        compare(4, 6)
+        if t:
+            sums(t, 1); z4(t, 1)
+        compare(6, 8); counts(4, 8)
+        if t:
+            lookup(t, 1); product(t, 1); address(t, 1)
+            send((q - 1, q + 1, q - 1)[t - 1], X("L%dr" % t), X("L%d" % t), "aL%d" % t, ["L%d0" % t, "L%d1" % t])
+        gather(t, "S", 8, 11)
+        counts0(1)
+        if t < 3:
+            if t:
+                places_pe(t)
+            scan_hi(0, 8)
+            verdict(t, 0); moves1(t, 0)
+            if t:
+                places(t)
+            select("S", "HI", 0)
+            old(t)
+            scan_lo(0, 4); moves2(t, 0); scan_lo(4, 8); moves3(t, 0)
+            mean_pe(t, 0, "HI")
+            gather(t, "S", 11, 13)
+            select("S", "LO", 0); mean_pe(t, 0, "LO"); newz("S", t, 0)
+            gather(t, "S", 13, 16)
+            rounded("S", 0)
+            moves0(t, 1)
+            compare(8, 11); compare(11, 12); counts(8, 12); compare(12, 13); compare(13, 16); counts(12, 16)
+            if t == 2:
+                grow_pe("L1r", ["L1r"], True, 1); grow("OA", 1024, 512)
+            sums(t + 1, 0)
+            scatter(0)
+            scan_hi(8, 16)
+            verdict(t, 1); moves1(t, 1)
+            number(t)
+            select("S", "HI", 1); mean_pe(t, 1, "HI")
+            lookup(t + 1, 0); product(t + 1, 0)
+            scan_lo(8, 12); moves2(t, 1); scan_lo(12, 16); moves3(t, 1)
+            select("S", "LO", 1); mean_pe(t, 1, "LO")
+            address(t + 1, 0)
+            rounded("V", 1); newz("S", t, 1)
+            scatter(1)
+            z4(t + 1, 0)
+            home(t)
+        else:
+            verdict(t, 0); moves1(t, 0)
+            scan_hi(0, 4); moves2(t, 0); scan_hi(4, 8); moves3(t, 0)
+            gather(t, "S", 11, 13); gather(t, "S", 13, 16)
+            moves0(t, 1)
+            grow_pe("L2r", ["L2r"], True, 2); grow("PS", 1280, 512)
+            scan_lo(0, 8)
+            select("S", "HI", 0); mean_pe(t, 0, "HI")
+            select("S", "LO", 0); mean_pe(t, 0, "LO")
+            compare(8, 11); compare(11, 12); counts(8, 12); compare(12, 13); compare(13, 16); counts(12, 16)
+            newz("S", t, 0)
+            verdict_rows("P2", 0, 2); verdict_out("P2", 0, 2); verdict_rows("P3", 2, 3); verdict_out("P3", 2, 3)
+            dma("Y", T.yk[:, 0:768], X("ykn", 0, 768, rows=slice(0, 8)), ["ykn0", "ykn2"], [])
+            op("T", [mm(X("P7", 0, 256), X("Se0"), X("N", 768, 1024), True, False), mm(X("P7", 0, 256), X("Sh1"), X("L3r"), False, True)],
+               ["Se0", "Sh1", "N", "L3r"], ["P7"])
+            op("S", act(X("yob"), X("P7", 0, 256)), ["P7"], ["yob"])
+            dma("Y", T.yo[:, :], X("yob"), ["yob"], [])
+            scan_hi(8, 12)
+            verdict(t, 1); moves1(t, 1); home(t)
+            scan_hi(12, 16); moves2(t, 1)
+            select("S", "HI", 1); mean_pe(t, 1, "HI")
+            scan_lo(8, 12); moves3(t, 1); scan_lo(12, 16)
+            select("V", "LO", 1); mean_pe(t, 1, "LO")
+            yp_half(0)
+            newz("V", t, 1)
+            yp_half(1)
+            dma("Y", T.yp[:, :], X("ypb"), ["ypb0", "ypb1"], [])
+            verdict_rows("P2", 3, 4); verdict_out("P2", 3, 4)
+            dma("S", T.yk[:, 768:1024], X("ykn", 768, 1024, rows=slice(0, 8)), ["ykn3"], [])
+            dma("Y", T.yz[:, :], X("zf"), ["zf0", "zf1"], [])
+
     for sem, v in used.items():
         if clock["G"].get(sem, 0) < v:
             g.wait_ge(T.sem[sem], v)

@@ -11,6 +11,8 @@ MAGIC = 12582912.0
 BIG = 8192.0
 STEP = 2048.0
 USES_OTHERS = True
+TAG = [""]
+VY = (6, 6)
 
 
 def _scratch():
@@ -22,9 +24,9 @@ def _scratch():
     sb("R", 9216, b); sb("Y", 4096, b); sb("HI", 4096, b); sb("LO", 4096, b)
     s["B"] = ("sbuf", [128, 16, 256], b)
     for k in range(2):
-        sb("al%d" % k, 128, u); sb("nb%d" % k, 128, h); sb("pr%d" % k, 128, i); sb("aj%d" % k, 128, i); sb("pf%d" % k, 128, f)
+        sb("al%d" % k, 128, u); sb("pr%d" % k, 128, i); sb("aj%d" % k, 128, i); sb("pf%d" % k, 128, f)
         sb("st%d" % k, 128, h); sb("ML%d" % k, 128, h); sb("hs%d" % k, 128, b); sb("ls%d" % k, 128, b)
-        sb("rn%d" % k, 128, i); sb("of%d" % k, 8, u); sb("zm%d" % k, 128, f)
+        sb("rn%d" % k, 128, i); sb("of%d" % k, 8, u); sb("qc%d" % k, 128, b); sb("zT%d" % k, 128, b)
     for t in range(4):
         sb("L%d" % t, 256, h); sb("zo%d" % t, 256, b); sb("zr%d" % t, 256, b); sb("d%d" % t, 16, b)
         for k in range(2):
@@ -32,21 +34,19 @@ def _scratch():
     sb("dk", 64, b); sb("zf", 256, b); sb("zs", 256, b); sb("sg", 16, b)
     for n in ("L0h", "L1r", "L2r", "L3r"):
         sb(n, 256, h)
-    for n in ("uI", "uJ", "uK", "rb", "mvI"):
-        sb(n, 16, i)
-    sb("UL", 16, u); sb("mvu", 16, u); sb("old", 256, b)
+    sb("mvI", 16, i); sb("rb", 16, b); sb("KP", 32, b); sb("KN", 2, b); sb("KU", 256, b); sb("UL", 16, u); sb("mvu", 16, u); sb("old", 256, b)
     for n, w, d in (("vpI", 1024, i), ("OS", 1024, i), ("OB", 1024, i), ("OA", 1536, i), ("PS", 1792, f), ("PC", 1280, f),
-                    ("pH", 1024, h), ("N", 1024, h), ("EX", 2048, b), ("s0", 2048, b), ("s1", 2048, b), ("ykn", 1024, f)):
+                    ("pH", 1024, h), ("N", 1024, h), ("EX", 2048, b), ("s0", 2048, b), ("s1", 2048, b), ("ykn", 1024, f),
+                    ("En", 512, b)):
         sb(n, w, d)
     for n in ("ip", "p16", "pg", "wI"):
         sb(n, 1, i)
-    for n in ("pf", "p16f", "pgf", "pg16", "wf", "ck32", "ckA", "cA", "cC", "acc", "x16", "x32", "low", "kk"):
+    for n in ("pf", "p16f", "pgf", "pg16", "wf", "ck32", "ck", "cA", "acc", "x16", "x32", "low", "kk", "m0"):
         sb(n, 1, f)
-    sb("n16", 1, h)
-    sb("fr", 144, f); sb("Dn", 144, b); sb("Dw", 144, b); sb("D16", 144, b)
-    for n in ("I1", "I2", "I2e", "I4", "I4k", "I2k", "I256", "KM", "bda", "bdb", "BD", "WB", "Cm", "ones", "qc", "Sh1", "Sh2", "Se0", "Se1"):
+    sb("fr", 144, f); sb("Dn", 144, b); sb("Dw", 144, b); sb("Dv", 144, b); sb("D16", 144, b)
+    for n in ("I1", "I2", "I2e", "I4", "Im", "Is", "KM", "bda", "bdb", "BD", "WB", "WN", "KQ", "KZ", "ones", "mones", "Sh1", "Sh2", "Se0", "Se1"):
         sb(n, 128, b)
-    sb("nones", 128, f); sb("ind", 16, f); sb("il", 256, f); sb("iy", 128, f); sb("Xc", 128, h); sb("ir", 16, f)
+    sb("nones", 128, f); sb("pones", 128, f); sb("il", 256, f); sb("iy", 128, f); sb("Xc", 128, h)
     sb("ypb", 256, f); sb("yob", 256, f)
     return s
 
@@ -76,7 +76,7 @@ def _pack():
 SCRATCH = _pack()
 _ARR = ["aL0", "az0", "aOB", "aPC", "aOA", "aL1", "aL2", "aL3", "ahand"] + ["am%d%d" % (t, h) for t in range(4) for h in (0, 1)] \
     + ["az%d%d" % (t, h) for t in (1, 2, 3, 4) for h in (0, 1)] + ["ad%d" % t for t in range(4)]
-SEMAPHORES = ["sV", "sT", "sS", "sG", "ls"] + ["d%d" % k for k in range(24)] + _ARR
+SEMAPHORES = ["sV", "sT", "sS", "sG", "ls", "sent"] + ["d%d" % k for k in range(24)] + _ARR
 
 HANDED = (("PC", 1280, "aPC", 3), ("OA", 1024, "aOA", 1))
 
@@ -169,6 +169,7 @@ def rank_program(g, core, T, topo):
 
     def op(qn, calls, R, W):
         before(qn, R, W)
+        TAG[0] = W[0]
         calls = calls if isinstance(calls, list) else [calls]
         for c in calls:
             ins = c()
@@ -225,6 +226,12 @@ def rank_program(g, core, T, topo):
         f = lambda s: X(s) if isinstance(s, str) else s
         op("V", ts(X(o), X(i), f(s1), f(s2), o0, o1), rd, [o])
 
+    def plus(e, o, i, c, R, W):
+        if e == "S":
+            op("S", act(o, i, IDN, bias=c), R, W)
+        else:
+            op("V", ts(o, i, c, None, A.add), R, W)
+
     def fill(name, v, a=None, b=None, step=None, rows=None, over=False):
         op("V", lambda: V.memset(X(name, a, b, step, rows), v), [name] if over else [], [name])
 
@@ -233,6 +240,9 @@ def rank_program(g, core, T, topo):
             op("G", lambda: G.iota(X(name), pattern, base, cm), [], [name])
         else:
             op("G", lambda: G.iota(X(name), pattern, base, cm, allow_small_or_imprecise_dtypes=True), [], [name])
+
+    def where(o, i, pattern, base, cm, R, W):
+        op("G", lambda: G.affine_select(o, i, pattern, A.is_equal, 0.0, base, cm), R + ["where"], W + ["where"])
 
     def scaled(o, i, s):
         op("S", act(X(o), X(i), scale=X(s) if isinstance(s, str) else s), [i] + ([s] if isinstance(s, str) else []), [o])
@@ -252,129 +262,53 @@ def rank_program(g, core, T, topo):
     for t in range(4):
         arrives(q + 1 + t % 3, "ad%d" % t, "dk%d" % t)
 
-    dma("Y", X("mvI"), T.mv[:, :], [], ["mvI"])
-    dma("Y", X("vpI"), T.vp[:, :], [], ["vpI"])
-    dma("S", X("zs"), T.z0[:, :], [], ["zs"])
-    dma("S", X("wI"), T.wt[:, :], [], ["wI"])
-    dma("Y", X("R", 0, 4096), T.strat[:, 0:4096], [], ["Ra"])
-    dma("S", X("R", 4096, 8192), T.strat[:, 4096:8192], [], ["R"])
-    dma("Y", X("OS", rows=slice(1, 128)), T.vo[0:127, :], [], ["OS"])
-    dma("Y", X("OS", rows=slice(0, 1)), T.vo[0:1, :], [], ["OSa"])
-    dma("Y", X("R", 8192, 9216), T.strat[:, 0:1024], [], ["Rd"])
-
-    iota("ip", [[0, 1]], 0, 1, integer=True)
-    iota("fr", [[1, 144]], -16)
-    iota("il", [[1, 256]], 1024)
-    iota("iy", [[256, 8], [1, 16]])
-    iota("ir", [[512, 16]])
-    send(q + 1, X("zr0"), X("zs"), "az0", ["zs"])
-    fill("s0", 1.0); fill("s1", 0.0)
-    vts("p16", "ip", 15, None, A.bitwise_and)
-    vts("pg", "ip", 112, None, A.bitwise_and)
-    op("V", cp(X("pf"), X("ip")), ["ip"], ["pf"])
-    op("V", cp(X("p16f"), X("p16")), ["p16"], ["p16f"])
-    op("V", cp(X("pgf"), X("pg")), ["pg"], ["pgf"])
-    fill("s0", 0.0, 0, 2048, 16, over=True); fill("s1", 256.0, 0, 2048, 16, over=True)
-    op("V", cp(X("mvu"), X("mvI")), ["mvI"], ["mvu"])
-    fr = X("fr", 16, 144)
-    op("V", ts(X("I1"), fr, X("pf"), None, A.is_equal), ["fr", "pf"], ["I1"])
-    vts("pg16", "pgf", 16.0, None, A.add)
-    op("V", ts(X("bda"), fr, X("pgf"), None, A.is_ge), ["fr", "pgf"], ["bda"])
-    op("V", ts(X("bdb"), fr, X("pg16"), None, A.is_lt), ["fr", "pg16"], ["bdb"])
-    op("V", ts(X("D16"), X("fr"), X("pgf"), None, A.is_equal), ["fr", "pgf"], ["D16"])
-    op("V", ts(X("ind"), X("fr", 16, 32), X("p16f"), STEP, A.is_equal, A.mult), ["fr", "p16f"], ["ind"])
-    op("V", tt(X("BD"), X("bda"), X("bdb"), A.mult), ["bda", "bdb"], ["BD"])
-    op("V", cp(X("wf"), X("wI")), ["wI"], ["wf"])
-    fill("ones", 1.0)
-    for k, v in enumerate((2.0 ** 17, 128.0, 1.0, 0.0)):
-        fill("Cm", v, rows=slice(32 * k, 32 * k + 32))
-    vts("ck32", "p16f", 37.0 * 32, None, A.mult)
-    scaled("WB", "BD", "wf"); scaled("I4k", "I1", -4096.0)
-    op("V", cp(X("L0h", 0, 128), X("vpI").indirect(X("mvu", 0, 8))), ["vpI", "mvu"], ["L0h0"])
-    op("S", act(X("L0h", 128, 256), X("vpI").indirect(X("mvu", 8, 16))), ["vpI", "mvu"], ["L0h1"])
-    send(q + 1, X("L0"), X("L0h"), "aL0", ["L0h0", "L0h1"])
-
-    op("V", cp(X("pH"), X("vpI")), ["vpI"], ["pH"])
-    for n, d in (("Sh1", 1), ("Sh2", 2)):
-        op("G", lambda n=n, d=d: G.affine_select(X(n), X("BD"), [[1, 128]], A.is_equal, 0.0, -d, -1), ["BD"], [n])
-    scaled("Dn", "D16", -BIG); scaled("Dw", "D16", "wf")
-    for x in range(16):
-        op("S", act(X("EX", 128 * x, 128 * x + 128), X("BD"), scale=X("ind", x, x + 1)), ["BD", "ind"], ["EX"])
-    fill("qc", 9.5 * BIG); fill("qc", -16 * BIG, 15, 128, 16, over=True)
-    fill("nones", -1.0)
-    vts("x16", "p16f", 16.0, None, A.mult)
-    vts("x32", "p16f", 32.0, None, A.mult)
-    vts("kk", "p16f", -STEP, 15 * STEP, A.mult, A.add)
-    vts("ckA", "p16f", 37.0, 256.0 * 1025, A.mult, A.add)
-    vts("low", "p16f", 0.0, -4096.0, A.is_gt, A.mult)
-    vts("Xc", "iy", "x16", None, A.add)
-    vts("rb", "ir", "x32", None, A.add)
-    for t in range(4):
-        op("V", ts(X("N", 256 * t, 256 * t + 256), X("il"), X("low"), 256.0 * t, A.add, A.add), ["il", "low"], ["N"])
-    for n, s in (("I2", 0.5), ("I2e", 0.5 - 2.0 ** -9), ("I4", 0.25), ("I2k", -STEP), ("KM", "kk")):
-        scaled(n, "I1", s)
-    for n, d in (("Se0", "I1"), ("Se1", "Sh1")):
-        op("V", ts(X(n), X(d), X("ind", 0, 1), 1.0 / STEP, A.mult, A.mult), [d, "ind"], [n])
-
-    def table_own():
-        for k in range(2):
-            a, p = 512 * k, "P%d" % (4 + k)
-            op("T", mm(X(p), X("Sh1"), X("pH", a, a + 512)), ["Sh1", "pH"], [p])
-            op("S", act(X("PS", a, a + 512), X(p)), [p], ["PS"])
-
-    def grow_pe(Lb, keys, resumed, t):
-        cs, n = [], 0
-        if resumed:
-            cs, n = [mm(X("P7", 0, 256), X("Sh1"), X(Lb))], 256
-        o = X("P7", n, n + 256)
-        cs += [mm(o, X("Se1"), X("N", 256 * t, 256 * t + 256), True, False), mm(o, X("Sh2"), X(Lb), False, True)]
-        op("T", cs, ["Sh1", "Sh2", "Se1", "N"] + keys, ["P7"])
-
-    def grow(w, at, n):
-        op("S", act(X(w, at, at + n), X("P7", 0, n)), ["P7"], [w + "x"])
-
-    def hand(k, src, keys):
-        buf, n, _, d = HANDED[k]
-        c = helpers(T, topo, q)[k]
-        write(c, inner(topo, core, c, T.cores[(q + d) % 4]), X(buf, 0, n), X(src, 0, n), "ahand", keys)
-
-    table_own()
-    grow_pe("L0h", ["L0h0", "L0h1"], False, 0)
-    grow("PS", 1024, 256)
-
     def lookup(t, h):
+        if t == 0:
+            return
         a, b = half(h)
         w = ("OB", "PC", "OA")[t - 1]
         op("V", tt(X("L%d" % t, a, b), X(w).indirect(X("mr%d%d" % (t - 1, h))), X("N", 256 * (t - 1) + a, 256 * (t - 1) + b), A.max),
            [w, w + "x", "mr%d%d" % (t - 1, h), "N"], ["L%d%d" % (t, h)])
 
-    def sums(t, h):
+    def const(o, k, a, n, st=False, sp=False, sign="ones"):
+        return mm(o, X(sign), X(k, a, a + n), st, sp)
+
+    def remainder(o, k, n, minus, plus_):
+        return [const(o, k, 0, n, True)] + minus + [const(o, k, n, n), const(o, k, n, n, sign="mones")] + plus_
+
+    def sums(t, h, pu="P2"):
         a, b = half(h)
-        zk, pu = "zr%d%d" % (t, h), "P%d" % (2 + h)
-        o, pn, z = X(pu, 0, 128), "P%d" % h, X("zr%d" % t, a, b)
-        op("T", [mm(o, X("Cm"), X("ones"), True, False)], ["Cm", "ones"], [pu])
-        op("T", [mm(X(pn, 128, 256), X("WB"), z)], ["WB", zk], [pn])
-        op("T", [mm(o, X("WB"), z, False, False)], ["WB", zk], [pu])
-        op("S", act(X("nb%d" % h), X(pn, 128, 256), IDN, bias=1025 - 2047.5 / 4096, scale=2.0 ** -12), [pn], ["nb%d" % h])
-        op("T", [mm(o, X("I4k"), X("nb%d" % h), False, True)], ["I4k", "nb%d" % h], [pu])
+        o, z = X(pu, 0, 128), X("zr%d" % t, a, b)
+        cs = remainder(o, "KU", 128, [mm(o, X("WN"), z, False, False)], [mm(o, X("WB"), z, False, False), const(o, "KQ", 0, 128, sp=True)])
+        op("T", cs[:1], ["KU", "KQ", "ones", "mones"], [pu])
+        op("T", cs[1:], ["WB", "WN", "zr%d%d" % (t, h)], [pu])
 
     def z4(t, h):
-        a, b = half(h)
-        op("T", [mm(X("P%d" % h, d, 512, 4), X("I1"), X("zr%d" % t, a, b)) for d in range(4)], ["I1", "zr%d%d" % (t, h)], ["P%d" % h])
+        n = 16 * VY[h]
+        op("T", [mm(X("P%d" % h, d, 4 * n, 4), X("I1"), X("zr%d" % t, 128 * h, 128 * h + n)) for d in range(4)],
+           ["I1", "zr%d%d" % (t, h)], ["P%d" % h])
 
-    def product(t, h):
+    def turned(t, h):
+        n = 128 - 16 * VY[h]
+        if n:
+            o = X("P3", 0, 128, rows=slice(0, n))
+            op("T", mm(o, X("zr%d" % t, 128 * h + 128 - n, 128 * h + 128), X("I1")), ["I1", "zr%d%d" % (t, h)], ["P3"])
+            op("S", act(X("zT%d" % h, rows=slice(0, n)), o, scale=-1.0), ["P3"], ["zT%d" % h])
+
+    def product(t, h, pu="P2"):
         a, b = half(h)
-        pu, o = "P%d" % (2 + h), ("pr%d" if t else "pf%d") % h
+        o = ("pr%d" if t else "pf%d") % h
         op("V", tt(X(o), X(pu, 0, 128), X("L%d" % t, a, b), A.mult), [pu, "L%d%d" % (t, h)], [o])
+
+    def raise0(t, h):
         if t == 0:
-            vts("pr%d" % h, o, "ck32", None, A.add)
+            vts("pr%d" % h, "pf%d" % h, "ck32", None, A.add)
+
+    def shift(h):
         vts("aj%d" % h, "pr%d" % h, 5, 8191, A.arith_shift_right, A.bitwise_and)
 
-    def address(t, h):
-        if t:
-            vts("al%d" % h, "aj%d" % h, "cA", None, A.add)
-        else:
-            op("V", cp(X("al%d" % h), X("aj%d" % h)), ["aj%d" % h], ["al%d" % h])
+    def address(e, t, h):
+        plus(e, X("al%d" % h), X("aj%d" % h), X("cA") if t else 0.0, ["aj%d" % h, "cA"][:2 if t else 1], ["al%d" % h])
 
     def ys(n, y0, y1):
         return ["%s_%d" % (n, y) for y in range(y0, y1)]
@@ -390,15 +324,26 @@ def rank_program(g, core, T, topo):
         op("V", [tt(T.B[:, y0:y1, d:256:4], X("Y", 256 * y0 + d, 256 * y1, 4), X("P%d" % h, 64 * (y0 - 8 * h), 64 * (y1 - 8 * h)), A.is_gt)
                  for d in range(4)], ys("Y", y0, y1) + ["P%d" % h], ys("B", y0, y1))
 
+    def less_z(y0, p):
+        h = y0 // 8
+        r = slice(16 * (y0 - 8 * h - VY[h]), 16 * (y0 - 8 * h - VY[h]) + 32)
+        op("T", mm(X(p), X("zT%d" % h, rows=r), X("En", rows=r), True, False), ["zT%d" % h, "En"], [p])
+
+    def differ(y0, p):
+        op("T", mm(X(p), X("I1"), X("Y", 256 * y0, 256 * y0 + 512), False, True), ["I1"] + ys("Y", y0, y0 + 2), [p])
+
+    def sign(y0, p):
+        op("S", act(T.B[:, y0:y0 + 2, :], X(p), SIGN, bias=-0.5), [p], ys("B", y0, y0 + 2))
+
     def counts0(h):
         pc = "P%d" % (4 + h)
-        op("T", mm(X(pc, 0, 128), X("I1"), X("qc"), True, False), ["I1", "qc"], [pc])
+        op("T", mm(X(pc, 0, 128), X("I1"), X("qc%d" % h), True, False), ["I1", "qc%d" % h], [pc])
 
-    def counts(y0, y1):
+    def counts(y0, y1, end=False):
         h = y0 // 8
         pc = "P%d" % (4 + h)
         op("T", [mm(X(pc, 16 * (y0 - 8 * h), 16 * (y1 - 8 * h)), X("Dn", 16 - x, 144 - x), T.B[:, y0:y1, 16 * x:16 * x + 16], False,
-                    x == 15 and y1 % 8 == 0) for x in range(16)], ["Dn"] + ys("B", y0, y1), [pc])
+                    x == 15 and end) for x in range(16)], ["Dn"] + ys("B", y0, y1), [pc])
 
     def scan_hi(y0, y1):
         a, b = 256 * y0, 256 * y1
@@ -410,42 +355,42 @@ def rank_program(g, core, T, topo):
         op("V", lambda: V.tensor_tensor_scan(X("LO", a, b), X("s1", 0, b - a), X("Y", a, b), 0.0, A.max, A.min), ["s1"] + ys("Y", y0, y1),
            ys("LO", y0, y1))
 
-    def verdict(t, h):
+    def verdict(h):
         pc, st = "P%d" % (4 + h), "st%d" % h
         op("V", lambda: V.tensor_tensor_scan(back(st), back(pc), back("Xc"), 0.0, A.min, A.max), [pc, "Xc"], [st])
+
+    def under(t, h):
+        st = "st%d" % h
         op("V", tt(X("d%d" % t, 8 * h, 8 * h + 8), X(st, 0, 128, 16), X("Xc", 15, 128, 16), A.subtract), [st, "Xc"], ["d%d%d" % (t, h)])
-        op("V", cp(X("of%d" % h), X(st, 0, 128, 16)), [st], ["of%d" % h])
+
+    def offsets(e, h):
+        plus(e, X("of%d" % h), X("st%d" % h, 0, 128, 16), 0.0, ["st%d" % h], ["of%d" % h])
 
     def select(e, w, h):
         s = ("hs%d" if w == "HI" else "ls%d") % h
         i = X(w, 2048 * h, 2048 * h + 2048).indirect(X("of%d" % h))
         op(e, cp(X(s), i) if e == "V" else act(X(s), i), ys(w, 8 * h, 8 * h + 8) + ["of%d" % h], [s])
 
-    def mean_pe(t, h, w):
-        a, b = half(h)
-        pz, pr = "P%d" % h, "P%d" % (2 + h)
-        s = ("hs%d" if w == "HI" else "ls%d") % h
+    def mean_z(h, w):
+        o = X("P%d" % h, 0, 128)
         if w == "HI":
-            op("T", [mm(X(pz, 0, 128), X("I2e"), X(s), True, False)], ["I2e", s], [pz])
-            if t < 3:
-                op("T", [mm(X(pr, 0, 128), X("I2"), X("old", a, b), True, False), mm(X(pr, 0, 128), X("I4"), X(s), False, False)],
-                   ["I2", "I4", "old", s], [pr])
+            op("T", mm(o, X("I2e"), X("hs%d" % h), True, False), ["I2e", "hs%d" % h], ["P%d" % h])
         else:
-            cs = [(mm(X(pz, 0, 128), X("I2"), X(s), False, True), pz)]
-            if t < 3:
-                cs.insert(h, (mm(X(pr, 0, 128), X("I4"), X(s), False, True), pr))
-                cs = cs[::-1] if h == 0 and False else cs
-            for c, p in (cs[::-1] if t < 3 else cs):
-                op("T", [c], ["I2", "I4", s], [p])
+            op("T", [mm(o, X("I2"), X("ls%d" % h), False, False), const(o, "KZ", 0, 128), const(o, "KZ", 0, 128, sp=True, sign="mones")],
+               ["I2", "KZ", "ls%d" % h], ["P%d" % h])
+
+    def mean_r(h, w, p):
+        a, b = half(h)
+        s = ("hs%d" if w == "HI" else "ls%d") % h
+        cs = [mm(X(p, 0, 128), X("I4"), X(s), False, w == "LO")]
+        if w == "HI":
+            cs.insert(0, mm(X(p, 0, 128), X("I2"), X("old", a, b), True, False))
+        op("T", cs, ["I2", "I4", "old", s], [p])
 
     def newz(e, t, h):
         a, b = half(h)
         pz, o, k = "P%d" % h, X("zo%d" % t, a, b), "zo%d%d" % (t, h)
-        if e == "V":
-            op("V", ts(o, X(pz, 0, 128), MAGIC, MAGIC, A.add, A.subtract), [pz], [k])
-        else:
-            op("S", act(X("zm%d" % h), X(pz, 0, 128), IDN, bias=MAGIC), [pz], ["zm%d" % h])
-            op("S", act(o, X("zm%d" % h), IDN, bias=-MAGIC), ["zm%d" % h], [k])
+        plus(e, o, X(pz, 0, 128), 0.0, [pz], [k])
         if t < 3:
             send(q + 1 if t < 2 else q + 2, X("zr%d" % (t + 1), a, b), o, "az%d%d" % (t + 1, h), [k])
         else:
@@ -454,58 +399,92 @@ def rank_program(g, core, T, topo):
     def moves0(t, h):
         a, b = half(h)
         o = X("P6", 0, 128)
-        op("T", [mm(o, X("KM"), X("ones"), True, False), mm(o, X("I1"), X("L%d" % t, a, b), False, False)],
-           ["KM", "ones", "I1", "L%d%d" % (t, h)], ["P6"])
+        op("T", [mm(o, X("KM"), X("ones"), True, False), mm(o, X("Is"), X("L%d" % t, a, b), False, False)],
+           ["KM", "ones", "Is", "L%d%d" % (t, h)], ["P6"])
 
     def moves1(t, h):
         d, pc = X("d%d" % t, 8 * h, 8 * h + 8), "P%d" % (4 + h)
         op("T", [mm(X("P6", x, 128, 16), X("EX", 128 * x, 128 * x + 128), d, False, x == 15) for x in range(16)],
            ["EX", "d%d%d" % (t, h)], ["P6"])
-        op("T", mm(X(pc, 128, 136), X("I2k"), d, True, False), ["I2k", "d%d%d" % (t, h)], [pc])
+        op("T", mm(X(pc, 128, 136), X("Im"), d, True, False), ["Im", "d%d%d" % (t, h)], [pc])
 
     def moves2(t, h):
         pc = "P%d" % (4 + h)
-        op("V", ts(X("ML%d" % h), X("P6", 0, 128), 0.0, STEP, A.max, A.min), ["P6"], ["ML%d" % h])
+        op("V", ts(X("ML%d" % h), X("P6", 0, 128), 0.0, 1.0, A.max, A.min), ["P6"], ["ML%d" % h])
         op("T", [mm(X(pc, 128, 136), X("D16", 16 - x, 144 - x), X("ML%d" % h, x, 128, 16), False, x == 15) for x in range(16)],
            ["D16", "ML%d" % h], [pc])
 
-    def moves3(t, h):
+    def moves3(e, t, h):
         pc, m = "P%d" % (4 + h), "mo%d%d" % (t, h)
-        op("V", ts(X(m), X(pc, 128, 136), -15 * STEP, None, A.add), [pc], [m])
+        if e == "V":
+            op("V", ts(X(m), X(pc, 128, 136), -15.0, STEP, A.add, A.mult), [pc], [m])
+        else:
+            op("S", act(X(m), X(pc, 128, 136), IDN, bias=-15 * STEP, scale=STEP), [pc], [m])
         send((q + 1, q + 1, q + 2, q - 1)[t], X("mr%d%d" % (t, h)), X(m), "am%d%d" % (t, h), [m])
 
     def home(t):
         send(q - 1 - t % 3, X("dk", 16 * t, 16 * t + 16), X("d%d" % t), "ad%d" % t, ["d%d0" % t, "d%d1" % t])
 
+    def views_on(t):
+        if t:
+            send((q - 1, q + 1, q - 1)[t - 1], X("L%dr" % t), X("L%d" % t), "aL%d" % t, ["L%d0" % t, "L%d1" % t])
+
     def number(t):
         o = X("P7", 32, 33)
         op("S", act(X("sg"), X("d%d" % t), SIGN, accum_out=X("acc")), ["d%d0" % t, "d%d1" % t], ["sg", "acc"])
-        op("T", mm(o, X("nones"), X("acc")), ["nones", "acc"], ["P7"])
-        op("S", act(X("n16"), o, IDN, bias=1025 - 127.5 / 256, scale=2.0 ** -8), ["P7"], ["n16"])
-        op("S", act(X("cC"), o, IDN, bias=X("ckA")), ["P7", "ckA"], ["cC"])
-        op("S", act(X("cA"), X("n16"), IDN, bias=X("cC"), scale=-256.0), ["n16", "cC"], ["cA"])
+        op("T", remainder(o, "KN", 1, [mm(o, X("pones"), X("acc"), False, False)], [mm(o, X("nones"), X("acc"), False, True)]),
+           ["KN", "pones", "nones", "acc"], ["P7"])
+        plus("S", X("cA"), o, X("ck"), ["P7", "ck"], ["cA"])
 
     def places_pe(t):
-        op("T", [mm(X("P7", 0, 16), X("Dw", 16 - x, 144 - x), X("zr%d" % t, x, 256, 16), x == 0, x == 15) for x in range(16)],
-           ["Dw", "zr%d0" % t, "zr%d1" % t], ["P7"])
+        o = X("P7", 128, 144)
+        s = [[mm(o, X(w, 16 - x, 144 - x), X("zr%d" % t, x, 256, 16), False, False) for x in range(16)] for w in ("Dv", "Dw")]
+        op("T", remainder(o, "KP", 16, s[0], s[1] + [mm(o, X("I1"), X("rb"), False, True)]),
+           ["Dw", "Dv", "KP", "rb", "zr%d0" % t, "zr%d1" % t], ["P7"])
 
-    def places(t):
-        op("V", cp(X("uI"), X("P7", 0, 16)), ["P7"], ["uI"])
-        vts("uJ", "uI", 31, None, A.bitwise_and)
-        op("V", tt(X("uK"), X("uJ"), X("rb"), A.add), ["uJ", "rb"], ["uK"])
-        op("V", cp(X("UL"), X("uK")), ["uK"], ["UL"])
+    def places(e):
+        plus(e, X("UL"), X("P7", 128, 144), X("x32"), ["P7", "x32"], ["UL"])
 
     def old(t):
         op("S", act(X("old"), X("R", 0, 8192).indirect(X("UL"))), ["R", "Ra", "UL"], ["old"])
 
-    def rounded(e, h):
-        pr, o = "P%d" % (2 + h), "rn%d" % h
-        op(e, ts(X(o), X(pr, 0, 128), -0.375, None, A.add) if e == "V" else act(X(o), X(pr, 0, 128), IDN, bias=-0.375), [pr], [o])
+    def rounded(e, h, p):
+        plus(e, X("rn%d" % h), X(p, 0, 128), -0.375, [p], ["rn%d" % h])
 
     def scatter(h):
-        op("V", cp(X("R", 0, 8192).indirect(X("UL", 8 * h, 8 * h + 8)), X("rn%d" % h)), ["rn%d" % h, "UL"], ["R"])
-        if h == 0:
-            op("V", cp(X("R", 8192, 9216).indirect(X("UL", 0, 2)), X("rn0", 0, 32)), ["rn0", "UL"], ["Rd"])
+        op("V", cp(X("R", 0, 8192).indirect(X("UL", 8 * h, 8 * h + 8)), X("rn%d" % h)), ["rn%d" % h, "UL", "R"], ["R"])
+
+    def mirror():
+        op("V", cp(X("R", 8192, 9216).indirect(X("UL", 0, 2)), X("rn0", 0, 32)), ["rn0", "UL"], ["Rd"])
+
+    def table_own():
+        for k in range(2):
+            a, p = 512 * k, "P%d" % (4 + k)
+            op("T", mm(X(p), X("Sh1"), X("pH", a, a + 512)), ["Sh1", "pH"], [p])
+            op("S", act(X("PS", a, a + 512), X(p)), [p], ["PS"])
+
+    def grow_pe(p, Lb, keys, resumed, t):
+        cs, n = [], 0
+        if resumed:
+            cs, n = [mm(X(p, 0, 256), X("Sh1"), X(Lb))], 256
+        o = X(p, n, n + 256)
+        cs += [mm(o, X("Se1"), X("N", 256 * t, 256 * t + 256), True, False), mm(o, X("Sh2"), X(Lb), False, True)]
+        op("T", cs, ["Sh1", "Sh2", "Se1", "N"] + keys, [p])
+
+    def grow(p, w, at, n):
+        op("S", act(X(w, at, at + n), X(p, 0, n)), [p], [w + "x"])
+
+    def grow_o(t, k):
+        if t == 2:
+            if k == 0:
+                grow_pe("P3", "L1r", ["L1r"], True, 1)
+            else:
+                grow("P3", "OA", 1024, 512)
+
+    def hand(k, src, keys):
+        buf, n, _, d = HANDED[k]
+        c = helpers(T, topo, q)[k]
+        write(c, inner(topo, core, c, T.cores[(q + d) % 4]), X(buf, 0, n), X(src, 0, n), "ahand", keys)
 
     def verdict_rows(p, t0, t1):
         n = 256 * (t1 - t0)
@@ -514,97 +493,143 @@ def rank_program(g, core, T, topo):
 
     def verdict_out(p, t0, t1):
         n = 256 * (t1 - t0)
-        op("S", act(X("ykn", 256 * t0, 256 * t1, rows=slice(0, 8)), X(p, 0, n, rows=slice(0, 8)), IDN, bias=15.0, scale=1.0 / STEP), [p],
-           ["ykn%d" % t0])
+        plus("S", X("ykn", 256 * t0, 256 * t1, rows=slice(0, 8)), X(p, 0, n, rows=slice(0, 8)), 15.0, [p], ["ykn%d" % t0])
+
+    def yo_pe(p):
+        op("T", [mm(X(p, 0, 256), X("Se0"), X("N", 768, 1024), True, False), mm(X(p, 0, 256), X("Sh1"), X("L3r"), False, True)],
+           ["Se0", "Sh1", "N", "L3r"], [p])
+
+    def yo_out(p):
+        op("S", act(X("yob"), X(p, 0, 256)), [p], ["yob"])
+        dma("Y", T.yo[:, :], X("yob"), ["yob"], [])
+
+    def yk_out(e, t0, t1):
+        dma(e, T.yk[:, 256 * t0:256 * t1], X("ykn", 256 * t0, 256 * t1, rows=slice(0, 8)), ["ykn0", "ykn2"] if t0 == 0 else ["ykn3"], [])
+
+    def yp_out():
+        dma("Y", T.yp[:, :], X("ypb"), ["ypb0", "ypb1"], [])
+
+    def yz_out():
+        dma("Y", T.yz[:, :], X("zf"), ["zf0", "zf1"], [])
 
     def yp_half(h):
         a, b = half(h)
         op("V", tt(X("ypb", a, b), X("PS").indirect(X("mr3%d" % h)), X("N", 768 + a, 768 + b), A.max), ["PS", "PSx", "mr3%d" % h, "N"],
            ["ypb%d" % h])
 
+    dma("Y", X("mvI"), T.mv[:, :], [], ["mvI"])
+    dma("Y", X("vpI"), T.vp[:, :], [], ["vpI"])
+    dma("S", X("zs"), T.z0[:, :], [], ["zs"])
+    dma("S", X("wI"), T.wt[:, :], [], ["wI"])
+    dma("Y", X("R", 0, 3072), T.strat[:, 0:3072], [], ["Ra"])
+
+    iota("ip", [[0, 1]], 0, 1, integer=True)
+    iota("fr", [[1, 144]], -16)
+    iota("il", [[1, 256]], 1024)
+    send(q + 1, X("zr0"), X("zs"), "az0", ["zs"])
+    iota("iy", [[256, 8], [1, 16]])
+    iota("rb", [[512, 16]])
+    fill("s0", 1.0)
+    vts("p16", "ip", 15, None, A.bitwise_and)
+    vts("pg", "ip", 112, None, A.bitwise_and)
+    op("V", cp(X("pf"), X("ip")), ["ip"], ["pf"])
+    op("V", cp(X("p16f"), X("p16")), ["p16"], ["p16f"])
+    op("V", cp(X("pgf"), X("pg")), ["pg"], ["pgf"])
+    fr = X("fr", 16, 144)
+    op("V", ts(X("I1"), fr, X("pf"), None, A.is_equal), ["fr", "pf"], ["I1"])
+    vts("pg16", "pgf", 16.0, None, A.add)
+    op("V", ts(X("bda"), fr, X("pgf"), None, A.is_ge), ["fr", "pgf"], ["bda"])
+    op("V", ts(X("bdb"), fr, X("pg16"), None, A.is_lt), ["fr", "pg16"], ["bdb"])
+    op("V", cp(X("mvu"), X("mvI")), ["mvI"], ["mvu"])
+    op("V", cp(X("wf"), X("wI")), ["wI"], ["wf"])
+    op("V", tt(X("BD"), X("bda"), X("bdb"), A.mult), ["bda", "bdb"], ["BD"])
+    op("V", cp(X("L0h", 0, 128), X("vpI").indirect(X("mvu", 0, 8))), ["vpI", "mvu"], ["L0h0"])
+    op("S", act(X("L0h", 128, 256), X("vpI").indirect(X("mvu", 8, 16))), ["vpI", "mvu"], ["L0h1"])
+    send(q + 1, X("L0"), X("L0h"), "aL0", ["L0h0", "L0h1"])
+    g.sem_inc(T.sem.sent, 1)
+    g.sync.wait_ge(T.sem.sent, 1)
+    dma("Y", X("R", 3072, 8192), T.strat[:, 3072:8192], [], ["R"])
+    dma("Y", X("OS", rows=slice(1, 128)), T.vo[0:127, :], [], ["OS"])
+    dma("Y", X("OS", rows=slice(0, 1)), T.vo[0:1, :], [], ["OSa"])
+    dma("Y", X("R", 8192, 9216), T.strat[:, 0:1024], [], ["Rd"])
+
+    scaled("WB", "BD", "wf"); scaled("WN", "WB", -1.0)
+    op("S", act(X("pH"), X("vpI")), ["vpI"], ["pH"])
+    for n, d in (("Sh1", 1), ("Sh2", 2)):
+        where(X(n), X("BD"), [[1, 128]], -d, -1, ["BD"], [n])
+    for r in (slice(0, 32), slice(32, 64)):
+        where(X("En", rows=r), X("s0", 0, 512, rows=r), [[-1, 32], [0, 16]], 0, 1, ["s0"], ["En"])
+    where(X("EX"), X("s0"), [[-1, 16], [-16, 8], [0, 16]], 0, 1, ["s0"], ["EX"])
+    fill("ones", 1.0); fill("mones", -1.0); fill("KQ", 32.0 / 128); fill("KZ", MAGIC / 128)
+    for k, m, n in (("KU", 4096.0, 128), ("KP", 32.0, 16), ("KN", 256.0, 1)):
+        fill(k, m / 128, 0, n, rows=slice(0, 64)); fill(k, -0.5 / 64, 0, n, rows=slice(64, 128)); fill(k, MAGIC * m / 128, n, 2 * n)
+    vts("ck32", "p16f", 37.0 * 32, None, A.mult)
+    op("V", ts(X("D16"), X("fr"), X("pgf"), None, A.is_equal), ["fr", "pgf"], ["D16"])
+    vts("low", "p16f", 0.0, -4096.0, A.is_gt, A.mult)
+    vts("m0", "p16f", 0.0, None, A.is_equal)
+    vts("x16", "p16f", 16.0, None, A.mult)
+    vts("x32", "p16f", 32.0, None, A.mult)
+    vts("kk", "p16f", -1.0, 15.0, A.mult, A.add)
+    vts("ck", "p16f", 37.0, None, A.mult)
+    for t in range(4):
+        op("V", ts(X("N", 256 * t, 256 * t + 256), X("il"), X("low"), 256.0 * t, A.add, A.add), ["il", "low"], ["N"])
+    for n, d in (("Se0", "I1"), ("Se1", "Sh1")):
+        vts(n, d, "m0", None, A.mult)
+    vts("Dn", "D16", -BIG, None, A.mult); vts("Dw", "D16", "wf", None, A.mult); vts("Dv", "D16", "wf", -1.0, A.mult, A.mult)
+    for n, s in (("I2", 0.5), ("I2e", 0.5 - 2.0 ** -9), ("I4", 0.25), ("Im", -1.0), ("Is", 1 / STEP), ("KM", "kk")):
+        vts(n, "I1", s, None, A.mult)
     for h in range(2):
-        sums(0, h); product(0, h); address(0, h); z4(0, h)
-    places_pe(0); places(0)
+        fill("qc%d" % h, 9.5 * BIG)
+        if VY[h] < 8:
+            fill("qc%d" % h, 3 * BIG, 16 * VY[h], 128, over=True)
+        fill("qc%d" % h, -32 * BIG, 15, 128, 16, over=True)
+    fill("s1", 0.0)
+    vts("Xc", "iy", "x16", None, A.add)
+    fill("nones", -1.0); fill("pones", 1.0)
+    fill("s1", 256.0, 0, 2048, 16, over=True)
+    table_own()
+    grow_pe("P6", "L0h", ["L0h0", "L0h1"], False, 0)
+    grow("P6", "PS", 1024, 256)
+
+    sums(0, 0); z4(0, 0); product(0, 0); raise0(0, 0); turned(0, 0); shift(0); address("V", 0, 0)
     send(q + 2, X("OB"), X("OS"), "aOB", ["OS", "OSa"])
     hand(0, "PS", ["PS", "PSx"])
     hand(1, "OS", ["OS", "OSa"])
+    fill("s0", 0.0, 0, 2048, 16)
 
-    for t in range(4):
-        gather(t, "V", 0, 2); gather(t, "S", 2, 4); gather(t, "S", 4, 6); gather(t, "S", 6, 8)
-        counts0(0); moves0(t, 0)
-        compare(0, 2); compare(2, 4); counts(0, 4)
-        compare(4, 6)
-        if t:
-            sums(t, 1); z4(t, 1)
-        compare(6, 8); counts(4, 8)
-        if t:
-            lookup(t, 1); product(t, 1); address(t, 1)
-            send((q - 1, q + 1, q - 1)[t - 1], X("L%dr" % t), X("L%d" % t), "aL%d" % t, ["L%d0" % t, "L%d1" % t])
-        gather(t, "S", 8, 11)
-        counts0(1)
-        if t < 3:
-            if t:
-                places_pe(t)
-            scan_hi(0, 8)
-            verdict(t, 0); moves1(t, 0)
-            if t:
-                places(t)
-            select("S", "HI", 0)
-            old(t)
-            scan_lo(0, 4); moves2(t, 0); scan_lo(4, 8); moves3(t, 0)
-            mean_pe(t, 0, "HI")
-            gather(t, "S", 11, 13)
-            select("S", "LO", 0); mean_pe(t, 0, "LO"); newz("S", t, 0)
-            gather(t, "S", 13, 16)
-            rounded("S", 0)
-            moves0(t, 1)
-            compare(8, 11); compare(11, 12); counts(8, 12); compare(12, 13); compare(13, 16); counts(12, 16)
-            if t == 2:
-                grow_pe("L1r", ["L1r"], True, 1); grow("OA", 1024, 512)
-            sums(t + 1, 0)
-            scatter(0)
-            scan_hi(8, 16)
-            verdict(t, 1); moves1(t, 1)
-            number(t)
-            select("S", "HI", 1); mean_pe(t, 1, "HI")
-            lookup(t + 1, 0); product(t + 1, 0)
-            scan_lo(8, 12); moves2(t, 1); scan_lo(12, 16); moves3(t, 1)
-            select("S", "LO", 1); mean_pe(t, 1, "LO")
-            address(t + 1, 0)
-            rounded("V", 1); newz("S", t, 1)
-            scatter(1)
-            z4(t + 1, 0)
-            home(t)
-        else:
-            verdict(t, 0); moves1(t, 0)
-            scan_hi(0, 4); moves2(t, 0); scan_hi(4, 8); moves3(t, 0)
-            gather(t, "S", 11, 13); gather(t, "S", 13, 16)
-            moves0(t, 1)
-            grow_pe("L2r", ["L2r"], True, 2); grow("PS", 1280, 512)
-            scan_lo(0, 8)
-            select("S", "HI", 0); mean_pe(t, 0, "HI")
-            select("S", "LO", 0); mean_pe(t, 0, "LO")
-            compare(8, 11); compare(11, 12); counts(8, 12); compare(12, 13); compare(13, 16); counts(12, 16)
-            newz("S", t, 0)
-            verdict_rows("P2", 0, 2); verdict_out("P2", 0, 2); verdict_rows("P3", 2, 3); verdict_out("P3", 2, 3)
-            dma("Y", T.yk[:, 0:768], X("ykn", 0, 768, rows=slice(0, 8)), ["ykn0", "ykn2"], [])
-            op("T", [mm(X("P7", 0, 256), X("Se0"), X("N", 768, 1024), True, False), mm(X("P7", 0, 256), X("Sh1"), X("L3r"), False, True)],
-               ["Se0", "Sh1", "N", "L3r"], ["P7"])
-            op("S", act(X("yob"), X("P7", 0, 256)), ["P7"], ["yob"])
-            dma("Y", T.yo[:, :], X("yob"), ["yob"], [])
-            scan_hi(8, 12)
-            verdict(t, 1); moves1(t, 1); home(t)
-            scan_hi(12, 16); moves2(t, 1)
-            select("S", "HI", 1); mean_pe(t, 1, "HI")
-            scan_lo(8, 12); moves3(t, 1); scan_lo(12, 16)
-            select("V", "LO", 1); mean_pe(t, 1, "LO")
-            yp_half(0)
-            newz("V", t, 1)
-            yp_half(1)
-            dma("Y", T.yp[:, :], X("ypb"), ["ypb0", "ypb1"], [])
-            verdict_rows("P2", 3, 4); verdict_out("P2", 3, 4)
-            dma("S", T.yk[:, 768:1024], X("ykn", 768, 1024, rows=slice(0, 8)), ["ykn3"], [])
-            dma("Y", T.yz[:, :], X("zf"), ["zf0", "zf1"], [])
+    def turn(t):
+        gather(t, "V", 0, 2); lookup(t, 1); counts0(0); less_z(6, "P3"); gather(t, "S", 2, 4); compare(0, 4); gather(t, "S", 6, 8)
+        views_on(t); sums(t, 1); differ(6, "P3"); product(t, 1); raise0(t, 1); gather(t, "S", 4, 6); sign(6, "P3"); counts(0, 4)
+        shift(1); compare(4, 6); address("S", t, 1); moves0(t, 0); gather(t, "S", 10, 12); counts0(1); gather(t, "S", 14, 16)
+        scan_lo(4, 8); turned(t, 1); scan_hi(4, 8); counts(4, 8, True); verdict(0); places_pe(t); gather(t, "S", 8, 10)
+        offsets("V", 0); under(t, 0); moves1(t, 0); scan_hi(0, 4); select("S", "HI", 0); z4(t, 1); scan_lo(0, 4); less_z(14, "P3")
+        moves2(t, 0); mean_z(0, "HI"); select("V", "LO", 0); mean_z(0, "LO"); gather(t, "S", 12, 14); differ(14, "P3")
+        compare(8, 12); newz("V", t, 0); moves3("V", t, 0); compare(12, 14); scan_hi(12, 16); counts(8, 12); moves0(t, 1)
+        places("S"); sign(14, "P3"); scan_lo(8, 12); counts(12, 16, True); old(t); verdict(1); mean_r(0, "HI", "P7")
+        offsets("S", 1); mean_r(0, "LO", "P7"); rounded("S", 0, "P7"); under(t, 1); grow_o(t, 0); home(t); scan_lo(12, 16)
+        grow_o(t, 1); moves1(t, 1); scan_hi(8, 12); number(t); select("S", "HI", 1); select("S", "LO", 1); sums(t + 1, 0)
+        moves2(t, 1); scatter(0); lookup(t + 1, 0); mean_r(1, "HI", "P7"); mean_z(1, "HI"); mean_z(1, "LO"); mean_r(1, "LO", "P7")
+        moves3("S", t, 1); mirror(); newz("S", t, 1); product(t + 1, 0); z4(t + 1, 0); shift(0); rounded("S", 1, "P7"); scatter(1)
+        address("S", t + 1, 0); turned(t + 1, 0)
+
+    def last_turn(t):
+        gather(t, "V", 0, 2); counts0(0); gather(t, "S", 2, 4); compare(0, 4); gather(t, "S", 6, 8); lookup(t, 1); less_z(6, "P3")
+        differ(6, "P3"); sums(t, 1); moves0(t, 0); scan_hi(0, 4); product(t, 1); gather(t, "S", 4, 6); z4(t, 1); sign(6, "P3")
+        compare(4, 6); shift(1); address("S", t, 1); scan_lo(0, 4); grow_pe("P7", "L2r", ["L2r"], True, 2); turned(t, 1)
+        counts(0, 4); counts(4, 8, True); verdict_rows("P2", 0, 2); scan_hi(4, 8); verdict(0); under(t, 0); offsets("V", 0)
+        counts0(1); gather(t, "S", 8, 10); scan_lo(4, 8); select("V", "LO", 0); gather(t, "S", 10, 12); less_z(14, "P3")
+        moves1(t, 0); moves2(t, 0); gather(t, "S", 14, 16); compare(8, 12); scan_hi(8, 12); gather(t, "S", 12, 14)
+        compare(12, 14); scan_hi(12, 16); scan_lo(12, 16); differ(14, "P3"); moves0(t, 1); sign(14, "P3"); counts(8, 12)
+        counts(12, 16, True); select("S", "HI", 0); views_on(t); grow("P7", "PS", 1280, 512); verdict_rows("P3", 2, 3)
+        mean_z(0, "HI"); mean_z(0, "LO"); verdict(1); yo_pe("P7"); moves3("V", t, 0); under(t, 1); home(t); moves1(t, 1)
+        verdict_out("P2", 0, 2); offsets("S", 1); select("S", "HI", 1); mean_z(1, "HI"); newz("V", t, 0); scan_lo(8, 12)
+        yo_out("P7"); moves2(t, 1); verdict_out("P3", 2, 3); yk_out("Y", 0, 3); moves3("S", t, 1); select("V", "LO", 1)
+        mean_z(1, "LO"); newz("V", t, 1); verdict_rows("P2", 3, 4); yp_half(0); verdict_out("P2", 3, 4); yk_out("S", 3, 4)
+        yp_half(1); yp_out(); yz_out()
+
+    for t in range(3):
+        turn(t)
+    last_turn(3)
 
     for sem, v in used.items():
         if clock["G"].get(sem, 0) < v:

@@ -41,12 +41,12 @@ def _scratch():
         sb(n, w, d)
     for n in ("ip", "p16", "pg", "wI"):
         sb(n, 1, i)
-    for n in ("pf", "p16f", "pgf", "pg16", "wf", "ck32", "ck", "cA", "acc", "x16", "x32", "low", "kk", "m0"):
+    for n in ("pf", "p16f", "pgf", "pg16", "wf", "ck32", "ck", "cA", "acc", "x16", "x32", "low", "m0"):
         sb(n, 1, f)
     sb("fr", 144, f); sb("Dn", 144, b); sb("Dw", 144, b); sb("Dv", 144, b); sb("D16", 144, b)
-    for n in ("I1", "I2", "I2e", "I4", "Im", "Is", "KM", "bda", "bdb", "BD", "WB", "WN", "KQ", "KZ", "ones", "mones", "Sh1", "Sh2", "Se0", "Se1"):
+    for n in ("I1", "I2", "I2e", "I4", "Im", "Is", "bda", "bdb", "BD", "WB", "WN", "KQ", "KZ", "ones", "mones", "Sh1", "Sh2", "Se0", "Se1"):
         sb(n, 128, b)
-    sb("nones", 128, f); sb("pones", 128, f); sb("il", 256, f); sb("iy", 128, f); sb("Xc", 128, h)
+    sb("nones", 128, f); sb("pones", 128, f); sb("il", 256, f); sb("iy", 128, f); sb("Xc", 128, h); sb("ik", 128, f); sb("ck16", 128, h)
     sb("ypb", 256, f); sb("yob", 256, f)
     return s
 
@@ -345,6 +345,10 @@ def rank_program(g, core, T, topo):
         op("T", [mm(X(pc, 16 * (y0 - 8 * h), 16 * (y1 - 8 * h)), X("Dn", 16 - x, 144 - x), T.B[:, y0:y1, 16 * x:16 * x + 16], False,
                     x == 15 and end) for x in range(16)], ["Dn"] + ys("B", y0, y1), [pc])
 
+    def restarts(t):
+        if t == 0:
+            fill("s0", 0.0, 0, 2048, 16)
+
     def scan_hi(y0, y1):
         a, b = 256 * y0, 256 * y1
         op("V", lambda: V.tensor_tensor_scan(X("HI", a, b), X("s0", 0, b - a), X("Y", a, b), 0.0, A.mult, A.max), ["s0"] + ys("Y", y0, y1),
@@ -359,9 +363,15 @@ def rank_program(g, core, T, topo):
         pc, st = "P%d" % (4 + h), "st%d" % h
         op("V", lambda: V.tensor_tensor_scan(back(st), back(pc), back("Xc"), 0.0, A.min, A.max), [pc, "Xc"], [st])
 
-    def under(t, h):
-        st = "st%d" % h
-        op("V", tt(X("d%d" % t, 8 * h, 8 * h + 8), X(st, 0, 128, 16), X("Xc", 15, 128, 16), A.subtract), [st, "Xc"], ["d%d%d" % (t, h)])
+    def under_pe(p):
+        cs = []
+        for h in range(2):
+            o = X(p, 8 * h, 8 * h + 8)
+            cs += [mm(o, X("Im"), X("Xc", 15, 128, 16), True, False), mm(o, X("I1"), X("st%d" % h, 0, 128, 16), False, True)]
+        op("T", cs, ["Im", "I1", "Xc", "st0", "st1"], [p])
+
+    def under(e, t, p):
+        plus(e, X("d%d" % t), X(p, 0, 16), 0.0, [p], ["d%d" % t])
 
     def offsets(e, h):
         plus(e, X("of%d" % h), X("st%d" % h, 0, 128, 16), 0.0, ["st%d" % h], ["of%d" % h])
@@ -399,42 +409,49 @@ def rank_program(g, core, T, topo):
     def moves0(t, h):
         a, b = half(h)
         o = X("P6", 0, 128)
-        op("T", [mm(o, X("KM"), X("ones"), True, False), mm(o, X("Is"), X("L%d" % t, a, b), False, False)],
-           ["KM", "ones", "Is", "L%d%d" % (t, h)], ["P6"])
+        op("T", [mm(o, X("Im"), X("ck16"), True, False), mm(o, X("Is"), X("L%d" % t, a, b), False, False)],
+           ["Im", "ck16", "Is", "L%d%d" % (t, h)], ["P6"])
 
     def moves1(t, h):
-        d, pc = X("d%d" % t, 8 * h, 8 * h + 8), "P%d" % (4 + h)
-        op("T", [mm(X("P6", x, 128, 16), X("EX", 128 * x, 128 * x + 128), d, False, x == 15) for x in range(16)],
-           ["EX", "d%d%d" % (t, h)], ["P6"])
-        op("T", mm(X(pc, 128, 136), X("Im"), d, True, False), ["Im", "d%d%d" % (t, h)], [pc])
+        st, pc = "st%d" % h, "P%d" % (4 + h)
+        d = X(st, 0, 128, 16)
+        op("T", [mm(X("P6", x, 128, 16), X("EX", 128 * x, 128 * x + 128), d, False, x == 15) for x in range(16)], ["EX", st], ["P6"])
+        op("T", [mm(X(pc, 128, 136), X("Im"), d, True, False), mm(X(pc, 128, 136), X("I1"), X("Xc", 0, 128, 16), False, False)],
+           ["Im", "I1", "Xc", st], [pc])
+
+    def clamp(h):
+        op("V", ts(X("ML%d" % h), X("P6", 0, 128), 0.0, 1.0, A.max, A.min), ["P6"], ["ML%d" % h])
 
     def moves2(t, h):
         pc = "P%d" % (4 + h)
-        op("V", ts(X("ML%d" % h), X("P6", 0, 128), 0.0, 1.0, A.max, A.min), ["P6"], ["ML%d" % h])
         op("T", [mm(X(pc, 128, 136), X("D16", 16 - x, 144 - x), X("ML%d" % h, x, 128, 16), False, x == 15) for x in range(16)],
            ["D16", "ML%d" % h], [pc])
 
     def moves3(e, t, h):
         pc, m = "P%d" % (4 + h), "mo%d%d" % (t, h)
         if e == "V":
-            op("V", ts(X(m), X(pc, 128, 136), -15.0, STEP, A.add, A.mult), [pc], [m])
+            op("V", ts(X(m), X(pc, 128, 136), STEP, None, A.mult), [pc], [m])
         else:
-            op("S", act(X(m), X(pc, 128, 136), IDN, bias=-15 * STEP, scale=STEP), [pc], [m])
+            op("S", act(X(m), X(pc, 128, 136), scale=STEP), [pc], [m])
         send((q + 1, q + 1, q + 2, q - 1)[t], X("mr%d%d" % (t, h)), X(m), "am%d%d" % (t, h), [m])
 
     def home(t):
-        send(q - 1 - t % 3, X("dk", 16 * t, 16 * t + 16), X("d%d" % t), "ad%d" % t, ["d%d0" % t, "d%d1" % t])
+        send(q - 1 - t % 3, X("dk", 16 * t, 16 * t + 16), X("d%d" % t), "ad%d" % t, ["d%d" % t])
 
     def views_on(t):
         if t:
             send((q - 1, q + 1, q - 1)[t - 1], X("L%dr" % t), X("L%d" % t), "aL%d" % t, ["L%d0" % t, "L%d1" % t])
 
-    def number(t):
-        o = X("P7", 32, 33)
-        op("S", act(X("sg"), X("d%d" % t), SIGN, accum_out=X("acc")), ["d%d0" % t, "d%d1" % t], ["sg", "acc"])
+    def number0(p):
+        op("S", act(X("sg"), X(p, 0, 16), SIGN, accum_out=X("acc")), [p], ["sg", "acc"])
+
+    def number1(p):
+        o = X(p, 32, 33)
         op("T", remainder(o, "KN", 1, [mm(o, X("pones"), X("acc"), False, False)], [mm(o, X("nones"), X("acc"), False, True)]),
-           ["KN", "pones", "nones", "acc"], ["P7"])
-        plus("S", X("cA"), o, X("ck"), ["P7", "ck"], ["cA"])
+           ["KN", "pones", "nones", "acc"], [p])
+
+    def number2(e, p):
+        plus(e, X("cA"), X(p, 32, 33), X("ck"), [p, "ck"], ["cA"])
 
     def places_pe(t):
         o = X("P7", 128, 144)
@@ -529,6 +546,7 @@ def rank_program(g, core, T, topo):
     send(q + 1, X("zr0"), X("zs"), "az0", ["zs"])
     iota("iy", [[256, 8], [1, 16]])
     iota("rb", [[512, 16]])
+    iota("ik", [[16, 128]])
     fill("s0", 1.0)
     vts("p16", "ip", 15, None, A.bitwise_and)
     vts("pg", "ip", 112, None, A.bitwise_and)
@@ -543,6 +561,9 @@ def rank_program(g, core, T, topo):
     op("V", cp(X("mvu"), X("mvI")), ["mvI"], ["mvu"])
     op("V", cp(X("wf"), X("wI")), ["wI"], ["wf"])
     op("V", tt(X("BD"), X("bda"), X("bdb"), A.mult), ["bda", "bdb"], ["BD"])
+    fill("ones", 1.0); fill("mones", -1.0); fill("KQ", 32.0 / 128); fill("KZ", MAGIC / 128)
+    for k, m, n in (("KU", 4096.0, 128), ("KP", 32.0, 16), ("KN", 256.0, 1)):
+        fill(k, m / 128, 0, n, rows=slice(0, 64)); fill(k, -0.5 / 64, 0, n, rows=slice(64, 128)); fill(k, MAGIC * m / 128, n, 2 * n)
     op("V", cp(X("L0h", 0, 128), X("vpI").indirect(X("mvu", 0, 8))), ["vpI", "mvu"], ["L0h0"])
     op("S", act(X("L0h", 128, 256), X("vpI").indirect(X("mvu", 8, 16))), ["vpI", "mvu"], ["L0h1"])
     send(q + 1, X("L0"), X("L0h"), "aL0", ["L0h0", "L0h1"])
@@ -557,32 +578,26 @@ def rank_program(g, core, T, topo):
     op("S", act(X("pH"), X("vpI")), ["vpI"], ["pH"])
     for n, d in (("Sh1", 1), ("Sh2", 2)):
         where(X(n), X("BD"), [[1, 128]], -d, -1, ["BD"], [n])
-    for r in (slice(0, 32), slice(32, 64)):
+    for r in (slice(0, 32), slice(32, 64))[:4 - min(VY) // 2]:
         where(X("En", rows=r), X("s0", 0, 512, rows=r), [[-1, 32], [0, 16]], 0, 1, ["s0"], ["En"])
     where(X("EX"), X("s0"), [[-1, 16], [-16, 8], [0, 16]], 0, 1, ["s0"], ["EX"])
-    fill("ones", 1.0); fill("mones", -1.0); fill("KQ", 32.0 / 128); fill("KZ", MAGIC / 128)
-    for k, m, n in (("KU", 4096.0, 128), ("KP", 32.0, 16), ("KN", 256.0, 1)):
-        fill(k, m / 128, 0, n, rows=slice(0, 64)); fill(k, -0.5 / 64, 0, n, rows=slice(64, 128)); fill(k, MAGIC * m / 128, n, 2 * n)
+    for h in range(2):
+        fill("qc%d" % h, 9.5 * BIG, 0, 16 * VY[h]); fill("qc%d" % h, 3 * BIG, 16 * VY[h], 128)
     vts("ck32", "p16f", 37.0 * 32, None, A.mult)
     op("V", ts(X("D16"), X("fr"), X("pgf"), None, A.is_equal), ["fr", "pgf"], ["D16"])
     vts("low", "p16f", 0.0, -4096.0, A.is_gt, A.mult)
     vts("m0", "p16f", 0.0, None, A.is_equal)
     vts("x16", "p16f", 16.0, None, A.mult)
     vts("x32", "p16f", 32.0, None, A.mult)
-    vts("kk", "p16f", -1.0, 15.0, A.mult, A.add)
+    vts("ck16", "ik", "p16f", None, A.add)
     vts("ck", "p16f", 37.0, None, A.mult)
+    for h in range(2):
+        fill("qc%d" % h, -32 * BIG, 15, 128, 16, over=True)
     for t in range(4):
         op("V", ts(X("N", 256 * t, 256 * t + 256), X("il"), X("low"), 256.0 * t, A.add, A.add), ["il", "low"], ["N"])
     for n, d in (("Se0", "I1"), ("Se1", "Sh1")):
         vts(n, d, "m0", None, A.mult)
     vts("Dn", "D16", -BIG, None, A.mult); vts("Dw", "D16", "wf", None, A.mult); vts("Dv", "D16", "wf", -1.0, A.mult, A.mult)
-    for n, s in (("I2", 0.5), ("I2e", 0.5 - 2.0 ** -9), ("I4", 0.25), ("Im", -1.0), ("Is", 1 / STEP), ("KM", "kk")):
-        vts(n, "I1", s, None, A.mult)
-    for h in range(2):
-        fill("qc%d" % h, 9.5 * BIG)
-        if VY[h] < 8:
-            fill("qc%d" % h, 3 * BIG, 16 * VY[h], 128, over=True)
-        fill("qc%d" % h, -32 * BIG, 15, 128, 16, over=True)
     fill("s1", 0.0)
     vts("Xc", "iy", "x16", None, A.add)
     fill("nones", -1.0); fill("pones", 1.0)
@@ -590,42 +605,44 @@ def rank_program(g, core, T, topo):
     table_own()
     grow_pe("P6", "L0h", ["L0h0", "L0h1"], False, 0)
     grow("P6", "PS", 1024, 256)
+    for n, s in (("Is", 1 / STEP), ("Im", -1.0), ("I2", 0.5), ("I2e", 0.5 - 2.0 ** -9), ("I4", 0.25)):
+        scaled(n, "I1", s)
 
     sums(0, 0); z4(0, 0); product(0, 0); raise0(0, 0); turned(0, 0); shift(0); address("V", 0, 0)
     send(q + 2, X("OB"), X("OS"), "aOB", ["OS", "OSa"])
     hand(0, "PS", ["PS", "PSx"])
     hand(1, "OS", ["OS", "OSa"])
-    fill("s0", 0.0, 0, 2048, 16)
 
     def turn(t):
-        gather(t, "V", 0, 2); lookup(t, 1); counts0(0); less_z(6, "P3"); gather(t, "S", 2, 4); compare(0, 4); gather(t, "S", 6, 8)
-        views_on(t); sums(t, 1); differ(6, "P3"); product(t, 1); raise0(t, 1); gather(t, "S", 4, 6); sign(6, "P3"); counts(0, 4)
-        shift(1); compare(4, 6); address("S", t, 1); moves0(t, 0); gather(t, "S", 10, 12); counts0(1); gather(t, "S", 14, 16)
-        scan_lo(4, 8); turned(t, 1); scan_hi(4, 8); counts(4, 8, True); verdict(0); places_pe(t); gather(t, "S", 8, 10)
-        offsets("V", 0); under(t, 0); moves1(t, 0); scan_hi(0, 4); select("S", "HI", 0); z4(t, 1); scan_lo(0, 4); less_z(14, "P3")
-        moves2(t, 0); mean_z(0, "HI"); select("V", "LO", 0); mean_z(0, "LO"); gather(t, "S", 12, 14); differ(14, "P3")
-        compare(8, 12); newz("V", t, 0); moves3("V", t, 0); compare(12, 14); scan_hi(12, 16); counts(8, 12); moves0(t, 1)
-        places("S"); sign(14, "P3"); scan_lo(8, 12); counts(12, 16, True); old(t); verdict(1); mean_r(0, "HI", "P7")
-        offsets("S", 1); mean_r(0, "LO", "P7"); rounded("S", 0, "P7"); under(t, 1); grow_o(t, 0); home(t); scan_lo(12, 16)
-        grow_o(t, 1); moves1(t, 1); scan_hi(8, 12); number(t); select("S", "HI", 1); select("S", "LO", 1); sums(t + 1, 0)
-        moves2(t, 1); scatter(0); lookup(t + 1, 0); mean_r(1, "HI", "P7"); mean_z(1, "HI"); mean_z(1, "LO"); mean_r(1, "LO", "P7")
-        moves3("S", t, 1); mirror(); newz("S", t, 1); product(t + 1, 0); z4(t + 1, 0); shift(0); rounded("S", 1, "P7"); scatter(1)
-        address("S", t + 1, 0); turned(t + 1, 0)
+        gather(t, "V", 0, 2); gather(t, "S", 2, 4); gather(t, "S", 6, 8); compare(0, 2); moves0(t, 0); less_z(6, "P3"); sums(t, 1)
+        lookup(t, 1); differ(6, "P3"); compare(2, 4); product(t, 1); raise0(t, 1); counts0(0); counts(0, 4); z4(t, 1); restarts(t)
+        shift(1); gather(t, "S", 4, 6); sign(6, "P3"); compare(4, 6); scan_hi(0, 4); views_on(t); address("S", t, 1); counts0(1)
+        gather(t, "S", 14, 16); gather(t, "S", 8, 10); scan_lo(4, 8); counts(4, 8, True); verdict(0); turned(t, 1); places_pe(t)
+        scan_hi(4, 8); offsets("V", 0); scan_lo(0, 4); select("V", "HI", 0); moves1(t, 0); select("V", "LO", 0); less_z(14, "P3")
+        mean_z(0, "HI"); clamp(0); mean_z(0, "LO"); gather(t, "S", 10, 12); gather(t, "S", 12, 14); newz("S", t, 0); places("S")
+        moves0(t, 1); compare(8, 10); compare(10, 12); differ(14, "P3"); moves2(t, 0); compare(12, 14); sign(14, "P3")
+        moves3("S", t, 0); counts(8, 12); old(t); counts(12, 16, True); scan_hi(8, 12); grow_o(t, 0); mean_r(0, "HI", "P7")
+        scan_lo(8, 12); grow_o(t, 1); mean_r(0, "LO", "P7"); verdict(1); moves1(t, 1); offsets("S", 1); under_pe("P3")
+        number0("P3"); under("S", t, "P3"); sums(t + 1, 0); scan_lo(12, 16); home(t); scan_hi(12, 16); clamp(1); moves2(t, 1)
+        select("S", "HI", 1); select("V", "LO", 1); mean_z(1, "HI"); rounded("V", 0, "P7"); moves3("S", t, 1); mean_z(1, "LO")
+        newz("S", t, 1); lookup(t + 1, 0); mean_r(1, "HI", "P7"); mean_r(1, "LO", "P7"); rounded("S", 1, "P7"); number1("P3")
+        number2("S", "P3"); scatter(0); product(t + 1, 0); shift(0); z4(t + 1, 0); address("S", t + 1, 0); mirror(); scatter(1)
+        turned(t + 1, 0)
 
     def last_turn(t):
-        gather(t, "V", 0, 2); counts0(0); gather(t, "S", 2, 4); compare(0, 4); gather(t, "S", 6, 8); lookup(t, 1); less_z(6, "P3")
-        differ(6, "P3"); sums(t, 1); moves0(t, 0); scan_hi(0, 4); product(t, 1); gather(t, "S", 4, 6); z4(t, 1); sign(6, "P3")
-        compare(4, 6); shift(1); address("S", t, 1); scan_lo(0, 4); grow_pe("P7", "L2r", ["L2r"], True, 2); turned(t, 1)
-        counts(0, 4); counts(4, 8, True); verdict_rows("P2", 0, 2); scan_hi(4, 8); verdict(0); under(t, 0); offsets("V", 0)
-        counts0(1); gather(t, "S", 8, 10); scan_lo(4, 8); select("V", "LO", 0); gather(t, "S", 10, 12); less_z(14, "P3")
-        moves1(t, 0); moves2(t, 0); gather(t, "S", 14, 16); compare(8, 12); scan_hi(8, 12); gather(t, "S", 12, 14)
-        compare(12, 14); scan_hi(12, 16); scan_lo(12, 16); differ(14, "P3"); moves0(t, 1); sign(14, "P3"); counts(8, 12)
-        counts(12, 16, True); select("S", "HI", 0); views_on(t); grow("P7", "PS", 1280, 512); verdict_rows("P3", 2, 3)
-        mean_z(0, "HI"); mean_z(0, "LO"); verdict(1); yo_pe("P7"); moves3("V", t, 0); under(t, 1); home(t); moves1(t, 1)
-        verdict_out("P2", 0, 2); offsets("S", 1); select("S", "HI", 1); mean_z(1, "HI"); newz("V", t, 0); scan_lo(8, 12)
-        yo_out("P7"); moves2(t, 1); verdict_out("P3", 2, 3); yk_out("Y", 0, 3); moves3("S", t, 1); select("V", "LO", 1)
-        mean_z(1, "LO"); newz("V", t, 1); verdict_rows("P2", 3, 4); yp_half(0); verdict_out("P2", 3, 4); yk_out("S", 3, 4)
-        yp_half(1); yp_out(); yz_out()
+        gather(t, "V", 4, 6); moves0(t, 0); less_z(6, "P3"); gather(t, "S", 6, 8); differ(6, "P3"); lookup(t, 1); scan_hi(4, 8)
+        gather(t, "S", 0, 2); gather(t, "S", 2, 4); sums(t, 1); compare(0, 2); sign(6, "P3"); product(t, 1); shift(1)
+        address("S", t, 1); gather(t, "S", 14, 16); compare(2, 4); grow_pe("P7", "L2r", ["L2r"], True, 2); counts0(1)
+        compare(4, 6); counts0(0); gather(t, "V", 8, 10); turned(t, 1); z4(t, 1); counts(0, 4); verdict_rows("P2", 0, 2)
+        scan_hi(0, 4); counts(4, 8, True); verdict(0); gather(t, "S", 10, 12); gather(t, "S", 12, 14); compare(8, 10)
+        less_z(14, "P3"); compare(10, 12); differ(14, "P3"); views_on(t); moves1(t, 0); clamp(0); compare(12, 14); sign(14, "P3")
+        scan_lo(12, 16); counts(8, 12); scan_hi(12, 16); counts(12, 16, True); verdict(1); verdict_out("P2", 0, 2); moves0(t, 1)
+        offsets("S", 1); moves2(t, 0); scan_lo(8, 12); moves1(t, 1); under_pe("P2"); grow("P7", "PS", 1280, 512)
+        select("S", "LO", 1); moves3("S", t, 0); under("S", t, "P2"); scan_hi(8, 12); select("S", "HI", 1); clamp(1); moves2(t, 1)
+        mean_z(1, "HI"); scan_lo(4, 8); offsets("S", 0); mean_z(1, "LO"); scan_lo(0, 4); verdict_rows("P3", 2, 3)
+        select("S", "HI", 0); home(t); select("V", "LO", 0); mean_z(0, "HI"); moves3("S", t, 1); mean_z(0, "LO"); newz("S", t, 1)
+        newz("V", t, 0); yo_pe("P7"); verdict_rows("P2", 3, 4); verdict_out("P2", 3, 4); yp_half(0); yo_out("P7"); yp_half(1)
+        verdict_out("P3", 2, 3); yp_out(); yk_out("S", 3, 4); yz_out(); yk_out("Y", 0, 3)
 
     for t in range(3):
         turn(t)

import math
import numpy as np
from concourse.bass import DstId, RemoteDMATransfer
from concourse.mybir import dt, AluOpType, AxisListType, ActivationFunctionType

A = AluOpType
COPY = ActivationFunctionType.Copy
IDN = ActivationFunctionType.Identity
SIGN = ActivationFunctionType.Sign
MAGIC = 12582912.0
BIG = 8192.0
STEP = 2048.0
USES_OTHERS = True
TAG = [""]
VY = (6, 6)


def _scratch():
    s = {}

    def sb(name, n, d):
        s[name] = ("sbuf", [128, n], d)
    f, b, i, u, h = "float32", "bfloat16", "int32", "uint16", "float16"
    sb("R", 9216, b); sb("Y", 4096, b); sb("HI", 4096, b); sb("LO", 4096, b)
    s["B"] = ("sbuf", [128, 16, 256], b)
    for k in range(2):
        sb("al%d" % k, 128, u); sb("pr%d" % k, 128, i); sb("aj%d" % k, 128, i); sb("pf%d" % k, 128, f)
        sb("st%d" % k, 128, h); sb("ML%d" % k, 128, h); sb("hs%d" % k, 128, b); sb("ls%d" % k, 128, b)
        sb("rn%d" % k, 128, i); sb("of%d" % k, 8, u); sb("qc%d" % k, 128, b); sb("zT%d" % k, 128, b)
    for t in range(4):
        sb("L%d" % t, 256, h); sb("zo%d" % t, 256, b); sb("zr%d" % t, 256, b); sb("d%d" % t, 16, b)
        for k in range(2):
            sb("mo%d%d" % (t, k), 8, u); sb("mr%d%d" % (t, k), 8, u)
    sb("dk", 64, b); sb("zf", 256, b); sb("zs", 256, b); sb("sg", 16, b)
    for n in ("L0h", "L1r", "L2r", "L3r"):
        sb(n, 256, h)
    sb("mvI", 16, i); sb("rb", 16, b); sb("KP", 32, b); sb("KN", 2, b); sb("KU", 256, b); sb("UL", 16, u); sb("mvu", 16, u); sb("old", 256, b)
    for n, w, d in (("vpI", 1024, i), ("OS", 1024, i), ("OB", 1024, i), ("OA", 1536, i), ("PS", 1792, f), ("PC", 1280, f),
                    ("pH", 1024, h), ("N", 1024, h), ("EX", 2048, b), ("s0", 2048, b), ("s1", 2048, b), ("ykn", 1024, f),
                    ("En", 512, b)):
        sb(n, w, d)
    for n in ("ip", "p16", "pg", "wI"):
        sb(n, 1, i)
    for n in ("pf", "p16f", "pgf", "pg16", "wf", "ck32", "ck", "cA", "acc", "x16", "x32", "low", "m0"):
        sb(n, 1, f)
    sb("fr", 144, f); sb("Dn", 144, b); sb("Dw", 144, b); sb("Dv", 144, b); sb("D16", 144, b)
    for n in ("I1", "I2", "I2e", "I4", "Im", "Is", "bda", "bdb", "BD", "WB", "WN", "KQ", "KZ", "ones", "mones", "Sh1", "Sh2", "Se0", "Se1"):
        sb(n, 128, b)
    sb("nones", 128, f); sb("pones", 128, f); sb("il", 256, f); sb("iy", 128, f); sb("Xc", 128, h); sb("ik", 128, f); sb("ck16", 128, h)
    sb("ypb", 256, f); sb("yob", 256, f)
    return s


_ALL = _scratch()
_PACK = {}


def _pack():
    out, width = {}, {}
    size = {"float32": 4, "int32": 4, "bfloat16": 2, "uint16": 2, "float16": 2}
    for name, (w, sh, d) in _ALL.items():
        if len(sh) == 2 and sh[1] <= 256:
            al = 32 // size[d]
            o = width.get(d, 0)
            _PACK[name] = ("pk_" + d, o, sh[1])
            width[d] = o + -(-sh[1] // al) * al
        else:
            out[name] = (w, sh, d)
    for d, w in width.items():
        out["pk_" + d] = ("sbuf", [128, w], d)
    for k in range(8):
        out["P%d" % k] = ("psum", [128, 512], "float32")
    return out


SCRATCH = _pack()
_ARR = ["aL0", "az0", "aOB", "aPC", "aOA", "aL1", "aL2", "aL3", "ahand"] + ["am%d%d" % (t, h) for t in range(4) for h in (0, 1)] \
    + ["az%d%d" % (t, h) for t in (1, 2, 3, 4) for h in (0, 1)] + ["ad%d" % t for t in range(4)]
SEMAPHORES = ["sV", "sT", "sS", "sG", "ls", "sent"] + ["d%d" % k for k in range(24)] + _ARR

HANDED = (("PC", 1280, "aPC", 3), ("OA", 1024, "aOA", 1))


def helpers(T, topo, r):
    c = T.cores[r]
    out = []
    for _, _, _, d in HANDED:
        to = T.cores[(r + d) % 4]
        out.append([k for k in topo.cores_of(c) if topo.die(k) != topo.die(c) and topo.may_write(k, to) and k not in out][0])
    return out


def hand_on(g, core, T, topo):
    for r in range(4):
        for k, (buf, n, sem, d) in zip(helpers(T, topo, r), HANDED):
            if k == core:
                to = T.cores[(r + d) % 4]
                rid, pid = topo.addr(to)[:2]
                g.wait_ge(T.sem.ahand, len(inner(topo, T.cores[r], k, to)))
                g.remote_dma(T[buf][:, 0:n], T[buf][:, 0:n], T.sem[sem], T.sem.ls, pid, rid, topo.mask(core, to))
                g.wait_ge(T.sem.ls, len(topo.engines(core, to)))


def inner(topo, c, k, far):
    return [e for e in topo.engines(c, k) if e not in topo.engines(c, far)]


def rank_program(g, core, T, topo):
    q = T.rank_of(core)
    if q is None:
        hand_on(g, core, T, topo)
        return
    ENG = {"V": g.vector, "T": g.tensor, "S": g.scalar, "G": g, "Y": g.sync}
    QSEM = {"V": "sV", "T": "sT", "S": "sS", "G": "sG"}
    cnt = {k: 0 for k in QSEM}
    clock = {k: {} for k in ENG}
    last, readers = {}, {}
    used = {}
    dn = [0]

    def X(name, a=None, b=None, step=None, rows=None):
        buf, o, w = _PACK.get(name, (name, 0, None))
        t = T[buf]
        if w is None:
            w = t.shape[1]
        a = 0 if a is None else a
        b = w if b is None else b
        r = slice(0, 128) if rows is None else rows
        if step is None:
            return t[r, o + a:o + b]
        return t[r, o + a:o + b:step]

    def back(name):
        buf, o, w = _PACK.get(name, (name, 0, None))
        return T[buf][:, o + 127:(o - 1 if o else None):-1]

    def wait(qn, tok):
        sem, val, snap, _ = tok
        ck = clock[qn]
        if ck.get(sem, 0) >= val:
            return
        ENG[qn].wait_ge(T.sem[sem], val)
        ck[sem] = val
        for s, v in snap.items():
            if ck.get(s, 0) < v:
                ck[s] = v

    def before(qn, R, W):
        for k in R:
            if k in last:
                wait(qn, last[k])
            if k[0] == "P" and k[1].isdigit():
                for e, tok in readers.get(k, {}).items():
                    if e != qn:
                        wait(qn, tok)
        for k in W:
            if k in last and (last[k][3] != qn or qn == "Y"):
                wait(qn, last[k])
            for e, tok in readers.get(k, {}).items():
                if e != qn:
                    wait(qn, tok)

    def after(qn, tok, R, W):
        for k in R:
            readers.setdefault(k, {})[qn] = tok
        for k in W:
            last[k] = tok
            readers[k] = {}

    def op(qn, calls, R, W):
        before(qn, R, W)
        TAG[0] = W[0]
        calls = calls if isinstance(calls, list) else [calls]
        for c in calls:
            ins = c()
        cnt[qn] += 1
        ins.then_inc(T.sem[QSEM[qn]], 1)
        used[QSEM[qn]] = cnt[qn]
        after(qn, (QSEM[qn], cnt[qn], dict(clock[qn]), qn), R, W)

    def dma(qn, out, in_, R, W):
        before(qn, R, W)
        sem = "d%d" % dn[0]
        dn[0] += 1
        ENG[qn].dma_start(out, in_).then_inc(T.sem[sem], 16)
        used[sem] = 16
        after("D" + sem, (sem, 16, dict(clock[qn]), "D" + sem), R, W)

    def write(c, eng, out, in_, sem, R):
        before("G", R, [])
        rid, pid = topo.addr(c)[:2]
        g.remote_dma(out, in_, T.sem[sem], T.sem.ls, pid, rid, sum(1 << e for e in eng))
        used["ls"] = used.get("ls", 0) + len(eng)

    def send(dst, out, in_, sem, R):
        c = T.cores[dst % 4]
        write(c, topo.engines(core, c), out, in_, sem, R)

    def arrives(src, sem, key):
        n = len(topo.engines(T.cores[src % 4], core))
        used[sem] = n
        last[key] = (sem, n, {}, "net")
        readers[key] = {}

    V, PE, S, G = g.vector, g.tensor, g.scalar, g

    def ts(out, i, s1, s2, o0, o1=None):
        if o1 is None:
            return lambda: V.tensor_scalar(out, i, s1, None, o0)
        return lambda: V.tensor_scalar(out, i, s1, s2, o0, o1)

    def tt(out, a, b, o):
        return lambda: V.tensor_tensor(out, a, b, o)

    def cp(out, a):
        return lambda: V.tensor_copy(out, a)

    def act(out, a, f=COPY, **kw):
        return lambda: S.activation(out, a, f, **kw)

    def mm(out, l, r, st=True, sp=True):
        return lambda: PE.matmul(out, l, r, st, sp)

    def vts(o, i, s1, s2, o0, o1=None):
        rd = [i] + [s for s in (s1, s2) if isinstance(s, str)]
        f = lambda s: X(s) if isinstance(s, str) else s
        op("V", ts(X(o), X(i), f(s1), f(s2), o0, o1), rd, [o])

    def plus(e, o, i, c, R, W):
        if e == "S":
            op("S", act(o, i, IDN, bias=c), R, W)
        else:
            op("V", ts(o, i, c, None, A.add), R, W)

    def fill(name, v, a=None, b=None, step=None, rows=None, over=False):
        op("V", lambda: V.memset(X(name, a, b, step, rows), v), [name] if over else [], [name])

    def iota(name, pattern, base=0, cm=0, integer=False):
        if integer:
            op("G", lambda: G.iota(X(name), pattern, base, cm), [], [name])
        else:
            op("G", lambda: G.iota(X(name), pattern, base, cm, allow_small_or_imprecise_dtypes=True), [], [name])

    def where(o, i, pattern, base, cm, R, W):
        op("G", lambda: G.affine_select(o, i, pattern, A.is_equal, 0.0, base, cm), R + ["where"], W + ["where"])

    def scaled(o, i, s):
        op("S", act(X(o), X(i), scale=X(s) if isinstance(s, str) else s), [i] + ([s] if isinstance(s, str) else []), [o])

    def half(h):
        return 128 * h, 128 * h + 128

    arrives(q - 1, "az0", "zr00"); arrives(q - 1, "az0", "zr01"); arrives(q - 1, "aL0", "L00"); arrives(q - 1, "aL0", "L01")
    arrives(q - 2, "aOB", "OB"); arrives(q + 1, "aPC", "PC"); arrives(q - 1, "aOA", "OA")
    arrives(q + 1, "aL1", "L1r"); arrives(q - 1, "aL2", "L2r"); arrives(q + 1, "aL3", "L3r")
    for h in range(2):
        for t in (1, 2, 3):
            arrives(q - 1 if t < 3 else q + 2, "am%d%d" % (t - 1, h), "mr%d%d" % (t - 1, h))
            arrives(q - 1 if t < 3 else q + 2, "az%d%d" % (t, h), "zr%d%d" % (t, h))
        arrives(q + 1, "am3%d" % h, "mr3%d" % h)
        arrives(q + 1, "az4%d" % h, "zf%d" % h)
    for t in range(4):
        arrives(q + 1 + t % 3, "ad%d" % t, "dk%d" % t)

    def lookup(t, h):
        if t == 0:
            return
        a, b = half(h)
        w = ("OB", "PC", "OA")[t - 1]
        op("V", tt(X("L%d" % t, a, b), X(w).indirect(X("mr%d%d" % (t - 1, h))), X("N", 256 * (t - 1) + a, 256 * (t - 1) + b), A.max),
           [w, w + "x", "mr%d%d" % (t - 1, h), "N"], ["L%d%d" % (t, h)])

    def const(o, k, a, n, st=False, sp=False, sign="ones"):
        return mm(o, X(sign), X(k, a, a + n), st, sp)

    def remainder(o, k, n, minus, plus_):
        return [const(o, k, 0, n, True)] + minus + [const(o, k, n, n), const(o, k, n, n, sign="mones")] + plus_

    def sums(t, h, pu="P2"):
        a, b = half(h)
        o, z = X(pu, 0, 128), X("zr%d" % t, a, b)
        cs = remainder(o, "KU", 128, [mm(o, X("WN"), z, False, False)], [mm(o, X("WB"), z, False, False), const(o, "KQ", 0, 128, sp=True)])
        op("T", cs[:1], ["KU", "KQ", "ones", "mones"], [pu])
        op("T", cs[1:], ["WB", "WN", "zr%d%d" % (t, h)], [pu])

    def z4(t, h):
        n = 16 * VY[h]
        op("T", [mm(X("P%d" % h, d, 4 * n, 4), X("I1"), X("zr%d" % t, 128 * h, 128 * h + n)) for d in range(4)],
           ["I1", "zr%d%d" % (t, h)], ["P%d" % h])

    def turned(t, h):
        n = 128 - 16 * VY[h]
        if n:
            o = X("P3", 0, 128, rows=slice(0, n))
            op("T", mm(o, X("zr%d" % t, 128 * h + 128 - n, 128 * h + 128), X("I1")), ["I1", "zr%d%d" % (t, h)], ["P3"])
            op("S", act(X("zT%d" % h, rows=slice(0, n)), o, scale=-1.0), ["P3"], ["zT%d" % h])

    def product(t, h, pu="P2"):
        a, b = half(h)
        o = ("pr%d" if t else "pf%d") % h
        op("V", tt(X(o), X(pu, 0, 128), X("L%d" % t, a, b), A.mult), [pu, "L%d%d" % (t, h)], [o])

    def raise0(t, h):
        if t == 0:
            vts("pr%d" % h, "pf%d" % h, "ck32", None, A.add)

    def shift(h):
        vts("aj%d" % h, "pr%d" % h, 5, 8191, A.arith_shift_right, A.bitwise_and)

    def address(e, t, h):
        plus(e, X("al%d" % h), X("aj%d" % h), X("cA") if t else 0.0, ["aj%d" % h, "cA"][:2 if t else 1], ["al%d" % h])

    def ys(n, y0, y1):
        return ["%s_%d" % (n, y) for y in range(y0, y1)]

    def gather(t, e, y0, y1):
        h = y0 // 8
        w = X("R") if t else X("R", 0, 8192)
        o, i = X("Y", 256 * y0, 256 * y1), w.indirect(X("al%d" % h, 16 * y0 - 128 * h, 16 * y1 - 128 * h))
        op(e, cp(o, i) if e == "V" else act(o, i), ["R", "Ra", "al%d" % h] + (["Rd"] if t else []), ys("Y", y0, y1))

    def compare(y0, y1):
        h = y0 // 8
        op("V", [tt(T.B[:, y0:y1, d:256:4], X("Y", 256 * y0 + d, 256 * y1, 4), X("P%d" % h, 64 * (y0 - 8 * h), 64 * (y1 - 8 * h)), A.is_gt)
                 for d in range(4)], ys("Y", y0, y1) + ["P%d" % h], ys("B", y0, y1))

    def less_z(y0, p):
        h = y0 // 8
        r = slice(16 * (y0 - 8 * h - VY[h]), 16 * (y0 - 8 * h - VY[h]) + 32)
        op("T", mm(X(p), X("zT%d" % h, rows=r), X("En", rows=r), True, False), ["zT%d" % h, "En"], [p])

    def differ(y0, p):
        op("T", mm(X(p), X("I1"), X("Y", 256 * y0, 256 * y0 + 512), False, True), ["I1"] + ys("Y", y0, y0 + 2), [p])

    def sign(y0, p):
        op("S", act(T.B[:, y0:y0 + 2, :], X(p), SIGN, bias=-0.5), [p], ys("B", y0, y0 + 2))

    def counts0(h):
        pc = "P%d" % (4 + h)
        op("T", mm(X(pc, 0, 128), X("I1"), X("qc%d" % h), True, False), ["I1", "qc%d" % h], [pc])

    def counts(y0, y1, end=False):
        h = y0 // 8
        pc = "P%d" % (4 + h)
        op("T", [mm(X(pc, 16 * (y0 - 8 * h), 16 * (y1 - 8 * h)), X("Dn", 16 - x, 144 - x), T.B[:, y0:y1, 16 * x:16 * x + 16], False,
                    x == 15 and end) for x in range(16)], ["Dn"] + ys("B", y0, y1), [pc])

    def restarts(t):
        if t == 0:
            fill("s0", 0.0, 0, 2048, 16)

    def scan_hi(y0, y1):
        a, b = 256 * y0, 256 * y1
        op("V", lambda: V.tensor_tensor_scan(X("HI", a, b), X("s0", 0, b - a), X("Y", a, b), 0.0, A.mult, A.max), ["s0"] + ys("Y", y0, y1),
           ys("HI", y0, y1))

    def scan_lo(y0, y1):
        a, b = 256 * y0, 256 * y1
        op("V", lambda: V.tensor_tensor_scan(X("LO", a, b), X("s1", 0, b - a), X("Y", a, b), 0.0, A.max, A.min), ["s1"] + ys("Y", y0, y1),
           ys("LO", y0, y1))

    def verdict(h):
        pc, st = "P%d" % (4 + h), "st%d" % h
        op("V", lambda: V.tensor_tensor_scan(back(st), back(pc), back("Xc"), 0.0, A.min, A.max), [pc, "Xc"], [st])

    def under_pe(p):
        cs = []
        for h in range(2):
            o = X(p, 8 * h, 8 * h + 8)
            cs += [mm(o, X("Im"), X("Xc", 15, 128, 16), True, False), mm(o, X("I1"), X("st%d" % h, 0, 128, 16), False, True)]
        op("T", cs, ["Im", "I1", "Xc", "st0", "st1"], [p])

    def under(e, t, p):
        plus(e, X("d%d" % t), X(p, 0, 16), 0.0, [p], ["d%d" % t])

    def offsets(e, h):
        plus(e, X("of%d" % h), X("st%d" % h, 0, 128, 16), 0.0, ["st%d" % h], ["of%d" % h])

    def select(e, w, h):
        s = ("hs%d" if w == "HI" else "ls%d") % h
        i = X(w, 2048 * h, 2048 * h + 2048).indirect(X("of%d" % h))
        op(e, cp(X(s), i) if e == "V" else act(X(s), i), ys(w, 8 * h, 8 * h + 8) + ["of%d" % h], [s])

    def mean_z(h, w):
        o = X("P%d" % h, 0, 128)
        if w == "HI":
            op("T", mm(o, X("I2e"), X("hs%d" % h), True, False), ["I2e", "hs%d" % h], ["P%d" % h])
        else:
            op("T", [mm(o, X("I2"), X("ls%d" % h), False, False), const(o, "KZ", 0, 128), const(o, "KZ", 0, 128, sp=True, sign="mones")],
               ["I2", "KZ", "ls%d" % h], ["P%d" % h])

    def mean_r(h, w, p):
        a, b = half(h)
        s = ("hs%d" if w == "HI" else "ls%d") % h
        cs = [mm(X(p, 0, 128), X("I4"), X(s), False, w == "LO")]
        if w == "HI":
            cs.insert(0, mm(X(p, 0, 128), X("I2"), X("old", a, b), True, False))
        op("T", cs, ["I2", "I4", "old", s], [p])

    def newz(e, t, h):
        a, b = half(h)
        pz, o, k = "P%d" % h, X("zo%d" % t, a, b), "zo%d%d" % (t, h)
        plus(e, o, X(pz, 0, 128), 0.0, [pz], [k])
        if t < 3:
            send(q + 1 if t < 2 else q + 2, X("zr%d" % (t + 1), a, b), o, "az%d%d" % (t + 1, h), [k])
        else:
            send(q - 1, X("zf", a, b), o, "az4%d" % h, [k])

    def moves0(t, h):
        a, b = half(h)
        o = X("P6", 0, 128)
        op("T", [mm(o, X("Im"), X("ck16"), True, False), mm(o, X("Is"), X("L%d" % t, a, b), False, False)],
           ["Im", "ck16", "Is", "L%d%d" % (t, h)], ["P6"])

    def moves1(t, h):
        st, pc = "st%d" % h, "P%d" % (4 + h)
        d = X(st, 0, 128, 16)
        op("T", [mm(X("P6", x, 128, 16), X("EX", 128 * x, 128 * x + 128), d, False, x == 15) for x in range(16)], ["EX", st], ["P6"])
        op("T", [mm(X(pc, 128, 136), X("Im"), d, True, False), mm(X(pc, 128, 136), X("I1"), X("Xc", 0, 128, 16), False, False)],
           ["Im", "I1", "Xc", st], [pc])

    def clamp(h):
        op("V", ts(X("ML%d" % h), X("P6", 0, 128), 0.0, 1.0, A.max, A.min), ["P6"], ["ML%d" % h])

    def moves2(t, h):
        pc = "P%d" % (4 + h)
        op("T", [mm(X(pc, 128, 136), X("D16", 16 - x, 144 - x), X("ML%d" % h, x, 128, 16), False, x == 15) for x in range(16)],
           ["D16", "ML%d" % h], [pc])

    def moves3(e, t, h):
        pc, m = "P%d" % (4 + h), "mo%d%d" % (t, h)
        if e == "V":
            op("V", ts(X(m), X(pc, 128, 136), STEP, None, A.mult), [pc], [m])
        else:
            op("S", act(X(m), X(pc, 128, 136), scale=STEP), [pc], [m])
        send((q + 1, q + 1, q + 2, q - 1)[t], X("mr%d%d" % (t, h)), X(m), "am%d%d" % (t, h), [m])

    def home(t):
        send(q - 1 - t % 3, X("dk", 16 * t, 16 * t + 16), X("d%d" % t), "ad%d" % t, ["d%d" % t])

    def views_on(t):
        if t:
            send((q - 1, q + 1, q - 1)[t - 1], X("L%dr" % t), X("L%d" % t), "aL%d" % t, ["L%d0" % t, "L%d1" % t])

    def number0(p):
        op("S", act(X("sg"), X(p, 0, 16), SIGN, accum_out=X("acc")), [p], ["sg", "acc"])

    def number1(p):
        o = X(p, 32, 33)
        op("T", remainder(o, "KN", 1, [mm(o, X("pones"), X("acc"), False, False)], [mm(o, X("nones"), X("acc"), False, True)]),
           ["KN", "pones", "nones", "acc"], [p])

    def number2(e, p):
        plus(e, X("cA"), X(p, 32, 33), X("ck"), [p, "ck"], ["cA"])

    def places_pe(t):
        o = X("P7", 128, 144)
        s = [[mm(o, X(w, 16 - x, 144 - x), X("zr%d" % t, x, 256, 16), False, False) for x in range(16)] for w in ("Dv", "Dw")]
        op("T", remainder(o, "KP", 16, s[0], s[1] + [mm(o, X("I1"), X("rb"), False, True)]),
           ["Dw", "Dv", "KP", "rb", "zr%d0" % t, "zr%d1" % t], ["P7"])

    def places(e):
        plus(e, X("UL"), X("P7", 128, 144), X("x32"), ["P7", "x32"], ["UL"])

    def old(t):
        op("S", act(X("old"), X("R", 0, 8192).indirect(X("UL"))), ["R", "Ra", "UL"], ["old"])

    def rounded(e, h, p):
        plus(e, X("rn%d" % h), X(p, 0, 128), -0.375, [p], ["rn%d" % h])

    def scatter(h):
        op("V", cp(X("R", 0, 8192).indirect(X("UL", 8 * h, 8 * h + 8)), X("rn%d" % h)), ["rn%d" % h, "UL", "R"], ["R"])

    def mirror():
        op("V", cp(X("R", 8192, 9216).indirect(X("UL", 0, 2)), X("rn0", 0, 32)), ["rn0", "UL"], ["Rd"])

    def table_own():
        for k in range(2):
            a, p = 512 * k, "P%d" % (4 + k)
            op("T", mm(X(p), X("Sh1"), X("pH", a, a + 512)), ["Sh1", "pH"], [p])
            op("S", act(X("PS", a, a + 512), X(p)), [p], ["PS"])

    def grow_pe(p, Lb, keys, resumed, t):
        cs, n = [], 0
        if resumed:
            cs, n = [mm(X(p, 0, 256), X("Sh1"), X(Lb))], 256
        o = X(p, n, n + 256)
        cs += [mm(o, X("Se1"), X("N", 256 * t, 256 * t + 256), True, False), mm(o, X("Sh2"), X(Lb), False, True)]
        op("T", cs, ["Sh1", "Sh2", "Se1", "N"] + keys, [p])

    def grow(p, w, at, n):
        op("S", act(X(w, at, at + n), X(p, 0, n)), [p], [w + "x"])

    def grow_o(t, k):
        if t == 2:
            if k == 0:
                grow_pe("P3", "L1r", ["L1r"], True, 1)
            else:
                grow("P3", "OA", 1024, 512)

    def hand(k, src, keys):
        buf, n, _, d = HANDED[k]
        c = helpers(T, topo, q)[k]
        write(c, inner(topo, core, c, T.cores[(q + d) % 4]), X(buf, 0, n), X(src, 0, n), "ahand", keys)

    def verdict_rows(p, t0, t1):
        n = 256 * (t1 - t0)
        op("T", [mm(X(p, x, n, 16, rows=slice(0, 8)), X("EX", 128 * x, 128 * x + 128, 16), X("dk", 16 * t0, 16 * t1)) for x in range(16)],
           ["EX"] + ["dk%d" % t for t in range(t0, t1)], [p])

    def verdict_out(p, t0, t1):
        n = 256 * (t1 - t0)
        plus("S", X("ykn", 256 * t0, 256 * t1, rows=slice(0, 8)), X(p, 0, n, rows=slice(0, 8)), 15.0, [p], ["ykn%d" % t0])

    def yo_pe(p):
        op("T", [mm(X(p, 0, 256), X("Se0"), X("N", 768, 1024), True, False), mm(X(p, 0, 256), X("Sh1"), X("L3r"), False, True)],
           ["Se0", "Sh1", "N", "L3r"], [p])

    def yo_out(p):
        op("S", act(X("yob"), X(p, 0, 256)), [p], ["yob"])
        dma("Y", T.yo[:, :], X("yob"), ["yob"], [])

    def yk_out(e, t0, t1):
        dma(e, T.yk[:, 256 * t0:256 * t1], X("ykn", 256 * t0, 256 * t1, rows=slice(0, 8)), ["ykn0", "ykn2"] if t0 == 0 else ["ykn3"], [])

    def yp_out():
        dma("Y", T.yp[:, :], X("ypb"), ["ypb0", "ypb1"], [])

    def yz_out():
        dma("Y", T.yz[:, :], X("zf"), ["zf0", "zf1"], [])

    def yp_half(h):
        a, b = half(h)
        op("V", tt(X("ypb", a, b), X("PS").indirect(X("mr3%d" % h)), X("N", 768 + a, 768 + b), A.max), ["PS", "PSx", "mr3%d" % h, "N"],
           ["ypb%d" % h])

    dma("Y", X("mvI"), T.mv[:, :], [], ["mvI"])
    dma("Y", X("vpI"), T.vp[:, :], [], ["vpI"])
    dma("S", X("zs"), T.z0[:, :], [], ["zs"])
    dma("S", X("wI"), T.wt[:, :], [], ["wI"])
    dma("Y", X("R", 0, 3072), T.strat[:, 0:3072], [], ["Ra"])

    iota("ip", [[0, 1]], 0, 1, integer=True)
    iota("fr", [[1, 144]], -16)
    iota("il", [[1, 256]], 1024)
    send(q + 1, X("zr0"), X("zs"), "az0", ["zs"])
    iota("iy", [[256, 8], [1, 16]])
    iota("rb", [[512, 16]])
    iota("ik", [[16, 128]])
    fill("s0", 1.0)
    vts("p16", "ip", 15, None, A.bitwise_and)
    vts("pg", "ip", 112, None, A.bitwise_and)
    op("V", cp(X("pf"), X("ip")), ["ip"], ["pf"])
    op("V", cp(X("p16f"), X("p16")), ["p16"], ["p16f"])
    op("V", cp(X("pgf"), X("pg")), ["pg"], ["pgf"])
    fr = X("fr", 16, 144)
    op("V", ts(X("I1"), fr, X("pf"), None, A.is_equal), ["fr", "pf"], ["I1"])
    vts("pg16", "pgf", 16.0, None, A.add)
    op("V", ts(X("bda"), fr, X("pgf"), None, A.is_ge), ["fr", "pgf"], ["bda"])
    op("V", ts(X("bdb"), fr, X("pg16"), None, A.is_lt), ["fr", "pg16"], ["bdb"])
    op("V", cp(X("mvu"), X("mvI")), ["mvI"], ["mvu"])
    op("V", cp(X("wf"), X("wI")), ["wI"], ["wf"])
    op("V", tt(X("BD"), X("bda"), X("bdb"), A.mult), ["bda", "bdb"], ["BD"])
    fill("ones", 1.0); fill("mones", -1.0); fill("KQ", 32.0 / 128); fill("KZ", MAGIC / 128)
    for k, m, n in (("KU", 4096.0, 128), ("KP", 32.0, 16), ("KN", 256.0, 1)):
        fill(k, m / 128, 0, n, rows=slice(0, 64)); fill(k, -0.5 / 64, 0, n, rows=slice(64, 128)); fill(k, MAGIC * m / 128, n, 2 * n)
    op("V", cp(X("L0h", 0, 128), X("vpI").indirect(X("mvu", 0, 8))), ["vpI", "mvu"], ["L0h0"])
    op("S", act(X("L0h", 128, 256), X("vpI").indirect(X("mvu", 8, 16))), ["vpI", "mvu"], ["L0h1"])
    send(q + 1, X("L0"), X("L0h"), "aL0", ["L0h0", "L0h1"])
    g.sem_inc(T.sem.sent, 1)
    g.sync.wait_ge(T.sem.sent, 1)
    dma("Y", X("R", 3072, 8192), T.strat[:, 3072:8192], [], ["R"])
    dma("Y", X("OS", rows=slice(1, 128)), T.vo[0:127, :], [], ["OS"])
    dma("Y", X("OS", rows=slice(0, 1)), T.vo[0:1, :], [], ["OSa"])
    dma("Y", X("R", 8192, 9216), T.strat[:, 0:1024], [], ["Rd"])

    scaled("WB", "BD", "wf"); scaled("WN", "WB", -1.0)
    op("S", act(X("pH"), X("vpI")), ["vpI"], ["pH"])
    for n, d in (("Sh1", 1), ("Sh2", 2)):
        where(X(n), X("BD"), [[1, 128]], -d, -1, ["BD"], [n])
    for r in (slice(0, 32), slice(32, 64))[:4 - min(VY) // 2]:
        where(X("En", rows=r), X("s0", 0, 512, rows=r), [[-1, 32], [0, 16]], 0, 1, ["s0"], ["En"])
    where(X("EX"), X("s0"), [[-1, 16], [-16, 8], [0, 16]], 0, 1, ["s0"], ["EX"])
    for h in range(2):
        fill("qc%d" % h, 9.5 * BIG, 0, 16 * VY[h]); fill("qc%d" % h, 3 * BIG, 16 * VY[h], 128)
    vts("ck32", "p16f", 37.0 * 32, None, A.mult)
    op("V", ts(X("D16"), X("fr"), X("pgf"), None, A.is_equal), ["fr", "pgf"], ["D16"])
    vts("low", "p16f", 0.0, -4096.0, A.is_gt, A.mult)
    vts("m0", "p16f", 0.0, None, A.is_equal)
    vts("x16", "p16f", 16.0, None, A.mult)
    vts("x32", "p16f", 32.0, None, A.mult)
    vts("ck16", "ik", "p16f", None, A.add)
    vts("ck", "p16f", 37.0, None, A.mult)
    for h in range(2):
        fill("qc%d" % h, -32 * BIG, 15, 128, 16, over=True)
    for t in range(4):
        op("V", ts(X("N", 256 * t, 256 * t + 256), X("il"), X("low"), 256.0 * t, A.add, A.add), ["il", "low"], ["N"])
    for n, d in (("Se0", "I1"), ("Se1", "Sh1")):
        vts(n, d, "m0", None, A.mult)
    vts("Dn", "D16", -BIG, None, A.mult); vts("Dw", "D16", "wf", None, A.mult); vts("Dv", "D16", "wf", -1.0, A.mult, A.mult)
    fill("s1", 0.0)
    vts("Xc", "iy", "x16", None, A.add)
    fill("nones", -1.0); fill("pones", 1.0)
    fill("s1", 256.0, 0, 2048, 16, over=True)
    table_own()
    grow_pe("P6", "L0h", ["L0h0", "L0h1"], False, 0)
    grow("P6", "PS", 1024, 256)
    for n, s in (("Is", 1 / STEP), ("Im", -1.0), ("I2", 0.5), ("I2e", 0.5 - 2.0 ** -9), ("I4", 0.25)):
        scaled(n, "I1", s)

    sums(0, 0); z4(0, 0); product(0, 0); raise0(0, 0); turned(0, 0); shift(0); address("V", 0, 0)
    send(q + 2, X("OB"), X("OS"), "aOB", ["OS", "OSa"])
    hand(0, "PS", ["PS", "PSx"])
    hand(1, "OS", ["OS", "OSa"])

    def turn(t):
        gather(t, "V", 0, 2); gather(t, "S", 2, 4); gather(t, "S", 6, 8); compare(0, 2); moves0(t, 0); less_z(6, "P3"); sums(t, 1)
        lookup(t, 1); differ(6, "P3"); compare(2, 4); product(t, 1); raise0(t, 1); counts0(0); counts(0, 4); z4(t, 1); restarts(t)
        shift(1); gather(t, "S", 4, 6); sign(6, "P3"); compare(4, 6); scan_hi(0, 4); views_on(t); address("S", t, 1); counts0(1)
        gather(t, "S", 14, 16); gather(t, "S", 8, 10); scan_lo(4, 8); counts(4, 8, True); verdict(0); turned(t, 1); places_pe(t)
        scan_hi(4, 8); offsets("V", 0); scan_lo(0, 4); select("V", "HI", 0); moves1(t, 0); select("V", "LO", 0); less_z(14, "P3")
        mean_z(0, "HI"); clamp(0); mean_z(0, "LO"); gather(t, "S", 10, 12); gather(t, "S", 12, 14); newz("S", t, 0); places("S")
        moves0(t, 1); compare(8, 10); compare(10, 12); differ(14, "P3"); moves2(t, 0); compare(12, 14); sign(14, "P3")
        moves3("S", t, 0); counts(8, 12); old(t); counts(12, 16, True); scan_hi(8, 12); grow_o(t, 0); mean_r(0, "HI", "P7")
        scan_lo(8, 12); grow_o(t, 1); mean_r(0, "LO", "P7"); verdict(1); moves1(t, 1); offsets("S", 1); under_pe("P3")
        number0("P3"); under("S", t, "P3"); sums(t + 1, 0); scan_lo(12, 16); home(t); scan_hi(12, 16); clamp(1); moves2(t, 1)
        select("S", "HI", 1); select("V", "LO", 1); mean_z(1, "HI"); rounded("V", 0, "P7"); moves3("S", t, 1); mean_z(1, "LO")
        newz("S", t, 1); lookup(t + 1, 0); mean_r(1, "HI", "P7"); mean_r(1, "LO", "P7"); rounded("S", 1, "P7"); number1("P3")
        number2("S", "P3"); scatter(0); product(t + 1, 0); shift(0); z4(t + 1, 0); address("S", t + 1, 0); mirror(); scatter(1)
        turned(t + 1, 0)

    def last_turn(t):
        gather(t, "V", 4, 6); moves0(t, 0); less_z(6, "P3"); gather(t, "S", 6, 8); differ(6, "P3"); lookup(t, 1); scan_hi(4, 8)
        gather(t, "S", 0, 2); gather(t, "S", 2, 4); sums(t, 1); compare(0, 2); sign(6, "P3"); product(t, 1); shift(1)
        address("S", t, 1); gather(t, "S", 14, 16); compare(2, 4); grow_pe("P7", "L2r", ["L2r"], True, 2); counts0(1)
        compare(4, 6); counts0(0); gather(t, "V", 8, 10); turned(t, 1); z4(t, 1); counts(0, 4); verdict_rows("P2", 0, 2)
        scan_hi(0, 4); counts(4, 8, True); verdict(0); gather(t, "S", 10, 12); gather(t, "S", 12, 14); compare(8, 10)
        less_z(14, "P3"); compare(10, 12); differ(14, "P3"); views_on(t); moves1(t, 0); clamp(0); compare(12, 14); sign(14, "P3")
        scan_lo(12, 16); counts(8, 12); scan_hi(12, 16); counts(12, 16, True); verdict(1); verdict_out("P2", 0, 2); moves0(t, 1)
        offsets("S", 1); moves2(t, 0); scan_lo(8, 12); moves1(t, 1); under_pe("P2"); grow("P7", "PS", 1280, 512)
        select("S", "LO", 1); moves3("S", t, 0); under("S", t, "P2"); scan_hi(8, 12); select("S", "HI", 1); clamp(1); moves2(t, 1)
        mean_z(1, "HI"); scan_lo(4, 8); offsets("S", 0); mean_z(1, "LO"); scan_lo(0, 4); verdict_rows("P3", 2, 3)
        select("S", "HI", 0); home(t); select("V", "LO", 0); mean_z(0, "HI"); moves3("S", t, 1); mean_z(0, "LO"); newz("S", t, 1)
        newz("V", t, 0); yo_pe("P7"); verdict_rows("P2", 3, 4); verdict_out("P2", 3, 4); yp_half(0); yo_out("P7"); yp_half(1)
        verdict_out("P3", 2, 3); yp_out(); yk_out("S", 3, 4); yz_out(); yk_out("Y", 0, 3)

    for t in range(3):
        turn(t)
    last_turn(3)

    for sem, v in used.items():
        if clock["G"].get(sem, 0) < v:
            g.wait_ge(T.sem[sem], v)
